import numpy as np
import ml_dtypes


def mxq(x, axis, fmt="e4m3"):
    dtype, down = {"e4m3": (ml_dtypes.float8_e4m3fn, 7), "e5m2": (ml_dtypes.float8_e5m2, 14)}[fmt]
    v = np.moveaxis(np.asarray(x, np.float32).astype(ml_dtypes.bfloat16).astype(np.float64), axis, -1)
    blocks = v.reshape(v.shape[:-1] + (-1, 32))
    amax = np.abs(blocks).max(-1, keepdims=True)
    byte = np.maximum(np.where(amax > 0, np.frexp(amax)[1] - 1 + 127, 0) - down, 1)
    scale = np.exp2(byte - 127.0)
    codes = (blocks / scale).astype(np.float32).astype(dtype).astype(np.float64)
    return np.moveaxis((codes * scale).reshape(v.shape), -1, axis)


WIDE = False


def mx_kscale(k):
    if not WIDE:
        return np.ones(k)
    levels = np.array([10, -10, 5, -5, 0])
    if k % 512:
        return np.exp2(np.random.permutation(np.resize(levels, k // 32))).repeat(32)
    a = np.empty((k // 512, 16))
    for p in range(k // 512):
        a[p, :8] = np.random.permutation(np.resize(levels, 8))
        for g in range(8):
            far = levels[np.abs(levels - a[p, g]) >= 10]
            a[p, g + 8] = far[np.random.randint(len(far))]
    return np.exp2(a.ravel()).repeat(32)


def f64(x):
    return np.asarray(x).astype(np.float64)


def striped(idx):
    return np.tile(idx.reshape(-1, 16).T, (8, 1)).astype(np.uint16)


def unstriped(offs):
    return offs[:16].T.reshape(-1).astype(np.int64)


E2M1 = np.array([0.0, 0.5, 1.0, 1.5, 2.0, 3.0, 4.0, 6.0, -0.0, -0.5, -1.0, -1.5, -2.0, -3.0, -4.0, -6.0])


def pack_weight(w, fmt):
    k, n = w.shape
    w = f64(np.asarray(w, np.float32).astype(ml_dtypes.bfloat16)).reshape(k // 32, 32, n)
    amax = np.abs(w).max(1)
    if fmt == "e4m3":
        byte = np.frexp(amax)[1] - 1 + 127 - 7
    else:
        mant, ex = np.frexp(amax / 6.0)
        byte = np.where(mant > 0.5, ex, ex - 1) + 127
    byte = np.clip(np.where(amax > 0, byte, 1), 1, 254)
    scaled = (w * np.exp2(127.0 - byte)[:, None, :]).reshape(k, n).astype(np.float32)
    by_word = np.ascontiguousarray(scaled.reshape(k // 512, 128, 4, n).transpose(0, 1, 3, 2))
    if fmt == "e4m3":
        words = by_word.astype(ml_dtypes.float8_e4m3fn).view(np.uint8)
    else:
        c = by_word.astype(ml_dtypes.float4_e2m1fn).view(np.uint8) & 0xF
        words = (c[..., 0::2] | (c[..., 1::2] << 4)).reshape(k // 512, 128, 2 * n)
    return np.ascontiguousarray(words), np.ascontiguousarray(byte.astype(np.uint8).reshape(k // 512, 16, n))


def unpack_weight(words, scales, fmt):
    g, _, n = scales.shape
    words = np.ascontiguousarray(words).reshape(g, 128, n, -1)
    if fmt == "e4m3":
        vals = words.view(ml_dtypes.float8_e4m3fn).astype(np.float64)
    else:
        nib = np.empty((g, 128, n, 4), np.uint8)
        nib[..., 0::2] = words & 0xF
        nib[..., 1::2] = words >> 4
        vals = E2M1[nib]
    vals = vals * np.repeat(np.exp2(scales.astype(np.float64) - 127.0), 8, axis=1)[..., None]
    return vals.transpose(0, 1, 3, 2).reshape(g * 512, n)


def gelu(v):
    return 0.5 * v * (1.0 + np.tanh(np.sqrt(2.0 / np.pi) * (v + 0.044715 * v**3)))


def striped8(idx):
    return np.concatenate([v.reshape(-1, 16).T for v in idx]).astype(np.uint16)


def unstriped8(offs):
    return np.stack([offs[16 * g:16 * g + 16].T.reshape(-1) for g in range(8)]).astype(np.int64)


def runs(v, idx8):
    k = np.arange(v.shape[0])
    return v[k[:, None], idx8[k % 512 // 64]]


def put_heads(h, wgs, idx8, t2):
    r = np.arange(h.shape[0])
    page = np.zeros((h.shape[0], t2))
    page[r[:, None], idx8[r % 512 // 64]] = wgs[r // 4 % 128] * h
    return page


def often(T, S):
    return np.random.permutation(T)[(T * np.random.uniform(0, 1, S) ** 4).astype(np.int64)]


K, H, N, T, S, T2 = 1024, 1024, 512, 2048, 512, 1024

def setup_inputs():
    n = np.random.standard_normal
    s = mx_kscale(K)[:, None]
    u = mx_kscale(H)[:, None]
    tab_words, tab_scales = pack_weight(n((K, T)) * s, "e4m3")
    wb_words, wb_scales = pack_weight(n((K, H)) / np.sqrt(K) / s, "e2m1")
    wc_words, wc_scales = pack_weight(n((K, H)) / np.sqrt(K) / s, "e4m3")
    return {
        "tab_words": tab_words, "tab_scales": tab_scales,
        "offs": striped8(np.stack([often(T, S) for _ in range(8)])),
        "wa": (n((K, H)) / np.sqrt(K) / s * u.T).astype(np.float32),
        "wb_words": wb_words, "wb_scales": wb_scales,
        "wc_words": wc_words, "wc_scales": wc_scales,
        "wd": (n((H, N)) / np.sqrt(H) / u).astype(np.float32),
        "bias": n(N).astype(np.float32),
        "offs2": striped8(np.stack([np.random.permutation(T2)[:S] for _ in range(8)])),
        "wgo": np.repeat(np.random.uniform(0.5, 2.0, (8, S)), 16, axis=0).astype(np.float32),
    }

def reference(tab_words, tab_scales, offs, wa, wb_words, wb_scales, wc_words, wc_scales,
              wd, bias, offs2, wgo):
    v = runs(unpack_weight(tab_words, tab_scales, "e4m3"), unstriped8(offs))
    wb = unpack_weight(wb_words, wb_scales, "e2m1")
    wc = unpack_weight(wc_words, wc_scales, "e4m3")
    a = mxq(f64(wa), 0, "e4m3").T @ v
    b = wb.T @ v
    c = wc.T @ v
    h = a * b * c
    y = (mxq(f64(wd), 0, "e4m3").T @ mxq(h, 0, "e4m3")) + f64(bias)[:, None]
    return put_heads(y, f64(wgo), unstriped8(offs2), T2)

@@ -1,0 +1,225 @@
+from contextlib import ExitStack
+
+import concourse.mybir as mybir
+
+K, H, N, T, S, T2 = 1024, 1024, 512, 2048, 512, 1024
+FLOPS = 2 * S * (3 * K * H + H * N)
+
+F32 = mybir.dt.float32
+BF16 = mybir.dt.bfloat16
+I32 = mybir.dt.int32
+U32 = mybir.dt.uint32
+U16 = mybir.dt.uint16
+U8 = mybir.dt.uint8
+E4M3 = mybir.dt.float8_e4m3fn_x4
+E2M1 = mybir.dt.float4_e2m1fn_x4
+MULT = mybir.AluOpType.mult
+EQUAL = mybir.AluOpType.is_equal
+IDENTITY = mybir.ActivationFunctionType.Identity
+
+P = 128
+PACK = 4
+PASS = P * PACK
+BANK = 512
+QUADS = 4
+SHIFT = 14
+MOVED = 112
+
+
+def tile_list_segment_reassortment_fitness_kernel(
+    tc, tab_words, tab_scales, offs, wa, wb_words, wb_scales, wc_words, wc_scales, wd, bias, offs2, wgo, out
+):
+    nc = tc.nc
+    kp, hp, chunks = K // PASS, H // PASS, S // P
+
+    with ExitStack() as ctx:
+        keep = ctx.enter_context(tc.tile_pool(name="keep", bufs=1))
+        ring = ctx.enter_context(tc.tile_pool(name="ring", bufs=3))
+        psum = ctx.enter_context(tc.psum_pool(name="psum", bufs=4))
+
+        def held(shape, dtype, name, tag=None):
+            return keep.tile(shape, dtype, name=name, tag=tag or name, align_bytes=64)
+
+        pick = held([P, S // 16], U16, "pick")
+        place = held([P, S // 16], U16, "place")
+        ts_both = held([P, kp * T], U8, "ts_both", "stage0")
+        ts_second = held([P, T], U8, "ts_second", "stage1")
+        ts_picked = held([P, kp, S], U8, "ts_picked", "stage4")
+        v_scales = held([P, kp, S], U8, "v_scales")
+        wb_sc = held([P, kp, H], U8, "wb_sc")
+        wc_sc = held([P, kp, H], U8, "wc_sc")
+        pages = [held([P, T2], F32, "page%d" % i) for i in range(PACK)]
+
+        nc.vector.memset(ts_both[:].bitcast(I32), 0)
+        column = held([P, P], F32, "column", "stage2")
+        row = held([P, 1], F32, "row", "stage3")
+        ident = held([P, P], F32, "ident")
+        nc.gpsimd.iota(row[:], [[0, 1]], base=0, channel_multiplier=1, allow_small_or_imprecise_dtypes=True)
+        nc.gpsimd.iota(column[:], [[1, P]], base=0, channel_multiplier=0, allow_small_or_imprecise_dtypes=True)
+        nc.vector.tensor_scalar(ident[:], column[:], row[:], None, EQUAL)
+        nc.vector.memset(wb_sc[:].bitcast(I32), 0)
+        nc.vector.memset(wc_sc[:].bitcast(I32), 0)
+        nc.vector.memset(v_scales[:].bitcast(I32), 0)
+
+        def load_scale_rows(queue, plane, scales, d, first):
+            queue.dma_start(
+                plane.bitcast(I32)[32 * d + first : 32 * d + first + 4],
+                scales[:, 4 * d : 4 * d + 4, :].rearrange("a r c -> r a c").bitcast(I32),
+            )
+
+        wb_w = held([P, kp, 2 * H], U8, "wb_w", "stage5")
+        tab = [held([P, T], I32, "tab%d" % a, "stage%d" % (2 + a)) for a in range(kp)]
+        nc.sync.dma_start(pick[:], offs)
+        nc.sync.dma_start(place[:], offs2)
+        nc.sync.dma_start(wb_w[:].bitcast(I32), wb_words.rearrange("a p c -> p a c").bitcast(I32))
+        for d in range(QUADS):
+            load_scale_rows(nc.sync, ts_both[:].rearrange("p (a t) -> p a t", a=kp), tab_scales, d, SHIFT)
+        for a in range(kp):
+            nc.sync.dma_start(tab[a][:], tab_words[a].rearrange("p t i -> p (t i)").bitcast(I32))
+        for d in range(QUADS):
+            load_scale_rows(nc.scalar, wb_sc[:], wb_scales, d, 0)
+        for d in range(QUADS):
+            load_scale_rows(nc.scalar, wc_sc[:], wc_scales, d, 0)
+
+        nc.vector.tensor_copy(ts_second[:].bitcast(I32), ts_both[:, T : 2 * T].bitcast(I32))
+        nc.vector.tensor_copy(ts_picked[:, 0, :], ts_both[:].indirect(pick[:]))
+        nc.vector.tensor_copy(ts_picked[:, 1, :], ts_second[:].indirect(pick[:]))
+        wc_w = held([P, kp, H], I32, "wc_w", "stage0")
+        nc.sync.dma_start(wc_w[:], wc_words.rearrange("a p c i -> p a (c i)").bitcast(I32))
+        nc.scalar.dma_start(
+            v_scales[:].rearrange("p a j -> p (a j)").bitcast(I32)[0:MOVED],
+            ts_picked[:].rearrange("p a j -> p (a j)").bitcast(I32)[SHIFT : SHIFT + MOVED],
+        )
+        v_words = [held([P, S], U32, "v_words%d" % a) for a in range(kp)]
+        for a in range(kp):
+            nc.vector.tensor_copy(v_words[a][:], tab[a][:].bitcast(U32).indirect(pick[:]))
+
+        for i, page in enumerate(pages):
+            (nc.gpsimd if i < 3 else nc.vector).memset(page[:], 0.0)
+
+        wa_raw = {}
+
+        def load_wa(a, b):
+            wa_raw[a, b] = held([P, PACK, BANK], F32, "wa_raw%d%d" % (a, b), "stage%d" % (1 + kp * b + a))
+            nc.sync.dma_start(
+                wa_raw[a, b][:],
+                wa[a * PASS : (a + 1) * PASS, b * BANK : (b + 1) * BANK].rearrange("(p j) c -> p j c", j=PACK),
+            )
+
+        def project(bank, jc, words, scales, fmt):
+            cols = slice(jc * P, (jc + 1) * P)
+            for a in range(kp):
+                nc.tensor.matmul_mx(
+                    out=bank[:],
+                    lhsT=v_words[a][:, cols].bitcast(E4M3),
+                    lhsT_scale=v_scales[:, a, cols],
+                    rhs=words[a].bitcast(fmt),
+                    rhs_scale=scales[a],
+                    start=(a == 0),
+                    stop=(a == kp - 1),
+                )
+
+        def interleave(copy, raw, name):
+            grouped = held([P, BANK * PACK], BF16, name)
+            copy(
+                grouped[:].rearrange("p (c i j) -> p c j i", i=4, j=PACK),
+                raw[:].rearrange("p j (c i) -> p c j i", i=4),
+            )
+            return grouped
+
+        def quantise(grouped, name):
+            words = held([P, BANK], U32, name + "_w")
+            scales = held([P, BANK], U8, name + "_s")
+            nc.vector.quantize_mx(out=words[:].bitcast(E4M3), scales=scales[:], in_=grouped[:])
+            return words, scales
+
+        bc = {}
+        wa_q = {}
+
+        def bc_unit(b, jc):
+            cols = slice(b * BANK, (b + 1) * BANK)
+            b_bank = psum.tile([P, BANK], F32, name="b_bank", tag="by_scalar")
+            project(b_bank, jc, [wb_w[:, a, 2 * b * BANK : 2 * (b + 1) * BANK] for a in range(kp)],
+                    [wb_sc[:, a, cols] for a in range(kp)], E2M1)
+            c_bank = psum.tile([P, BANK], F32, name="c_bank", tag="by_vector")
+            project(c_bank, jc, [wc_w[:, a, cols] for a in range(kp)], [wc_sc[:, a, cols] for a in range(kp)], E4M3)
+            b_sb = ring.tile([P, BANK], F32, name="b_sb")
+            nc.scalar.copy(b_sb[:], b_bank[:])
+            bc[b, jc] = held([P, BANK], F32, "bc%d%d" % (b, jc))
+            nc.vector.tensor_tensor(bc[b, jc][:], c_bank[:], b_sb[:], MULT)
+
+        for b in range(hp):
+            for jc in range(chunks):
+                bc_unit(b, jc)
+
+        for b in range(hp):
+            for a in range(kp):
+                load_wa(a, b)
+
+        def h_half(b):
+            h_rows = []
+            for jc in range(chunks):
+                a_bank = psum.tile([P, BANK], F32, name="a_bank", tag="by_vector")
+                project(a_bank, jc, [wa_q[a, b][0][:] for a in range(kp)], [wa_q[a, b][1][:] for a in range(kp)], E4M3)
+                h_jr = held([P, BANK], BF16, "h%d%d" % (b, jc))
+                nc.vector.tensor_tensor(h_jr[:], a_bank[:], bc[b, jc][:], MULT)
+                h_rows.append(h_jr)
+            grouped = held([P, S * PACK], BF16, "hT%d" % b)
+            for pair in range(chunks // 2):
+                turned = psum.tile([P, 2, 2, P], F32, name="turned", tag="by_scalar")
+                for e in range(2):
+                    words = h_rows[2 * pair + e][:].bitcast(F32)
+                    for u in range(2):
+                        nc.tensor.transpose(turned[:, e, u, :], words[:, u : 2 * P : 2], ident[:])
+                nc.scalar.copy(
+                    grouped[:].bitcast(F32)[:, pair * BANK : (pair + 1) * BANK].rearrange("p (e j u) -> p e j u", e=2, u=2),
+                    turned[:].rearrange("p e u j -> p e j u"),
+                )
+            return grouped
+
+        h_q = {}
+        for b in range(hp):
+            for a in range(kp):
+                copy = nc.vector.tensor_copy if (a, b) == (0, 0) else nc.scalar.copy
+                wa_q[a, b] = quantise(interleave(copy, wa_raw[a, b], "wa_g%d%d" % (a, b)), "wa_q%d%d" % (a, b))
+            h_q[b] = quantise(h_half(b), "h_q%d" % b)
+
+        wd_raw = [held([P, PACK, N], F32, "wd_raw%d" % b, "stage%d" % (5 * (1 - b))) for b in range(hp)]
+        for b in range(hp):
+            nc.sync.dma_start(wd_raw[b][:], wd[b * PASS : (b + 1) * PASS, :].rearrange("(p j) n -> p j n", j=PACK))
+        weights = held([P, S], F32, "weights", "stage2")
+        nc.sync.dma_start(weights[:], wgo)
+
+        bias_cols = held([P, PACK], F32, "bias_cols", "stage1")
+        nc.sync.dma_start(bias_cols[:], bias.rearrange("(p i) -> p i", i=PACK))
+
+        wd_q = {}
+        for b in range(hp):
+            grouped = held([P, N * PACK], BF16, "wd_g%d" % b)
+            dst = grouped[:].rearrange("p (i m j) -> p m j i", i=PACK, j=PACK)
+            src = wd_raw[b][:].rearrange("p j (m i) -> p m j i", i=PACK)
+            if b == 0:
+                nc.scalar.copy(dst, src)
+            else:
+                nc.scalar.copy(dst[:, 0:48], src[:, 0:48])
+                nc.vector.tensor_copy(dst[:, 48:P], src[:, 48:P])
+            wd_q[b] = quantise(grouped, "wd_q%d" % b)
+
+        rows = out.rearrange("(p i) t -> p i t", i=PACK)
+        for i in range(PACK):
+            cols = slice(i * P, (i + 1) * P)
+            y_bank = psum.tile([P, S], F32, name="y_bank", tag="by_scalar")
+            for b in range(hp):
+                nc.tensor.matmul_mx(
+                    out=y_bank[:],
+                    lhsT=wd_q[b][0][:, cols].bitcast(E4M3),
+                    lhsT_scale=wd_q[b][1][:, cols],
+                    rhs=h_q[b][0][:].bitcast(E4M3),
+                    rhs_scale=h_q[b][1][:],
+                    start=(b == 0),
+                    stop=(b == hp - 1),
+                )
+            y = held([P, S], F32, "y%d" % i)
+            nc.scalar.activation(y[:], y_bank[:], IDENTITY, bias=bias_cols[:, i : i + 1])
+            nc.vector.tensor_tensor(pages[i][:].indirect(place[:]), y[:], weights[:], MULT)
+            nc.sync.dma_start(rows[:, i, :], pages[i][:])

@@ -24,6 +24,7 @@ BANK = 512
 QUADS = 4
 SHIFT = 14
 MOVED = 112
+A = 8192
 
 
 def tile_list_segment_reassortment_fitness_kernel(
@@ -34,31 +35,33 @@ def tile_list_segment_reassortment_fitness_kernel(
 
     with ExitStack() as ctx:
         keep = ctx.enter_context(tc.tile_pool(name="keep", bufs=1))
+        stage = ctx.enter_context(tc.tile_pool(name="stage", bufs=1))
         ring = ctx.enter_context(tc.tile_pool(name="ring", bufs=3))
         psum = ctx.enter_context(tc.psum_pool(name="psum", bufs=4))
 
-        def held(shape, dtype, name, tag=None):
-            return keep.tile(shape, dtype, name=name, tag=tag or name, align_bytes=64)
+        def held(shape, dtype, name, offset=None):
+            if offset is None:
+                return keep.tile(shape, dtype, name=name, align_bytes=64)
+            return stage.tile(shape, dtype, name=name, align_bytes=64, offset=offset)
 
         pick = held([P, S // 16], U16, "pick")
         place = held([P, S // 16], U16, "place")
-        ts_both = held([P, kp * T], U8, "ts_both", "stage0")
-        ts_second = held([P, T], U8, "ts_second", "stage1")
-        ts_picked = held([P, kp, S], U8, "ts_picked", "stage4")
+        ts_both = held([P, kp * T], U8, "ts_both")
+        ts_second = held([P, T], U8, "ts_second", 8 * A - 1024)
+        ts_picked = held([P, kp, S], U8, "ts_picked", 5 * A - 256)
         v_scales = held([P, kp, S], U8, "v_scales")
         wb_sc = held([P, kp, H], U8, "wb_sc")
-        wc_sc = held([P, kp, H], U8, "wc_sc")
         pages = [held([P, T2], F32, "page%d" % i) for i in range(PACK)]
 
-        nc.vector.memset(ts_both[:].bitcast(I32), 0)
-        column = held([P, P], F32, "column", "stage2")
-        row = held([P, 1], F32, "row", "stage3")
+        nc.gpsimd.memset(ts_both[:, 0:T].bitcast(I32), 0)
+        nc.vector.memset(ts_both[:, T : 2 * T].bitcast(I32), 0)
+        column = held([P, P], F32, "column", A // 2)
+        row = held([P, 1], F32, "row", 5 * A // 2)
         ident = held([P, P], F32, "ident")
         nc.gpsimd.iota(row[:], [[0, 1]], base=0, channel_multiplier=1, allow_small_or_imprecise_dtypes=True)
         nc.gpsimd.iota(column[:], [[1, P]], base=0, channel_multiplier=0, allow_small_or_imprecise_dtypes=True)
         nc.vector.tensor_scalar(ident[:], column[:], row[:], None, EQUAL)
         nc.vector.memset(wb_sc[:].bitcast(I32), 0)
-        nc.vector.memset(wc_sc[:].bitcast(I32), 0)
         nc.vector.memset(v_scales[:].bitcast(I32), 0)
 
         def load_scale_rows(queue, plane, scales, d, first):
@@ -67,40 +70,43 @@ def tile_list_segment_reassortment_fitness_kernel(
                 scales[:, 4 * d : 4 * d + 4, :].rearrange("a r c -> r a c").bitcast(I32),
             )
 
-        wb_w = held([P, kp, 2 * H], U8, "wb_w", "stage5")
-        tab = [held([P, T], I32, "tab%d" % a, "stage%d" % (2 + a)) for a in range(kp)]
+        tab = [held([P, T], I32, "tab%d" % a, (4 * a + 1) * A // 2) for a in range(kp)]
         nc.sync.dma_start(pick[:], offs)
         nc.sync.dma_start(place[:], offs2)
+        wb_w = held([P, kp, 2 * H], U8, "wb_w")
         nc.sync.dma_start(wb_w[:].bitcast(I32), wb_words.rearrange("a p c -> p a c").bitcast(I32))
         for d in range(QUADS):
             load_scale_rows(nc.sync, ts_both[:].rearrange("p (a t) -> p a t", a=kp), tab_scales, d, SHIFT)
         for a in range(kp):
             nc.sync.dma_start(tab[a][:], tab_words[a].rearrange("p t i -> p (t i)").bitcast(I32))
         for d in range(QUADS):
-            load_scale_rows(nc.scalar, wb_sc[:], wb_scales, d, 0)
-        for d in range(QUADS):
-            load_scale_rows(nc.scalar, wc_sc[:], wc_scales, d, 0)
+            load_scale_rows(nc.sync, wb_sc[:], wb_scales, d, 0)
 
-        nc.vector.tensor_copy(ts_second[:].bitcast(I32), ts_both[:, T : 2 * T].bitcast(I32))
+        wc_sc = held([P, kp, H], U8, "wc_sc")
+        nc.gpsimd.memset(wc_sc[:].bitcast(I32), 0)
+        for d in range(QUADS):
+            load_scale_rows(nc.gpsimd, wc_sc[:], wc_scales, d, 0)
+
         nc.vector.tensor_copy(ts_picked[:, 0, :], ts_both[:].indirect(pick[:]))
+        nc.vector.tensor_copy(ts_second[:].bitcast(I32), ts_both[:, T : 2 * T].bitcast(I32))
         nc.vector.tensor_copy(ts_picked[:, 1, :], ts_second[:].indirect(pick[:]))
-        wc_w = held([P, kp, H], I32, "wc_w", "stage0")
-        nc.sync.dma_start(wc_w[:], wc_words.rearrange("a p c i -> p a (c i)").bitcast(I32))
         nc.scalar.dma_start(
             v_scales[:].rearrange("p a j -> p (a j)").bitcast(I32)[0:MOVED],
             ts_picked[:].rearrange("p a j -> p (a j)").bitcast(I32)[SHIFT : SHIFT + MOVED],
         )
-        v_words = [held([P, S], U32, "v_words%d" % a) for a in range(kp)]
+        wc_w = held([P, kp, H], I32, "wc_w", 7 * A)
+        nc.sync.dma_start(wc_w[:], wc_words.rearrange("a p c i -> p a (c i)").bitcast(I32))
+        v_words = [held([P, S], U32, "v_words%d" % a, (8 * A, None)[a]) for a in range(kp)]
         for a in range(kp):
             nc.vector.tensor_copy(v_words[a][:], tab[a][:].bitcast(U32).indirect(pick[:]))
 
-        for i, page in enumerate(pages):
-            (nc.gpsimd if i < 3 else nc.vector).memset(page[:], 0.0)
+        for page in pages:
+            nc.gpsimd.memset(page[:], 0.0)
 
         wa_raw = {}
 
         def load_wa(a, b):
-            wa_raw[a, b] = held([P, PACK, BANK], F32, "wa_raw%d%d" % (a, b), "stage%d" % (1 + kp * b + a))
+            wa_raw[a, b] = held([P, PACK, BANK], F32, "wa_raw%d%d" % (a, b), (kp * b + a) * A)
             nc.sync.dma_start(
                 wa_raw[a, b][:],
                 wa[a * PASS : (a + 1) * PASS, b * BANK : (b + 1) * BANK].rearrange("(p j) c -> p j c", j=PACK),
@@ -119,17 +125,24 @@ def tile_list_segment_reassortment_fitness_kernel(
                     stop=(a == kp - 1),
                 )
 
-        def interleave(copy, raw, name):
+        def round_shares(dst, src, shares):
+            first = 0
+            for copy, count in shares:
+                copy(dst[:, first : first + count], src[:, first : first + count])
+                first = first + count
+
+        def interleave(shares, raw, name):
             grouped = held([P, BANK * PACK], BF16, name)
-            copy(
+            round_shares(
                 grouped[:].rearrange("p (c i j) -> p c j i", i=4, j=PACK),
                 raw[:].rearrange("p j (c i) -> p c j i", i=4),
+                shares,
             )
             return grouped
 
-        def quantise(grouped, name):
-            words = held([P, BANK], U32, name + "_w")
-            scales = held([P, BANK], U8, name + "_s")
+        def quantise(grouped, width, name):
+            words = held([P, width], U32, name + "_w")
+            scales = held([P, width], U8, name + "_s")
             nc.vector.quantize_mx(out=words[:].bitcast(E4M3), scales=scales[:], in_=grouped[:])
             return words, scales
 
@@ -138,7 +151,7 @@ def tile_list_segment_reassortment_fitness_kernel(
 
         def bc_unit(b, jc):
             cols = slice(b * BANK, (b + 1) * BANK)
-            b_bank = psum.tile([P, BANK], F32, name="b_bank", tag="by_scalar")
+            b_bank = psum.tile([P, BANK], F32, name="b_bank", tag="by_scalar", bufs=2)
             project(b_bank, jc, [wb_w[:, a, 2 * b * BANK : 2 * (b + 1) * BANK] for a in range(kp)],
                     [wb_sc[:, a, cols] for a in range(kp)], E2M1)
             c_bank = psum.tile([P, BANK], F32, name="c_bank", tag="by_vector")
@@ -149,77 +162,92 @@ def tile_list_segment_reassortment_fitness_kernel(
             nc.vector.tensor_tensor(bc[b, jc][:], c_bank[:], b_sb[:], MULT)
 
         for b in range(hp):
-            for jc in range(chunks):
-                bc_unit(b, jc)
-
-        for b in range(hp):
             for a in range(kp):
                 load_wa(a, b)
 
-        def h_half(b):
-            h_rows = []
-            for jc in range(chunks):
+        wa_shares = [[(nc.vector.tensor_copy, 64), (nc.vector.tensor_copy, 64)], [(nc.vector.tensor_copy, 64), (nc.vector.tensor_copy, 64)], [(nc.scalar.copy, 32), (nc.scalar.copy, 32), (nc.scalar.copy, 32), (nc.scalar.copy, 32)], [(nc.scalar.copy, 64), (nc.scalar.copy, 64)]]
+        wd_shares = [[(nc.scalar.copy, 64), (nc.scalar.copy, 64)], [(nc.scalar.copy, 80), (nc.vector.tensor_copy, 48)]]
+        pairs = chunks // 2
+        h_q = {}
+        wd_q = {}
+
+        def h_pair(b, pair):
+            turned = psum.tile([P, 2, 2, P], F32, name="turned", tag="by_scalar", bufs=2)
+            for e in range(2):
+                jc = 2 * pair + e
                 a_bank = psum.tile([P, BANK], F32, name="a_bank", tag="by_vector")
                 project(a_bank, jc, [wa_q[a, b][0][:] for a in range(kp)], [wa_q[a, b][1][:] for a in range(kp)], E4M3)
                 h_jr = held([P, BANK], BF16, "h%d%d" % (b, jc))
                 nc.vector.tensor_tensor(h_jr[:], a_bank[:], bc[b, jc][:], MULT)
-                h_rows.append(h_jr)
-            grouped = held([P, S * PACK], BF16, "hT%d" % b)
-            for pair in range(chunks // 2):
-                turned = psum.tile([P, 2, 2, P], F32, name="turned", tag="by_scalar")
-                for e in range(2):
-                    words = h_rows[2 * pair + e][:].bitcast(F32)
-                    for u in range(2):
-                        nc.tensor.transpose(turned[:, e, u, :], words[:, u : 2 * P : 2], ident[:])
-                nc.scalar.copy(
-                    grouped[:].bitcast(F32)[:, pair * BANK : (pair + 1) * BANK].rearrange("p (e j u) -> p e j u", e=2, u=2),
-                    turned[:].rearrange("p e u j -> p e j u"),
-                )
-            return grouped
+                words = h_jr[:].bitcast(F32)
+                for u in range(2):
+                    nc.tensor.transpose(turned[:, e, u, :], words[:, u : 2 * P : 2], ident[:])
+            grouped = held([P, 2 * P * PACK], BF16, "hT%d%d" % (b, pair))
+            nc.scalar.copy(
+                grouped[:].bitcast(F32).rearrange("p (e j u) -> p e j u", e=2, u=2),
+                turned[:].rearrange("p e u j -> p e j u"),
+            )
+            h_q[b, pair] = quantise(grouped, 2 * P, "h_q%d%d" % (b, pair))
 
-        h_q = {}
-        for b in range(hp):
-            for a in range(kp):
-                copy = nc.vector.tensor_copy if (a, b) == (0, 0) else nc.scalar.copy
-                wa_q[a, b] = quantise(interleave(copy, wa_raw[a, b], "wa_g%d%d" % (a, b)), "wa_q%d%d" % (a, b))
-            h_q[b] = quantise(h_half(b), "h_q%d" % b)
-
-        wd_raw = [held([P, PACK, N], F32, "wd_raw%d" % b, "stage%d" % (5 * (1 - b))) for b in range(hp)]
-        for b in range(hp):
-            nc.sync.dma_start(wd_raw[b][:], wd[b * PASS : (b + 1) * PASS, :].rearrange("(p j) n -> p j n", j=PACK))
-        weights = held([P, S], F32, "weights", "stage2")
-        nc.sync.dma_start(weights[:], wgo)
-
-        bias_cols = held([P, PACK], F32, "bias_cols", "stage1")
-        nc.sync.dma_start(bias_cols[:], bias.rearrange("(p i) -> p i", i=PACK))
-
-        wd_q = {}
-        for b in range(hp):
+        def prepare_wd(b):
+            raw = held([P, PACK, N], F32, "wd_raw%d" % b, (4 * A, 5 * A + 64)[b])
+            nc.sync.dma_start(raw[:], wd[b * PASS : (b + 1) * PASS, :].rearrange("(p j) n -> p j n", j=PACK))
             grouped = held([P, N * PACK], BF16, "wd_g%d" % b)
             dst = grouped[:].rearrange("p (i m j) -> p m j i", i=PACK, j=PACK)
-            src = wd_raw[b][:].rearrange("p j (m i) -> p m j i", i=PACK)
-            if b == 0:
-                nc.scalar.copy(dst, src)
-            else:
-                nc.scalar.copy(dst[:, 0:48], src[:, 0:48])
-                nc.vector.tensor_copy(dst[:, 48:P], src[:, 48:P])
-            wd_q[b] = quantise(grouped, "wd_q%d" % b)
+            src = raw[:].rearrange("p j (m i) -> p m j i", i=PACK)
+            round_shares(dst, src, wd_shares[b])
+            wd_q[b] = quantise(grouped, N, "wd_q%d" % b)
+            return raw
+
+        for pair in range(pairs):
+            for b in range(hp):
+                for e in range(2):
+                    bc_unit(b, 2 * pair + e)
+        for b in range(hp):
+            for a in range(kp):
+                grouped = interleave(wa_shares[kp * b + a], wa_raw[a, b], "wa_g%d%d" % (a, b))
+                wa_q[a, b] = quantise(grouped, BANK, "wa_q%d%d" % (a, b))
+        for pair in range(pairs):
+            for b in range(hp):
+                h_pair(b, pair)
+            if pair == 0:
+                for b in range(hp):
+                    wd_last = prepare_wd(b)
+
+        weights = held([P, S], F32, "weights", 0)
+        nc.sync.dma_start(weights[:], wgo)
+        bias_cols = held([P, PACK], F32, "bias_cols", 5 * A)
+        nc.sync.dma_start(bias_cols[:], bias.rearrange("(p i) -> p i", i=PACK))
 
         rows = out.rearrange("(p i) t -> p i t", i=PACK)
-        for i in range(PACK):
-            cols = slice(i * P, (i + 1) * P)
-            y_bank = psum.tile([P, S], F32, name="y_bank", tag="by_scalar")
-            for b in range(hp):
-                nc.tensor.matmul_mx(
-                    out=y_bank[:],
-                    lhsT=wd_q[b][0][:, cols].bitcast(E4M3),
-                    lhsT_scale=wd_q[b][1][:, cols],
-                    rhs=h_q[b][0][:].bitcast(E4M3),
-                    rhs_scale=h_q[b][1][:],
-                    start=(b == 0),
-                    stop=(b == hp - 1),
+        half = S // pairs
+        ys = {}
+        for pair in range(pairs):
+            for i2 in range(PACK // 2):
+                y_bank = psum.tile([P, 2, half], F32, name="y_bank", tag="results", bufs=2)
+                for e in range(2):
+                    cols = slice((2 * i2 + e) * P, (2 * i2 + e + 1) * P)
+                    for b in range(hp):
+                        nc.tensor.matmul_mx(
+                            out=y_bank[:, e, :],
+                            lhsT=wd_q[b][0][:, cols].bitcast(E4M3),
+                            lhsT_scale=wd_q[b][1][:, cols],
+                            rhs=h_q[b, pair][0][:].bitcast(E4M3),
+                            rhs_scale=h_q[b, pair][1][:],
+                            start=(b == 0),
+                            stop=(b == hp - 1),
+                        )
+                for e in range(2):
+                    i = 2 * i2 + e
+                    ys[pair, i] = held([P, half], F32, "y%d%d" % (pair, i))
+                    nc.scalar.activation(ys[pair, i][:], y_bank[:, e, :], IDENTITY, bias=bias_cols[:, i : i + 1])
+        for pair in range(pairs):
+            for i in range(PACK):
+                nc.vector.tensor_tensor(
+                    pages[i][:].indirect(place[:, pair * half // 16 : (pair + 1) * half // 16]),
+                    ys[pair, i][:],
+                    weights[:, pair * half : (pair + 1) * half],
+                    MULT,
                 )
-            y = held([P, S], F32, "y%d" % i)
-            nc.scalar.activation(y[:], y_bank[:], IDENTITY, bias=bias_cols[:, i : i + 1])
-            nc.vector.tensor_tensor(pages[i][:].indirect(place[:]), y[:], weights[:], MULT)
-            nc.sync.dma_start(rows[:, i, :], pages[i][:])
+                if pair == pairs - 1:
+                    nc.sync.dma_start(rows[:, i, :], pages[i][:])

@@ -22,41 +22,57 @@ PACK = 4
 PASS = P * PACK
 BANK = 512
 QUADS = 4
-SHIFT = 14
+GROUP = 16
+K_PASSES = K // PASS
+R_PASSES = H // PASS
+HALVES = 2
+HALF = S // HALVES
+CHUNKS = HALF // P
+
+SHIFT = GROUP - 2
 MOVED = 112
-A = 8192
+
+PIECE = PACK * BANK * 4
+AT_WA = 0
+AT_WD = 4 * PIECE
+BIAS_ROOM = 64
+OVERLAP = 256
+AT_WC = 7 * PIECE
+
+STEP = P // 2
+WD_LAST_ON_SCALAR = 80
 
 
 def tile_list_segment_reassortment_fitness_kernel(
     tc, tab_words, tab_scales, offs, wa, wb_words, wb_scales, wc_words, wc_scales, wd, bias, offs2, wgo, out
 ):
     nc = tc.nc
-    kp, hp, chunks = K // PASS, H // PASS, S // P
 
     with ExitStack() as ctx:
         keep = ctx.enter_context(tc.tile_pool(name="keep", bufs=1))
         stage = ctx.enter_context(tc.tile_pool(name="stage", bufs=1))
         ring = ctx.enter_context(tc.tile_pool(name="ring", bufs=3))
-        psum = ctx.enter_context(tc.psum_pool(name="psum", bufs=4))
+        psum = ctx.enter_context(tc.psum_pool(name="psum", bufs=2))
 
-        def held(shape, dtype, name, offset=None):
-            if offset is None:
-                return keep.tile(shape, dtype, name=name, align_bytes=64)
+        def held(shape, dtype, name):
+            return keep.tile(shape, dtype, name=name, align_bytes=64)
+
+        def staged(shape, dtype, name, offset):
             return stage.tile(shape, dtype, name=name, align_bytes=64, offset=offset)
 
-        pick = held([P, S // 16], U16, "pick")
-        place = held([P, S // 16], U16, "place")
-        ts_both = held([P, kp * T], U8, "ts_both")
-        ts_second = held([P, T], U8, "ts_second", 8 * A - 1024)
-        ts_picked = held([P, kp, S], U8, "ts_picked", 5 * A - 256)
-        v_scales = held([P, kp, S], U8, "v_scales")
-        wb_sc = held([P, kp, H], U8, "wb_sc")
+        pick = held([P, S // GROUP], U16, "pick")
+        place = held([P, S // GROUP], U16, "place")
+        ts_both = held([P, K_PASSES * T], U8, "ts_both")
+        ts_second = staged([P, T], U8, "ts_second", AT_WC + PIECE - T // 2)
+        ts_picked = staged([P, K_PASSES, S], U8, "ts_picked", AT_WD + PIECE - OVERLAP)
+        v_scales = held([P, K_PASSES, S], U8, "v_scales")
+        wb_sc = held([P, K_PASSES, H], U8, "wb_sc")
         pages = [held([P, T2], F32, "page%d" % i) for i in range(PACK)]
 
         nc.gpsimd.memset(ts_both[:, 0:T].bitcast(I32), 0)
         nc.vector.memset(ts_both[:, T : 2 * T].bitcast(I32), 0)
-        column = held([P, P], F32, "column", A // 2)
-        row = held([P, 1], F32, "row", 5 * A // 2)
+        column = staged([P, P], F32, "column", AT_WA + PIECE // 2)
+        row = staged([P, 1], F32, "row", AT_WA + 5 * PIECE // 2)
         ident = held([P, P], F32, "ident")
         nc.gpsimd.iota(row[:], [[0, 1]], base=0, channel_multiplier=1, allow_small_or_imprecise_dtypes=True)
         nc.gpsimd.iota(column[:], [[1, P]], base=0, channel_multiplier=0, allow_small_or_imprecise_dtypes=True)
@@ -64,81 +80,69 @@ def tile_list_segment_reassortment_fitness_kernel(
         nc.vector.memset(wb_sc[:].bitcast(I32), 0)
         nc.vector.memset(v_scales[:].bitcast(I32), 0)
 
-        def load_scale_rows(queue, plane, scales, d, first):
-            queue.dma_start(
-                plane.bitcast(I32)[32 * d + first : 32 * d + first + 4],
-                scales[:, 4 * d : 4 * d + 4, :].rearrange("a r c -> r a c").bitcast(I32),
-            )
+        def load_scale_rows(queue, tile, scales, first):
+            for d in range(QUADS):
+                queue.dma_start(
+                    tile.bitcast(I32)[32 * d + first : 32 * d + first + 4],
+                    scales[:, 4 * d : 4 * d + 4, :].rearrange("g x c -> x g c").bitcast(I32),
+                )
 
-        tab = [held([P, T], I32, "tab%d" % a, (4 * a + 1) * A // 2) for a in range(kp)]
+        tab = [staged([P, T], I32, "tab%d" % g, AT_WA + (4 * g + 1) * PIECE // 2) for g in range(K_PASSES)]
         nc.sync.dma_start(pick[:], offs)
         nc.sync.dma_start(place[:], offs2)
-        wb_w = held([P, kp, 2 * H], U8, "wb_w")
-        nc.sync.dma_start(wb_w[:].bitcast(I32), wb_words.rearrange("a p c -> p a c").bitcast(I32))
-        for d in range(QUADS):
-            load_scale_rows(nc.sync, ts_both[:].rearrange("p (a t) -> p a t", a=kp), tab_scales, d, SHIFT)
-        for a in range(kp):
-            nc.sync.dma_start(tab[a][:], tab_words[a].rearrange("p t i -> p (t i)").bitcast(I32))
-        for d in range(QUADS):
-            load_scale_rows(nc.sync, wb_sc[:], wb_scales, d, 0)
-
-        wc_sc = held([P, kp, H], U8, "wc_sc")
+        wb_w = held([P, K_PASSES, 2 * H], U8, "wb_w")
+        nc.sync.dma_start(wb_w[:].bitcast(I32), wb_words.rearrange("g p c -> p g c").bitcast(I32))
+        load_scale_rows(nc.sync, ts_both[:].rearrange("p (g t) -> p g t", g=K_PASSES), tab_scales, SHIFT)
+        for g in range(K_PASSES):
+            nc.sync.dma_start(tab[g][:], tab_words[g].rearrange("p t i -> p (t i)").bitcast(I32))
+        load_scale_rows(nc.sync, wb_sc[:], wb_scales, 0)
+        wc_sc = held([P, K_PASSES, H], U8, "wc_sc")
         nc.gpsimd.memset(wc_sc[:].bitcast(I32), 0)
-        for d in range(QUADS):
-            load_scale_rows(nc.gpsimd, wc_sc[:], wc_scales, d, 0)
+        load_scale_rows(nc.gpsimd, wc_sc[:], wc_scales, 0)
 
         nc.vector.tensor_copy(ts_picked[:, 0, :], ts_both[:].indirect(pick[:]))
         nc.vector.tensor_copy(ts_second[:].bitcast(I32), ts_both[:, T : 2 * T].bitcast(I32))
         nc.vector.tensor_copy(ts_picked[:, 1, :], ts_second[:].indirect(pick[:]))
-        nc.scalar.dma_start(
-            v_scales[:].rearrange("p a j -> p (a j)").bitcast(I32)[0:MOVED],
-            ts_picked[:].rearrange("p a j -> p (a j)").bitcast(I32)[SHIFT : SHIFT + MOVED],
+        nc.sync.dma_start(
+            v_scales[:].rearrange("p g j -> p (g j)").bitcast(I32)[0:MOVED],
+            ts_picked[:].rearrange("p g j -> p (g j)").bitcast(I32)[SHIFT : SHIFT + MOVED],
         )
-        wc_w = held([P, kp, H], I32, "wc_w", 7 * A)
-        nc.sync.dma_start(wc_w[:], wc_words.rearrange("a p c i -> p a (c i)").bitcast(I32))
-        v_words = [held([P, S], U32, "v_words%d" % a, (8 * A, None)[a]) for a in range(kp)]
-        for a in range(kp):
-            nc.vector.tensor_copy(v_words[a][:], tab[a][:].bitcast(U32).indirect(pick[:]))
+        wc_w = staged([P, K_PASSES, H], I32, "wc_w", AT_WC)
+        nc.sync.dma_start(wc_w[:], wc_words.rearrange("g p c i -> p g (c i)").bitcast(I32))
+        v_words = [staged([P, S], U32, "v_words0", AT_WC + PIECE), held([P, S], U32, "v_words1")]
+        for g in range(K_PASSES):
+            nc.vector.tensor_copy(v_words[g][:], tab[g][:].bitcast(U32).indirect(pick[:]))
 
         for page in pages:
             nc.gpsimd.memset(page[:], 0.0)
 
         wa_raw = {}
-
-        def load_wa(a, b):
-            wa_raw[a, b] = held([P, PACK, BANK], F32, "wa_raw%d%d" % (a, b), (kp * b + a) * A)
-            nc.sync.dma_start(
-                wa_raw[a, b][:],
-                wa[a * PASS : (a + 1) * PASS, b * BANK : (b + 1) * BANK].rearrange("(p j) c -> p j c", j=PACK),
-            )
-
-        def project(bank, jc, words, scales, fmt):
-            cols = slice(jc * P, (jc + 1) * P)
-            for a in range(kp):
-                nc.tensor.matmul_mx(
-                    out=bank[:],
-                    lhsT=v_words[a][:, cols].bitcast(E4M3),
-                    lhsT_scale=v_scales[:, a, cols],
-                    rhs=words[a].bitcast(fmt),
-                    rhs_scale=scales[a],
-                    start=(a == 0),
-                    stop=(a == kp - 1),
+        for rp in range(R_PASSES):
+            for g in range(K_PASSES):
+                wa_raw[g, rp] = staged([P, PACK, BANK], F32, "wa_raw%d%d" % (g, rp), AT_WA + (K_PASSES * rp + g) * PIECE)
+                nc.sync.dma_start(
+                    wa_raw[g, rp][:],
+                    wa[g * PASS : (g + 1) * PASS, rp * BANK : (rp + 1) * BANK].rearrange("(p t) c -> p t c", t=PACK),
                 )
 
-        def round_shares(dst, src, shares):
+        def project(bank, chunk, words, scales, fmt):
+            cols = slice(chunk * P, (chunk + 1) * P)
+            for g in range(K_PASSES):
+                nc.tensor.matmul_mx(
+                    out=bank[:],
+                    lhsT=v_words[g][:, cols].bitcast(E4M3),
+                    lhsT_scale=v_scales[:, g, cols],
+                    rhs=words[g].bitcast(fmt),
+                    rhs_scale=scales[g],
+                    start=(g == 0),
+                    stop=(g == K_PASSES - 1),
+                )
+
+        def round_in_shares(dst, src, shares):
             first = 0
             for copy, count in shares:
                 copy(dst[:, first : first + count], src[:, first : first + count])
                 first = first + count
-
-        def interleave(shares, raw, name):
-            grouped = held([P, BANK * PACK], BF16, name)
-            round_shares(
-                grouped[:].rearrange("p (c i j) -> p c j i", i=4, j=PACK),
-                raw[:].rearrange("p j (c i) -> p c j i", i=4),
-                shares,
-            )
-            return grouped
 
         def quantise(grouped, width, name):
             words = held([P, width], U32, name + "_w")
@@ -146,108 +150,128 @@ def tile_list_segment_reassortment_fitness_kernel(
             nc.vector.quantize_mx(out=words[:].bitcast(E4M3), scales=scales[:], in_=grouped[:])
             return words, scales
 
+        def by_pairs(bank):
+            return bank[:].rearrange("p (m u e) -> p u m e", u=2, e=2)
+
+        def as_pairs(view):
+            return view.rearrange("p (u m e) -> p u m e", u=2, e=2)
+
         bc = {}
         wa_q = {}
-
-        def bc_unit(b, jc):
-            cols = slice(b * BANK, (b + 1) * BANK)
-            b_bank = psum.tile([P, BANK], F32, name="b_bank", tag="by_scalar", bufs=2)
-            project(b_bank, jc, [wb_w[:, a, 2 * b * BANK : 2 * (b + 1) * BANK] for a in range(kp)],
-                    [wb_sc[:, a, cols] for a in range(kp)], E2M1)
-            c_bank = psum.tile([P, BANK], F32, name="c_bank", tag="by_vector")
-            project(c_bank, jc, [wc_w[:, a, cols] for a in range(kp)], [wc_sc[:, a, cols] for a in range(kp)], E4M3)
-            b_sb = ring.tile([P, BANK], F32, name="b_sb")
-            nc.scalar.copy(b_sb[:], b_bank[:])
-            bc[b, jc] = held([P, BANK], F32, "bc%d%d" % (b, jc))
-            nc.vector.tensor_tensor(bc[b, jc][:], c_bank[:], b_sb[:], MULT)
-
-        for b in range(hp):
-            for a in range(kp):
-                load_wa(a, b)
-
-        wa_shares = [[(nc.vector.tensor_copy, 64), (nc.vector.tensor_copy, 64)], [(nc.vector.tensor_copy, 64), (nc.vector.tensor_copy, 64)], [(nc.scalar.copy, 32), (nc.scalar.copy, 32), (nc.scalar.copy, 32), (nc.scalar.copy, 32)], [(nc.scalar.copy, 64), (nc.scalar.copy, 64)]]
-        wd_shares = [[(nc.scalar.copy, 64), (nc.scalar.copy, 64)], [(nc.scalar.copy, 80), (nc.vector.tensor_copy, 48)]]
-        pairs = chunks // 2
         h_q = {}
         wd_q = {}
+        ys = {}
 
-        def h_pair(b, pair):
-            turned = psum.tile([P, 2, 2, P], F32, name="turned", tag="by_scalar", bufs=2)
-            for e in range(2):
-                jc = 2 * pair + e
-                a_bank = psum.tile([P, BANK], F32, name="a_bank", tag="by_vector")
-                project(a_bank, jc, [wa_q[a, b][0][:] for a in range(kp)], [wa_q[a, b][1][:] for a in range(kp)], E4M3)
-                h_jr = held([P, BANK], BF16, "h%d%d" % (b, jc))
-                nc.vector.tensor_tensor(h_jr[:], a_bank[:], bc[b, jc][:], MULT)
-                words = h_jr[:].bitcast(F32)
-                for u in range(2):
-                    nc.tensor.transpose(turned[:, e, u, :], words[:, u : 2 * P : 2], ident[:])
-            grouped = held([P, 2 * P * PACK], BF16, "hT%d%d" % (b, pair))
-            nc.scalar.copy(
-                grouped[:].bitcast(F32).rearrange("p (e j u) -> p e j u", e=2, u=2),
-                turned[:].rearrange("p e u j -> p e j u"),
+        def multiply_b_c(rp, chunk):
+            cols = slice(rp * BANK, (rp + 1) * BANK)
+            b_bank = psum.tile([P, BANK], F32, name="b_bank", tag="b_then_y")
+            wb_cols = slice(2 * rp * BANK, 2 * (rp + 1) * BANK)
+            project(b_bank, chunk, [wb_w[:, g, wb_cols] for g in range(K_PASSES)],
+                    [wb_sc[:, g, cols] for g in range(K_PASSES)], E2M1)
+            c_bank = psum.tile([P, BANK], F32, name="c_bank")
+            project(c_bank, chunk, [wc_w[:, g, cols] for g in range(K_PASSES)],
+                    [wc_sc[:, g, cols] for g in range(K_PASSES)], E4M3)
+            b_sb = ring.tile([P, BANK], F32, name="b_sb")
+            nc.scalar.copy(as_pairs(b_sb[:]), by_pairs(b_bank))
+            bc[rp, chunk] = held([P, BANK], F32, "bc%d%d" % (rp, chunk))
+            nc.vector.tensor_tensor(as_pairs(bc[rp, chunk][:]), by_pairs(c_bank), as_pairs(b_sb[:]), MULT)
+
+        def prepare_wa(g, rp, shares):
+            grouped = held([P, BANK * PACK], BF16, "wa_g%d%d" % (g, rp))
+            round_in_shares(
+                grouped[:].rearrange("p (c i t) -> p c t i", i=4, t=PACK),
+                wa_raw[g, rp][:].rearrange("p t (c i) -> p c t i", i=4),
+                shares,
             )
-            h_q[b, pair] = quantise(grouped, 2 * P, "h_q%d%d" % (b, pair))
+            wa_q[g, rp] = quantise(grouped, BANK, "wa_q%d%d" % (g, rp))
 
-        def prepare_wd(b):
-            raw = held([P, PACK, N], F32, "wd_raw%d" % b, (4 * A, 5 * A + 64)[b])
-            nc.sync.dma_start(raw[:], wd[b * PASS : (b + 1) * PASS, :].rearrange("(p j) n -> p j n", j=PACK))
-            grouped = held([P, N * PACK], BF16, "wd_g%d" % b)
-            dst = grouped[:].rearrange("p (i m j) -> p m j i", i=PACK, j=PACK)
-            src = raw[:].rearrange("p j (m i) -> p m j i", i=PACK)
-            round_shares(dst, src, wd_shares[b])
-            wd_q[b] = quantise(grouped, N, "wd_q%d" % b)
-            return raw
+        def make_h(rp, half, h_jr):
+            for s in range(CHUNKS):
+                chunk = CHUNKS * half + s
+                a_bank = psum.tile([P, BANK], F32, name="a_bank")
+                project(a_bank, chunk, [wa_q[g, rp][0][:] for g in range(K_PASSES)],
+                        [wa_q[g, rp][1][:] for g in range(K_PASSES)], E4M3)
+                nc.vector.tensor_tensor(as_pairs(h_jr[:, s, :]), by_pairs(a_bank), as_pairs(bc[rp, chunk][:]), MULT)
+            words = h_jr[:].rearrange("p s r -> p (s r)").bitcast(F32)
+            turned = psum.tile([P, CHUNKS, 2, P], F32, name="turned")
+            for s in range(CHUNKS):
+                for u in range(2):
+                    nc.tensor.transpose(turned[:, s, u, :], words[:, (2 * s + u) * P : (2 * s + u + 1) * P], ident[:])
+            grouped = held([P, HALF * PACK], BF16, "hT%d%d" % (rp, half))
+            nc.scalar.copy(
+                grouped[:].bitcast(F32).rearrange("p (s j u) -> p s j u", s=CHUNKS, u=2),
+                turned[:].rearrange("p s u j -> p s j u"),
+            )
+            h_q[rp, half] = quantise(grouped, HALF, "h_q%d%d" % (rp, half))
 
-        for pair in range(pairs):
-            for b in range(hp):
-                for e in range(2):
-                    bc_unit(b, 2 * pair + e)
-        for b in range(hp):
-            for a in range(kp):
-                grouped = interleave(wa_shares[kp * b + a], wa_raw[a, b], "wa_g%d%d" % (a, b))
-                wa_q[a, b] = quantise(grouped, BANK, "wa_q%d%d" % (a, b))
-        for pair in range(pairs):
-            for b in range(hp):
-                h_pair(b, pair)
-            if pair == 0:
-                for b in range(hp):
-                    wd_last = prepare_wd(b)
+        def prepare_wd(rp, offset, shares):
+            raw = staged([P, PACK, N], F32, "wd_raw%d" % rp, offset)
+            nc.sync.dma_start(raw[:], wd[rp * PASS : (rp + 1) * PASS, :].rearrange("(p t) n -> p t n", t=PACK))
+            grouped = held([P, N * PACK], BF16, "wd_g%d" % rp)
+            round_in_shares(
+                grouped[:].rearrange("p (i m t) -> p m t i", i=PACK, t=PACK),
+                raw[:].rearrange("p t (m i) -> p m t i", i=PACK),
+                shares,
+            )
+            wd_q[rp] = quantise(grouped, N, "wd_q%d" % rp)
 
-        weights = held([P, S], F32, "weights", 0)
+        def make_y(half, first, tiles):
+            y_bank = psum.tile([P, 2, HALF], F32, name="y_bank", tag="b_then_y")
+            for i in (first, first + 1):
+                cols = slice(i * P, (i + 1) * P)
+                for rp in range(R_PASSES):
+                    nc.tensor.matmul_mx(
+                        out=y_bank[:, i - first, :],
+                        lhsT=wd_q[rp][0][:, cols].bitcast(E4M3),
+                        lhsT_scale=wd_q[rp][1][:, cols],
+                        rhs=h_q[rp, half][0][:].bitcast(E4M3),
+                        rhs_scale=h_q[rp, half][1][:],
+                        start=(rp == 0),
+                        stop=(rp == R_PASSES - 1),
+                    )
+            for i in (first, first + 1):
+                ys[half, i] = tiles[i - first]
+                nc.scalar.activation(ys[half, i][:], y_bank[:, i - first, :], IDENTITY, bias=bias_cols[:, i : i + 1])
+
+        def h_tile(rp, half):
+            return held([P, CHUNKS, BANK], BF16, "h%d%d" % (rp, half))
+
+        def y_tiles(half, first):
+            return [held([P, HALF], F32, "y%d%d" % (half, i)) for i in (first, first + 1)]
+
+        on_vector, on_scalar = nc.vector.tensor_copy, nc.scalar.copy
+        for half in range(HALVES):
+            for rp in range(R_PASSES):
+                for s in range(CHUNKS):
+                    multiply_b_c(rp, CHUNKS * half + s)
+        prepare_wa(0, 0, [(on_vector, STEP), (on_vector, STEP)])
+        prepare_wa(1, 0, [(on_vector, STEP), (on_vector, STEP)])
+        prepare_wa(0, 1, [(on_scalar, STEP), (on_scalar, STEP)])
+        prepare_wa(1, 1, [(on_scalar, P)])
+        for rp in range(R_PASSES):
+            make_h(rp, 0, h_tile(rp, 0))
+        prepare_wd(0, AT_WD, [(on_scalar, P)])
+        prepare_wd(1, AT_WD + PIECE + BIAS_ROOM, [(on_scalar, WD_LAST_ON_SCALAR), (on_vector, P - WD_LAST_ON_SCALAR)])
+        weights = staged([P, S], F32, "weights", AT_WA)
         nc.sync.dma_start(weights[:], wgo)
-        bias_cols = held([P, PACK], F32, "bias_cols", 5 * A)
+        bias_cols = staged([P, PACK], F32, "bias_cols", AT_WD + PIECE)
         nc.sync.dma_start(bias_cols[:], bias.rearrange("(p i) -> p i", i=PACK))
 
+        make_y(0, 0, y_tiles(0, 0))
+        make_h(0, 1, h_tile(0, 1))
+        make_h(1, 1, staged([P, CHUNKS, BANK], BF16, "h_last", AT_WC))
+        make_y(0, 2, [staged([P, HALF], F32, "y_late%d" % e, AT_WC + 4 * HALF * e) for e in range(2)])
+        for first in range(0, PACK, 2):
+            make_y(1, first, y_tiles(1, first))
+
         rows = out.rearrange("(p i) t -> p i t", i=PACK)
-        half = S // pairs
-        ys = {}
-        for pair in range(pairs):
-            for i2 in range(PACK // 2):
-                y_bank = psum.tile([P, 2, half], F32, name="y_bank", tag="results", bufs=2)
-                for e in range(2):
-                    cols = slice((2 * i2 + e) * P, (2 * i2 + e + 1) * P)
-                    for b in range(hp):
-                        nc.tensor.matmul_mx(
-                            out=y_bank[:, e, :],
-                            lhsT=wd_q[b][0][:, cols].bitcast(E4M3),
-                            lhsT_scale=wd_q[b][1][:, cols],
-                            rhs=h_q[b, pair][0][:].bitcast(E4M3),
-                            rhs_scale=h_q[b, pair][1][:],
-                            start=(b == 0),
-                            stop=(b == hp - 1),
-                        )
-                for e in range(2):
-                    i = 2 * i2 + e
-                    ys[pair, i] = held([P, half], F32, "y%d%d" % (pair, i))
-                    nc.scalar.activation(ys[pair, i][:], y_bank[:, e, :], IDENTITY, bias=bias_cols[:, i : i + 1])
-        for pair in range(pairs):
+        for half in range(HALVES):
             for i in range(PACK):
                 nc.vector.tensor_tensor(
-                    pages[i][:].indirect(place[:, pair * half // 16 : (pair + 1) * half // 16]),
-                    ys[pair, i][:],
-                    weights[:, pair * half : (pair + 1) * half],
+                    pages[i][:].indirect(place[:, half * HALF // GROUP : (half + 1) * HALF // GROUP]),
+                    ys[half, i][:],
+                    weights[:, half * HALF : (half + 1) * HALF],
                     MULT,
                 )
-                if pair == pairs - 1:
+                if half == HALVES - 1:
                     nc.sync.dma_start(rows[:, i, :], pages[i][:])

@@ -14,6 +14,7 @@ U8 = mybir.dt.uint8
 E4M3 = mybir.dt.float8_e4m3fn_x4
 E2M1 = mybir.dt.float4_e2m1fn_x4
 MULT = mybir.AluOpType.mult
+ADD = mybir.AluOpType.add
 EQUAL = mybir.AluOpType.is_equal
 IDENTITY = mybir.ActivationFunctionType.Identity
 
@@ -33,14 +34,34 @@ SHIFT = GROUP - 2
 MOVED = 112
 
 PIECE = PACK * BANK * 4
-AT_WA = 0
-AT_WD = 4 * PIECE
-BIAS_ROOM = 64
-OVERLAP = 256
-AT_WC = 7 * PIECE
-
-STEP = P // 2
-WD_LAST_ON_SCALAR = 80
+PAGE = 4 * T2
+EDGE = 64
+AT_V = 0
+AT_TS = AT_V
+AT_WA00 = 1024
+AT_WC0 = AT_WA00 + PIECE
+AT_TS2 = AT_WC0
+AT_WB1 = 2 * PIECE
+AT_WC1 = AT_WB1 + 2048
+AT_WA10 = AT_WC1 + 4096
+AT_TAB0 = AT_WB1 + 2048 - EDGE
+AT_WA01 = AT_WA10 + PIECE
+AT_PAGES = AT_WA01 + PIECE
+AT_WA11 = AT_PAGES + PAGE
+AT_TAB1 = AT_PAGES - 2048
+AT_WA = [AT_WA00, AT_WA10, AT_WA01, AT_WA11]
+AT_WD0 = AT_WA11 + PIECE
+AT_BIAS = AT_WD0 + PIECE
+AT_WD = [AT_WD0, AT_BIAS + EDGE]
+AT_WGO = AT_WA00 + 4096
+AT_WC = [AT_WC0, AT_WC1]
+AT_Y = AT_WD[1] + PIECE
+V_ON = {(0, 0): AT_V}
+B_ON = {}
+BC_ON = {}
+HT_ON = {}
+H_ON = {(1, 1): AT_Y}
+Y_ON = {(0, 2): AT_Y, (0, 3): AT_Y + 1024}
 
 
 def tile_list_segment_reassortment_fitness_kernel(
@@ -51,7 +72,6 @@ def tile_list_segment_reassortment_fitness_kernel(
     with ExitStack() as ctx:
         keep = ctx.enter_context(tc.tile_pool(name="keep", bufs=1))
         stage = ctx.enter_context(tc.tile_pool(name="stage", bufs=1))
-        ring = ctx.enter_context(tc.tile_pool(name="ring", bufs=3))
         psum = ctx.enter_context(tc.psum_pool(name="psum", bufs=2))
 
         def held(shape, dtype, name):
@@ -60,23 +80,35 @@ def tile_list_segment_reassortment_fitness_kernel(
         def staged(shape, dtype, name, offset):
             return stage.tile(shape, dtype, name=name, align_bytes=64, offset=offset)
 
+        def placed(shape, dtype, name, offset):
+            return held(shape, dtype, name) if offset is None else staged(shape, dtype, name, offset)
+
         pick = held([P, S // GROUP], U16, "pick")
         place = held([P, S // GROUP], U16, "place")
-        ts_both = held([P, K_PASSES * T], U8, "ts_both")
-        ts_second = staged([P, T], U8, "ts_second", AT_WC + PIECE - T // 2)
-        ts_picked = staged([P, K_PASSES, S], U8, "ts_picked", AT_WD + PIECE - OVERLAP)
+        ts_both = staged([P, K_PASSES * T], U8, "ts_both", AT_TS)
+        ts_picked = staged([P, K_PASSES, S], U8, "ts_picked", AT_BIAS - 512)
         v_scales = held([P, K_PASSES, S], U8, "v_scales")
-        wb_sc = held([P, K_PASSES, H], U8, "wb_sc")
-        pages = [held([P, T2], F32, "page%d" % i) for i in range(PACK)]
+        wc_sc = held([P, K_PASSES, H], U8, "wc_sc")
+        tab = {}
 
-        nc.gpsimd.memset(ts_both[:, 0:T].bitcast(I32), 0)
-        nc.vector.memset(ts_both[:, T : 2 * T].bitcast(I32), 0)
-        column = staged([P, P], F32, "column", AT_WA + PIECE // 2)
-        row = staged([P, 1], F32, "row", AT_WA + 5 * PIECE // 2)
-        ident = held([P, P], F32, "ident")
-        nc.gpsimd.iota(row[:], [[0, 1]], base=0, channel_multiplier=1, allow_small_or_imprecise_dtypes=True)
-        nc.gpsimd.iota(column[:], [[1, P]], base=0, channel_multiplier=0, allow_small_or_imprecise_dtypes=True)
-        nc.vector.tensor_scalar(ident[:], column[:], row[:], None, EQUAL)
+        def load_table(g, offset):
+            tab[g] = staged([P, T], I32, "tab%d" % g, offset)
+            nc.sync.dma_start(tab[g][:], tab_words[g].rearrange("p t i -> p (t i)").bitcast(I32))
+
+        nc.sync.dma_start(pick[:], offs)
+        wb_w = {}
+
+        def load_wb(rp, offset):
+            wb_w[rp] = placed([P, K_PASSES, 2 * BANK], U8, "wb_w%d" % rp, offset)
+            cols = wb_words[:, :, 2 * rp * BANK : 2 * (rp + 1) * BANK]
+            nc.sync.dma_start(wb_w[rp][:].bitcast(I32), cols.rearrange("g p c -> p g c").bitcast(I32))
+
+        load_wb(0, None)
+
+        nc.gpsimd.memset(ts_both[:, 0 : T // 2].bitcast(I32), 0)
+        nc.vector.memset(ts_both[:, T // 2 : 2 * T].bitcast(I32), 0)
+        ts_second = staged([P, T], U8, "ts_second", AT_TS2)
+        wb_sc = held([P, K_PASSES, H], U8, "wb_sc")
         nc.vector.memset(wb_sc[:].bitcast(I32), 0)
         nc.vector.memset(v_scales[:].bitcast(I32), 0)
 
@@ -87,50 +119,80 @@ def tile_list_segment_reassortment_fitness_kernel(
                     scales[:, 4 * d : 4 * d + 4, :].rearrange("g x c -> x g c").bitcast(I32),
                 )
 
-        tab = [staged([P, T], I32, "tab%d" % g, AT_WA + (4 * g + 1) * PIECE // 2) for g in range(K_PASSES)]
-        nc.sync.dma_start(pick[:], offs)
-        nc.sync.dma_start(place[:], offs2)
-        wb_w = held([P, K_PASSES, 2 * H], U8, "wb_w")
-        nc.sync.dma_start(wb_w[:].bitcast(I32), wb_words.rearrange("g p c -> p g c").bitcast(I32))
         load_scale_rows(nc.sync, ts_both[:].rearrange("p (g t) -> p g t", g=K_PASSES), tab_scales, SHIFT)
-        for g in range(K_PASSES):
-            nc.sync.dma_start(tab[g][:], tab_words[g].rearrange("p t i -> p (t i)").bitcast(I32))
-        load_scale_rows(nc.sync, wb_sc[:], wb_scales, 0)
-        wc_sc = held([P, K_PASSES, H], U8, "wc_sc")
         nc.gpsimd.memset(wc_sc[:].bitcast(I32), 0)
         load_scale_rows(nc.gpsimd, wc_sc[:], wc_scales, 0)
+        load_table(0, AT_TAB0)
+        load_table(1, AT_TAB1)
+        wc_w = {}
 
-        nc.vector.tensor_copy(ts_picked[:, 0, :], ts_both[:].indirect(pick[:]))
-        nc.vector.tensor_copy(ts_second[:].bitcast(I32), ts_both[:, T : 2 * T].bitcast(I32))
-        nc.vector.tensor_copy(ts_picked[:, 1, :], ts_second[:].indirect(pick[:]))
-        nc.sync.dma_start(
-            v_scales[:].rearrange("p g j -> p (g j)").bitcast(I32)[0:MOVED],
-            ts_picked[:].rearrange("p g j -> p (g j)").bitcast(I32)[SHIFT : SHIFT + MOVED],
-        )
-        wc_w = staged([P, K_PASSES, H], I32, "wc_w", AT_WC)
-        nc.sync.dma_start(wc_w[:], wc_words.rearrange("g p c i -> p g (c i)").bitcast(I32))
-        v_words = [staged([P, S], U32, "v_words0", AT_WC + PIECE), held([P, S], U32, "v_words1")]
-        for g in range(K_PASSES):
-            nc.vector.tensor_copy(v_words[g][:], tab[g][:].bitcast(U32).indirect(pick[:]))
+        def load_wc(rp, offset):
+            wc_w[rp] = staged([P, K_PASSES, BANK], I32, "wc_w%d" % rp, offset)
+            cols = wc_words[:, :, rp * BANK : (rp + 1) * BANK, :]
+            nc.sync.dma_start(wc_w[rp][:], cols.rearrange("g p c i -> p g (c i)").bitcast(I32))
 
-        for page in pages:
-            nc.gpsimd.memset(page[:], 0.0)
+        load_scale_rows(nc.sync, wb_sc[:], wb_scales, 0)
+
+        ones = held([P, P], F32, "ones")
+        column = held([P, P], F32, "column")
+        row = held([P, P], F32, "row")
+        ident = held([P, P], F32, "ident")
+        nc.vector.memset(ones[:], 1.0)
+        nc.vector.tensor_tensor_scan(column[:], ones[:], ones[:], 0.0, MULT, ADD)
+        nc.vector.transpose(row[:], column[:])
+        for d in range(QUADS):
+            part = slice(32 * d, 32 * (d + 1))
+            nc.vector.tensor_scalar(ident[part, :], column[part, :], row[part, 32 * d : 32 * d + 1], None, EQUAL)
 
         wa_raw = {}
-        for rp in range(R_PASSES):
+
+        def load_wa(g, rp):
+            wa_raw[g, rp] = staged([P, PACK, BANK], F32, "wa_raw%d%d" % (g, rp), AT_WA[K_PASSES * rp + g])
+            rows = wa[g * PASS : (g + 1) * PASS, rp * BANK : (rp + 1) * BANK]
+            nc.sync.dma_start(wa_raw[g, rp][:], rows.rearrange("(p t) c -> p t c", t=PACK))
+
+        def entries(half):
+            return slice(half * HALF, (half + 1) * HALF)
+
+        def offsets(half):
+            return pick[:, half * HALF // GROUP : (half + 1) * HALF // GROUP]
+
+        def move_scale_rows(first, last):
+            nc.sync.dma_start(
+                v_scales[:].rearrange("p g j -> p (g j)")[0:MOVED, first:last].bitcast(I32),
+                ts_picked[:].rearrange("p g j -> p (g j)")[SHIFT : SHIFT + MOVED, first:last].bitcast(I32),
+            )
+
+        nc.vector.tensor_copy(ts_second[:].bitcast(I32), ts_both[:, T : 2 * T].bitcast(I32))
+        nc.vector.tensor_copy(ts_picked[:, 1, entries(0)], ts_second[:].indirect(offsets(0)))
+        nc.vector.tensor_copy(ts_picked[:, 0, :], ts_both[:].indirect(pick[:]))
+        move_scale_rows(0, S + HALF)
+        load_wa(0, 0)
+        nc.vector.tensor_copy(ts_picked[:, 1, entries(1)], ts_second[:].indirect(offsets(1)))
+        move_scale_rows(S + HALF, 2 * S)
+        load_wc(0, AT_WC[0])
+        v_words = {}
+        for half in range(HALVES):
             for g in range(K_PASSES):
-                wa_raw[g, rp] = staged([P, PACK, BANK], F32, "wa_raw%d%d" % (g, rp), AT_WA + (K_PASSES * rp + g) * PIECE)
-                nc.sync.dma_start(
-                    wa_raw[g, rp][:],
-                    wa[g * PASS : (g + 1) * PASS, rp * BANK : (rp + 1) * BANK].rearrange("(p t) c -> p t c", t=PACK),
-                )
+                v_words[g, half] = placed([P, HALF], U32, "v_words%d%d" % (g, half), V_ON.get((g, half)))
+                nc.vector.tensor_copy(v_words[g, half][:], tab[g][:].bitcast(U32).indirect(offsets(half)))
+
+        load_wb(1, AT_WB1)
+        load_wc(1, AT_WC[1])
+        load_wa(1, 0)
+        load_wa(0, 1)
+        load_wa(1, 1)
+        pages = [staged([P, T2], F32, "page0", AT_PAGES)] + [held([P, T2], F32, "page%d" % i) for i in range(1, PACK)]
+        for page in pages[:3]:
+            nc.gpsimd.memset(page[:], 0.0)
+        nc.vector.memset(pages[3][:], 0.0)
 
         def project(bank, chunk, words, scales, fmt):
             cols = slice(chunk * P, (chunk + 1) * P)
             for g in range(K_PASSES):
                 nc.tensor.matmul_mx(
                     out=bank[:],
-                    lhsT=v_words[g][:, cols].bitcast(E4M3),
+                    lhsT=v_words[g, chunk // CHUNKS][:, (chunk % CHUNKS) * P : (chunk % CHUNKS + 1) * P].bitcast(E4M3),
                     lhsT_scale=v_scales[:, g, cols],
                     rhs=words[g].bitcast(fmt),
                     rhs_scale=scales[g],
@@ -144,11 +206,8 @@ def tile_list_segment_reassortment_fitness_kernel(
                 copy(dst[:, first : first + count], src[:, first : first + count])
                 first = first + count
 
-        def quantise(grouped, width, name):
-            words = held([P, width], U32, name + "_w")
-            scales = held([P, width], U8, name + "_s")
-            nc.vector.quantize_mx(out=words[:].bitcast(E4M3), scales=scales[:], in_=grouped[:])
-            return words, scales
+        def quantise(words, scales, grouped):
+            nc.vector.quantize_mx(out=words.bitcast(E4M3), scales=scales, in_=grouped)
 
         def by_pairs(bank):
             return bank[:].rearrange("p (m u e) -> p u m e", u=2, e=2)
@@ -158,22 +217,21 @@ def tile_list_segment_reassortment_fitness_kernel(
 
         bc = {}
         wa_q = {}
-        h_q = {}
         wd_q = {}
+        h_q = {}
         ys = {}
 
         def multiply_b_c(rp, chunk):
             cols = slice(rp * BANK, (rp + 1) * BANK)
             b_bank = psum.tile([P, BANK], F32, name="b_bank", tag="b_then_y")
-            wb_cols = slice(2 * rp * BANK, 2 * (rp + 1) * BANK)
-            project(b_bank, chunk, [wb_w[:, g, wb_cols] for g in range(K_PASSES)],
+            project(b_bank, chunk, [wb_w[rp][:, g, :] for g in range(K_PASSES)],
                     [wb_sc[:, g, cols] for g in range(K_PASSES)], E2M1)
-            c_bank = psum.tile([P, BANK], F32, name="c_bank")
-            project(c_bank, chunk, [wc_w[:, g, cols] for g in range(K_PASSES)],
+            c_bank = psum.tile([P, BANK], F32, name="c_bank", tag="c_then_y")
+            project(c_bank, chunk, [wc_w[rp][:, g, :] for g in range(K_PASSES)],
                     [wc_sc[:, g, cols] for g in range(K_PASSES)], E4M3)
-            b_sb = ring.tile([P, BANK], F32, name="b_sb")
+            b_sb = placed([P, BANK], F32, "b_sb%d%d" % (rp, chunk), B_ON.get((rp, chunk)))
             nc.scalar.copy(as_pairs(b_sb[:]), by_pairs(b_bank))
-            bc[rp, chunk] = held([P, BANK], F32, "bc%d%d" % (rp, chunk))
+            bc[rp, chunk] = placed([P, BANK], F32, "bc%d%d" % (rp, chunk), BC_ON.get((rp, chunk)))
             nc.vector.tensor_tensor(as_pairs(bc[rp, chunk][:]), by_pairs(c_bank), as_pairs(b_sb[:]), MULT)
 
         def prepare_wa(g, rp, shares):
@@ -183,9 +241,11 @@ def tile_list_segment_reassortment_fitness_kernel(
                 wa_raw[g, rp][:].rearrange("p t (c i) -> p c t i", i=4),
                 shares,
             )
-            wa_q[g, rp] = quantise(grouped, BANK, "wa_q%d%d" % (g, rp))
+            wa_q[g, rp] = (held([P, BANK], U32, "wa_w%d%d" % (g, rp)), held([P, BANK], U8, "wa_s%d%d" % (g, rp)))
+            quantise(wa_q[g, rp][0][:], wa_q[g, rp][1][:], grouped[:])
 
-        def make_h(rp, half, h_jr):
+        def make_h(rp, half):
+            h_jr = placed([P, CHUNKS, BANK], BF16, "h%d%d" % (rp, half), H_ON.get((rp, half)))
             for s in range(CHUNKS):
                 chunk = CHUNKS * half + s
                 a_bank = psum.tile([P, BANK], F32, name="a_bank")
@@ -197,14 +257,15 @@ def tile_list_segment_reassortment_fitness_kernel(
             for s in range(CHUNKS):
                 for u in range(2):
                     nc.tensor.transpose(turned[:, s, u, :], words[:, (2 * s + u) * P : (2 * s + u + 1) * P], ident[:])
-            grouped = held([P, HALF * PACK], BF16, "hT%d%d" % (rp, half))
+            grouped = placed([P, HALF * PACK], BF16, "hT%d%d" % (rp, half), HT_ON.get((rp, half)))
             nc.scalar.copy(
                 grouped[:].bitcast(F32).rearrange("p (s j u) -> p s j u", s=CHUNKS, u=2),
                 turned[:].rearrange("p s u j -> p s j u"),
             )
-            h_q[rp, half] = quantise(grouped, HALF, "h_q%d%d" % (rp, half))
+            h_q[rp, half] = (held([P, HALF], U32, "h_w%d%d" % (rp, half)), held([P, HALF], U8, "h_s%d%d" % (rp, half)))
+            quantise(h_q[rp, half][0][:], h_q[rp, half][1][:], grouped[:])
 
-        def prepare_wd(rp, offset, shares):
+        def prepare_wd(rp, offset, shares, parts):
             raw = staged([P, PACK, N], F32, "wd_raw%d" % rp, offset)
             nc.sync.dma_start(raw[:], wd[rp * PASS : (rp + 1) * PASS, :].rearrange("(p t) n -> p t n", t=PACK))
             grouped = held([P, N * PACK], BF16, "wd_g%d" % rp)
@@ -213,10 +274,14 @@ def tile_list_segment_reassortment_fitness_kernel(
                 raw[:].rearrange("p t (m i) -> p m t i", i=PACK),
                 shares,
             )
-            wd_q[rp] = quantise(grouped, N, "wd_q%d" % rp)
+            wd_q[rp] = (held([P, N], U32, "wd_w%d" % rp), held([P, N], U8, "wd_s%d" % rp))
+            width = N // parts
+            for e in range(parts):
+                cols = slice(e * width, (e + 1) * width)
+                quantise(wd_q[rp][0][:, cols], wd_q[rp][1][:, cols], grouped[:, PACK * e * width : PACK * (e + 1) * width])
 
-        def make_y(half, first, tiles):
-            y_bank = psum.tile([P, 2, HALF], F32, name="y_bank", tag="b_then_y")
+        def make_y(half, first):
+            y_bank = psum.tile([P, 2, HALF], F32, name="y_bank", tag=("b_then_y", "c_then_y")[first // 2])
             for i in (first, first + 1):
                 cols = slice(i * P, (i + 1) * P)
                 for rp in range(R_PASSES):
@@ -230,39 +295,33 @@ def tile_list_segment_reassortment_fitness_kernel(
                         stop=(rp == R_PASSES - 1),
                     )
             for i in (first, first + 1):
-                ys[half, i] = tiles[i - first]
+                ys[half, i] = placed([P, HALF], F32, "y%d%d" % (half, i), Y_ON.get((half, i)))
                 nc.scalar.activation(ys[half, i][:], y_bank[:, i - first, :], IDENTITY, bias=bias_cols[:, i : i + 1])
 
-        def h_tile(rp, half):
-            return held([P, CHUNKS, BANK], BF16, "h%d%d" % (rp, half))
-
-        def y_tiles(half, first):
-            return [held([P, HALF], F32, "y%d%d" % (half, i)) for i in (first, first + 1)]
-
         on_vector, on_scalar = nc.vector.tensor_copy, nc.scalar.copy
+        prepare_wa(0, 0, [(on_vector, 128)])
         for half in range(HALVES):
             for rp in range(R_PASSES):
-                for s in range(CHUNKS):
-                    multiply_b_c(rp, CHUNKS * half + s)
-        prepare_wa(0, 0, [(on_vector, STEP), (on_vector, STEP)])
-        prepare_wa(1, 0, [(on_vector, STEP), (on_vector, STEP)])
-        prepare_wa(0, 1, [(on_scalar, STEP), (on_scalar, STEP)])
-        prepare_wa(1, 1, [(on_scalar, P)])
+                for chunk in range(CHUNKS * half, CHUNKS * (half + 1)):
+                    multiply_b_c(rp, chunk)
+        prepare_wa(1, 0, [(on_vector, 64), (on_scalar, 64)])
+        prepare_wa(0, 1, [(on_scalar, 64), (on_scalar, 64)])
+        prepare_wa(1, 1, [(on_scalar, 128)])
         for rp in range(R_PASSES):
-            make_h(rp, 0, h_tile(rp, 0))
-        prepare_wd(0, AT_WD, [(on_scalar, P)])
-        prepare_wd(1, AT_WD + PIECE + BIAS_ROOM, [(on_scalar, WD_LAST_ON_SCALAR), (on_vector, P - WD_LAST_ON_SCALAR)])
-        weights = staged([P, S], F32, "weights", AT_WA)
-        nc.sync.dma_start(weights[:], wgo)
-        bias_cols = staged([P, PACK], F32, "bias_cols", AT_WD + PIECE)
+            make_h(rp, 0)
+        prepare_wd(0, AT_WD[0], [(on_scalar, 128)], 1)
+        prepare_wd(1, AT_WD[1], [(on_scalar, 80), (on_vector, 48)], 1)
+        bias_cols = staged([P, PACK], F32, "bias_cols", AT_BIAS)
         nc.sync.dma_start(bias_cols[:], bias.rearrange("(p i) -> p i", i=PACK))
-
-        make_y(0, 0, y_tiles(0, 0))
-        make_h(0, 1, h_tile(0, 1))
-        make_h(1, 1, staged([P, CHUNKS, BANK], BF16, "h_last", AT_WC))
-        make_y(0, 2, [staged([P, HALF], F32, "y_late%d" % e, AT_WC + 4 * HALF * e) for e in range(2)])
+        weights = staged([P, S], F32, "weights", AT_WGO)
+        nc.sync.dma_start(weights[:], wgo)
+        nc.sync.dma_start(place[:], offs2)
+        make_y(0, 0)
+        make_h(0, 1)
+        make_h(1, 1)
+        make_y(0, 2)
         for first in range(0, PACK, 2):
-            make_y(1, first, y_tiles(1, first))
+            make_y(1, first)
 
         rows = out.rearrange("(p i) t -> p i t", i=PACK)
         for half in range(HALVES):
@@ -270,7 +329,7 @@ def tile_list_segment_reassortment_fitness_kernel(
                 nc.vector.tensor_tensor(
                     pages[i][:].indirect(place[:, half * HALF // GROUP : (half + 1) * HALF // GROUP]),
                     ys[half, i][:],
-                    weights[:, half * HALF : (half + 1) * HALF],
+                    weights[:, entries(half)],
                     MULT,
                 )
                 if half == HALVES - 1:

@@ -38,7 +38,7 @@ PAGE = 4 * T2
 EDGE = 64
 AT_V = 0
 AT_TS = AT_V
-AT_WA00 = 1024
+AT_WA00 = AT_V + 1024
 AT_WC0 = AT_WA00 + PIECE
 AT_TS2 = AT_WC0
 AT_WB1 = 2 * PIECE
@@ -47,15 +47,15 @@ AT_WA10 = AT_WC1 + 4096
 AT_TAB0 = AT_WB1 + 2048 - EDGE
 AT_WA01 = AT_WA10 + PIECE
 AT_PAGES = AT_WA01 + PIECE
-AT_WA11 = AT_PAGES + PAGE
-AT_TAB1 = AT_PAGES - 2048
+AT_TAB1 = AT_PAGES - EDGE
+AT_WA11 = AT_PAGES + 2 * PAGE
 AT_WA = [AT_WA00, AT_WA10, AT_WA01, AT_WA11]
-AT_WD0 = AT_WA11 + PIECE
-AT_BIAS = AT_WD0 + PIECE
-AT_WD = [AT_WD0, AT_BIAS + EDGE]
-AT_WGO = AT_WA00 + 4096
+AT_BIAS = AT_WA11 + PIECE
+AT_WD = [AT_BIAS + EDGE, AT_WA00]
+AT_WGO = AT_WD[0] + PIECE
 AT_WC = [AT_WC0, AT_WC1]
-AT_Y = AT_WD[1] + PIECE
+AT_Y = AT_WGO + 4096
+WA_G_ON = {(0, 0): AT_WGO}
 V_ON = {(0, 0): AT_V}
 B_ON = {}
 BC_ON = {}
@@ -88,7 +88,6 @@ def tile_list_segment_reassortment_fitness_kernel(
         ts_both = staged([P, K_PASSES * T], U8, "ts_both", AT_TS)
         ts_picked = staged([P, K_PASSES, S], U8, "ts_picked", AT_BIAS - 512)
         v_scales = held([P, K_PASSES, S], U8, "v_scales")
-        wc_sc = held([P, K_PASSES, H], U8, "wc_sc")
         tab = {}
 
         def load_table(g, offset):
@@ -105,11 +104,12 @@ def tile_list_segment_reassortment_fitness_kernel(
 
         load_wb(0, None)
 
-        nc.gpsimd.memset(ts_both[:, 0 : T // 2].bitcast(I32), 0)
-        nc.vector.memset(ts_both[:, T // 2 : 2 * T].bitcast(I32), 0)
+        nc.vector.memset(ts_both[:].bitcast(I32), 0)
         ts_second = staged([P, T], U8, "ts_second", AT_TS2)
         wb_sc = held([P, K_PASSES, H], U8, "wb_sc")
         nc.vector.memset(wb_sc[:].bitcast(I32), 0)
+        wc_sc = held([P, K_PASSES, H], U8, "wc_sc")
+        nc.vector.memset(wc_sc[:].bitcast(I32), 0)
         nc.vector.memset(v_scales[:].bitcast(I32), 0)
 
         def load_scale_rows(queue, tile, scales, first):
@@ -120,10 +120,7 @@ def tile_list_segment_reassortment_fitness_kernel(
                 )
 
         load_scale_rows(nc.sync, ts_both[:].rearrange("p (g t) -> p g t", g=K_PASSES), tab_scales, SHIFT)
-        nc.gpsimd.memset(wc_sc[:].bitcast(I32), 0)
-        load_scale_rows(nc.gpsimd, wc_sc[:], wc_scales, 0)
         load_table(0, AT_TAB0)
-        load_table(1, AT_TAB1)
         wc_w = {}
 
         def load_wc(rp, offset):
@@ -132,6 +129,8 @@ def tile_list_segment_reassortment_fitness_kernel(
             nc.sync.dma_start(wc_w[rp][:], cols.rearrange("g p c i -> p g (c i)").bitcast(I32))
 
         load_scale_rows(nc.sync, wb_sc[:], wb_scales, 0)
+        load_table(1, AT_TAB1)
+        load_scale_rows(nc.sync, wc_sc[:], wc_scales, 0)
 
         ones = held([P, P], F32, "ones")
         column = held([P, P], F32, "column")
@@ -182,10 +181,10 @@ def tile_list_segment_reassortment_fitness_kernel(
         load_wa(1, 0)
         load_wa(0, 1)
         load_wa(1, 1)
-        pages = [staged([P, T2], F32, "page0", AT_PAGES)] + [held([P, T2], F32, "page%d" % i) for i in range(1, PACK)]
-        for page in pages[:3]:
-            nc.gpsimd.memset(page[:], 0.0)
-        nc.vector.memset(pages[3][:], 0.0)
+        pages = [staged([P, T2], F32, "page%d" % i, AT_PAGES + i * PAGE) for i in range(2)]
+        pages = pages + [held([P, T2], F32, "page%d" % i) for i in range(2, PACK)]
+        for page in pages:
+            nc.vector.memset(page[:], 0.0)
 
         def project(bank, chunk, words, scales, fmt):
             cols = slice(chunk * P, (chunk + 1) * P)
@@ -235,7 +234,7 @@ def tile_list_segment_reassortment_fitness_kernel(
             nc.vector.tensor_tensor(as_pairs(bc[rp, chunk][:]), by_pairs(c_bank), as_pairs(b_sb[:]), MULT)
 
         def prepare_wa(g, rp, shares):
-            grouped = held([P, BANK * PACK], BF16, "wa_g%d%d" % (g, rp))
+            grouped = placed([P, BANK * PACK], BF16, "wa_g%d%d" % (g, rp), WA_G_ON.get((g, rp)))
             round_in_shares(
                 grouped[:].rearrange("p (c i t) -> p c t i", i=4, t=PACK),
                 wa_raw[g, rp][:].rearrange("p t (c i) -> p c t i", i=4),

@@ -15,8 +15,9 @@ E4M3 = mybir.dt.float8_e4m3fn_x4
 E2M1 = mybir.dt.float4_e2m1fn_x4
 MULT = mybir.AluOpType.mult
 ADD = mybir.AluOpType.add
-EQUAL = mybir.AluOpType.is_equal
 IDENTITY = mybir.ActivationFunctionType.Identity
+ABS = mybir.ActivationFunctionType.Abs
+RELU = mybir.ActivationFunctionType.Relu
 
 P = 128
 PACK = 4
@@ -36,6 +37,7 @@ MOVED = 112
 PIECE = PACK * BANK * 4
 PAGE = 4 * T2
 EDGE = 64
+WC_ROW = 4
 AT_V = 0
 AT_TS = AT_V
 AT_WA00 = AT_V + 1024
@@ -104,12 +106,11 @@ def tile_list_segment_reassortment_fitness_kernel(
 
         load_wb(0, None)
 
-        nc.vector.memset(ts_both[:].bitcast(I32), 0)
+        nc.gpsimd.memset(ts_both[:, 0:T].bitcast(I32), 0)
+        nc.vector.memset(ts_both[:, T : 2 * T].bitcast(I32), 0)
         ts_second = staged([P, T], U8, "ts_second", AT_TS2)
-        wb_sc = held([P, K_PASSES, H], U8, "wb_sc")
-        nc.vector.memset(wb_sc[:].bitcast(I32), 0)
-        wc_sc = held([P, K_PASSES, H], U8, "wc_sc")
-        nc.vector.memset(wc_sc[:].bitcast(I32), 0)
+        w_sc = held([P, K_PASSES, H], U8, "w_sc")
+        nc.vector.memset(w_sc[:].bitcast(I32), 0)
         nc.vector.memset(v_scales[:].bitcast(I32), 0)
 
         def load_scale_rows(queue, tile, scales, first):
@@ -128,20 +129,22 @@ def tile_list_segment_reassortment_fitness_kernel(
             cols = wc_words[:, :, rp * BANK : (rp + 1) * BANK, :]
             nc.sync.dma_start(wc_w[rp][:], cols.rearrange("g p c i -> p g (c i)").bitcast(I32))
 
-        load_scale_rows(nc.sync, wb_sc[:], wb_scales, 0)
+        load_scale_rows(nc.sync, w_sc[:], wb_scales, 0)
         load_table(1, AT_TAB1)
-        load_scale_rows(nc.sync, wc_sc[:], wc_scales, 0)
+        load_scale_rows(nc.sync, w_sc[:], wc_scales, WC_ROW)
 
         ones = held([P, P], F32, "ones")
         column = held([P, P], F32, "column")
         row = held([P, P], F32, "row")
+        apart = held([P, P], F32, "apart")
         ident = held([P, P], F32, "ident")
         nc.vector.memset(ones[:], 1.0)
         nc.vector.tensor_tensor_scan(column[:], ones[:], ones[:], 0.0, MULT, ADD)
         nc.vector.transpose(row[:], column[:])
         for d in range(QUADS):
             part = slice(32 * d, 32 * (d + 1))
-            nc.vector.tensor_scalar(ident[part, :], column[part, :], row[part, 32 * d : 32 * d + 1], None, EQUAL)
+            nc.scalar.activation(apart[part, :], column[part, :], ABS, bias=row[part, 32 * d : 32 * d + 1], scale=-1.0)
+        nc.scalar.activation(ident[:], apart[:], RELU, bias=1.0, scale=-1.0)
 
         wa_raw = {}
 
@@ -224,10 +227,10 @@ def tile_list_segment_reassortment_fitness_kernel(
             cols = slice(rp * BANK, (rp + 1) * BANK)
             b_bank = psum.tile([P, BANK], F32, name="b_bank", tag="b_then_y")
             project(b_bank, chunk, [wb_w[rp][:, g, :] for g in range(K_PASSES)],
-                    [wb_sc[:, g, cols] for g in range(K_PASSES)], E2M1)
+                    [w_sc[:, g, cols] for g in range(K_PASSES)], E2M1)
             c_bank = psum.tile([P, BANK], F32, name="c_bank", tag="c_then_y")
             project(c_bank, chunk, [wc_w[rp][:, g, :] for g in range(K_PASSES)],
-                    [wc_sc[:, g, cols] for g in range(K_PASSES)], E4M3)
+                    [w_sc[WC_ROW:P, g, cols] for g in range(K_PASSES)], E4M3)
             b_sb = placed([P, BANK], F32, "b_sb%d%d" % (rp, chunk), B_ON.get((rp, chunk)))
             nc.scalar.copy(as_pairs(b_sb[:]), by_pairs(b_bank))
             bc[rp, chunk] = placed([P, BANK], F32, "bc%d%d" % (rp, chunk), BC_ON.get((rp, chunk)))

@@ -37,12 +37,13 @@ MOVED = 112
 PIECE = PACK * BANK * 4
 PAGE = 4 * T2
 EDGE = 64
+WARM_UPS = 5
 WC_ROW = 4
 AT_V = 0
 AT_TS = AT_V
-AT_WA00 = AT_V + 1024
-AT_WC0 = AT_WA00 + PIECE
-AT_TS2 = AT_WC0
+AT_WC0 = 1024
+AT_WA00 = AT_WC0 + 4096
+AT_TS2 = AT_WA00
 AT_WB1 = 2 * PIECE
 AT_WC1 = AT_WB1 + 2048
 AT_WA10 = AT_WC1 + 4096
@@ -169,10 +170,21 @@ def tile_list_segment_reassortment_fitness_kernel(
         nc.vector.tensor_copy(ts_picked[:, 1, entries(0)], ts_second[:].indirect(offsets(0)))
         nc.vector.tensor_copy(ts_picked[:, 0, :], ts_both[:].indirect(pick[:]))
         move_scale_rows(0, S + HALF)
-        load_wa(0, 0)
+        load_wc(0, AT_WC[0])
+        unread = psum.tile([P, BANK], F32, name="unread", tag="turned")
+        for n in range(WARM_UPS):
+            nc.tensor.matmul_mx(
+                out=unread[:],
+                lhsT=tab[0][:, 0:P].bitcast(E4M3),
+                lhsT_scale=ts_picked[:, 0, 0:P],
+                rhs=tab[0][:, 0:BANK].bitcast(E4M3),
+                rhs_scale=ts_picked[:, 0, :],
+                start=True,
+                stop=True,
+            )
         nc.vector.tensor_copy(ts_picked[:, 1, entries(1)], ts_second[:].indirect(offsets(1)))
         move_scale_rows(S + HALF, 2 * S)
-        load_wc(0, AT_WC[0])
+        load_wa(0, 0)
         v_words = {}
         for half in range(HALVES):
             for g in range(K_PASSES):
@@ -255,7 +267,7 @@ def tile_list_segment_reassortment_fitness_kernel(
                         [wa_q[g, rp][1][:] for g in range(K_PASSES)], E4M3)
                 nc.vector.tensor_tensor(as_pairs(h_jr[:, s, :]), by_pairs(a_bank), as_pairs(bc[rp, chunk][:]), MULT)
             words = h_jr[:].rearrange("p s r -> p (s r)").bitcast(F32)
-            turned = psum.tile([P, CHUNKS, 2, P], F32, name="turned")
+            turned = psum.tile([P, CHUNKS, 2, P], F32, name="turned", tag="turned")
             for s in range(CHUNKS):
                 for u in range(2):
                     nc.tensor.transpose(turned[:, s, u, :], words[:, (2 * s + u) * P : (2 * s + u + 1) * P], ident[:])
@@ -301,11 +313,11 @@ def tile_list_segment_reassortment_fitness_kernel(
                 nc.scalar.activation(ys[half, i][:], y_bank[:, i - first, :], IDENTITY, bias=bias_cols[:, i : i + 1])
 
         on_vector, on_scalar = nc.vector.tensor_copy, nc.scalar.copy
-        prepare_wa(0, 0, [(on_vector, 128)])
         for half in range(HALVES):
             for rp in range(R_PASSES):
                 for chunk in range(CHUNKS * half, CHUNKS * (half + 1)):
                     multiply_b_c(rp, chunk)
+        prepare_wa(0, 0, [(on_vector, 64), (on_vector, 64)])
         prepare_wa(1, 0, [(on_vector, 64), (on_scalar, 64)])
         prepare_wa(0, 1, [(on_scalar, 64), (on_scalar, 64)])
         prepare_wa(1, 1, [(on_scalar, 128)])

@@ -58,12 +58,14 @@ AT_WD = [AT_BIAS + EDGE, AT_WA00]
 AT_WGO = AT_WD[0] + PIECE
 AT_WC = [AT_WC0, AT_WC1]
 AT_Y = AT_WGO + 4096
-WA_G_ON = {(0, 0): AT_WGO}
+AT_G11 = AT_Y + 2048
+AT_WD_G = [AT_G11 + 4096, AT_G11 + 2 * 4096]
+WA_G_ON = {(0, 0): AT_WGO, (1, 1): AT_G11}
 V_ON = {(0, 0): AT_V}
 B_ON = {}
-BC_ON = {}
+BC_ON = {(0, 0): AT_G11, (1, 2): AT_WD_G[1]}
 HT_ON = {}
-H_ON = {(1, 1): AT_Y}
+H_ON = {(0, 1): AT_WD_G[0], (1, 1): AT_Y}
 Y_ON = {(0, 2): AT_Y, (0, 3): AT_Y + 1024}
 
 
@@ -232,7 +234,7 @@ def tile_list_segment_reassortment_fitness_kernel(
         bc = {}
         wa_q = {}
         wd_q = {}
-        h_q = {}
+        h_q, h_jr, h_rj, wa_g, wd_g, wd_raw = {}, {}, {}, {}, {}, {}
         ys = {}
 
         def multiply_b_c(rp, chunk):
@@ -248,51 +250,59 @@ def tile_list_segment_reassortment_fitness_kernel(
             bc[rp, chunk] = placed([P, BANK], F32, "bc%d%d" % (rp, chunk), BC_ON.get((rp, chunk)))
             nc.vector.tensor_tensor(as_pairs(bc[rp, chunk][:]), by_pairs(c_bank), as_pairs(b_sb[:]), MULT)
 
-        def prepare_wa(g, rp, shares):
-            grouped = placed([P, BANK * PACK], BF16, "wa_g%d%d" % (g, rp), WA_G_ON.get((g, rp)))
+        def round_wa(g, rp, shares):
+            wa_g[g, rp] = placed([P, BANK * PACK], BF16, "wa_g%d%d" % (g, rp), WA_G_ON.get((g, rp)))
             round_in_shares(
-                grouped[:].rearrange("p (c i t) -> p c t i", i=4, t=PACK),
+                wa_g[g, rp][:].rearrange("p (c i t) -> p c t i", i=4, t=PACK),
                 wa_raw[g, rp][:].rearrange("p t (c i) -> p c t i", i=4),
                 shares,
             )
-            wa_q[g, rp] = (held([P, BANK], U32, "wa_w%d%d" % (g, rp)), held([P, BANK], U8, "wa_s%d%d" % (g, rp)))
-            quantise(wa_q[g, rp][0][:], wa_q[g, rp][1][:], grouped[:])
 
-        def make_h(rp, half):
-            h_jr = placed([P, CHUNKS, BANK], BF16, "h%d%d" % (rp, half), H_ON.get((rp, half)))
-            for s in range(CHUNKS):
-                chunk = CHUNKS * half + s
-                a_bank = psum.tile([P, BANK], F32, name="a_bank")
-                project(a_bank, chunk, [wa_q[g, rp][0][:] for g in range(K_PASSES)],
-                        [wa_q[g, rp][1][:] for g in range(K_PASSES)], E4M3)
-                nc.vector.tensor_tensor(as_pairs(h_jr[:, s, :]), by_pairs(a_bank), as_pairs(bc[rp, chunk][:]), MULT)
-            words = h_jr[:].rearrange("p s r -> p (s r)").bitcast(F32)
+        def quantise_wa(g, rp):
+            wa_q[g, rp] = (held([P, BANK], U32, "wa_w%d%d" % (g, rp)), held([P, BANK], U8, "wa_s%d%d" % (g, rp)))
+            quantise(wa_q[g, rp][0][:], wa_q[g, rp][1][:], wa_g[g, rp][:])
+
+        def make_h(rp, chunk):
+            half, s = divmod(chunk, CHUNKS)
+            if s == 0:
+                h_jr[rp, half] = placed([P, CHUNKS, BANK], BF16, "h%d%d" % (rp, half), H_ON.get((rp, half)))
+            a_bank = psum.tile([P, BANK], F32, name="a_bank")
+            project(a_bank, chunk, [wa_q[g, rp][0][:] for g in range(K_PASSES)],
+                    [wa_q[g, rp][1][:] for g in range(K_PASSES)], E4M3)
+            nc.vector.tensor_tensor(as_pairs(h_jr[rp, half][:, s, :]), by_pairs(a_bank), as_pairs(bc[rp, chunk][:]), MULT)
+
+        def turn_h(rp, half):
+            words = h_jr[rp, half][:].rearrange("p s r -> p (s r)").bitcast(F32)
             turned = psum.tile([P, CHUNKS, 2, P], F32, name="turned", tag="turned")
             for s in range(CHUNKS):
                 for u in range(2):
                     nc.tensor.transpose(turned[:, s, u, :], words[:, (2 * s + u) * P : (2 * s + u + 1) * P], ident[:])
-            grouped = placed([P, HALF * PACK], BF16, "hT%d%d" % (rp, half), HT_ON.get((rp, half)))
+            h_rj[rp, half] = placed([P, HALF * PACK], BF16, "hT%d%d" % (rp, half), HT_ON.get((rp, half)))
             nc.scalar.copy(
-                grouped[:].bitcast(F32).rearrange("p (s j u) -> p s j u", s=CHUNKS, u=2),
+                h_rj[rp, half][:].bitcast(F32).rearrange("p (s j u) -> p s j u", s=CHUNKS, u=2),
                 turned[:].rearrange("p s u j -> p s j u"),
             )
-            h_q[rp, half] = (held([P, HALF], U32, "h_w%d%d" % (rp, half)), held([P, HALF], U8, "h_s%d%d" % (rp, half)))
-            quantise(h_q[rp, half][0][:], h_q[rp, half][1][:], grouped[:])
 
-        def prepare_wd(rp, offset, shares, parts):
-            raw = staged([P, PACK, N], F32, "wd_raw%d" % rp, offset)
-            nc.sync.dma_start(raw[:], wd[rp * PASS : (rp + 1) * PASS, :].rearrange("(p t) n -> p t n", t=PACK))
-            grouped = held([P, N * PACK], BF16, "wd_g%d" % rp)
+        def quantise_h(rp, half):
+            h_q[rp, half] = (held([P, HALF], U32, "h_w%d%d" % (rp, half)), held([P, HALF], U8, "h_s%d%d" % (rp, half)))
+            quantise(h_q[rp, half][0][:], h_q[rp, half][1][:], h_rj[rp, half][:])
+
+        def load_wd(rp):
+            wd_raw[rp] = staged([P, PACK, N], F32, "wd_raw%d" % rp, AT_WD[rp])
+            nc.sync.dma_start(wd_raw[rp][:], wd[rp * PASS : (rp + 1) * PASS, :].rearrange("(p t) n -> p t n", t=PACK))
+
+        def round_wd(rp, shares):
+            wd_g[rp] = staged([P, N * PACK], BF16, "wd_g%d" % rp, AT_WD_G[rp])
             round_in_shares(
-                grouped[:].rearrange("p (i m t) -> p m t i", i=PACK, t=PACK),
-                raw[:].rearrange("p t (m i) -> p m t i", i=PACK),
+                wd_g[rp][:].rearrange("p (i m t) -> p m t i", i=PACK, t=PACK),
+                wd_raw[rp][:].rearrange("p t (m i) -> p m t i", i=PACK),
                 shares,
             )
-            wd_q[rp] = (held([P, N], U32, "wd_w%d" % rp), held([P, N], U8, "wd_s%d" % rp))
-            width = N // parts
-            for e in range(parts):
-                cols = slice(e * width, (e + 1) * width)
-                quantise(wd_q[rp][0][:, cols], wd_q[rp][1][:, cols], grouped[:, PACK * e * width : PACK * (e + 1) * width])
+
+        def quantise_wd(rp, first=0, last=N):
+            if first == 0:
+                wd_q[rp] = (held([P, N], U32, "wd_w%d" % rp), held([P, N], U8, "wd_s%d" % rp))
+            quantise(wd_q[rp][0][:, first:last], wd_q[rp][1][:, first:last], wd_g[rp][:, PACK * first : PACK * last])
 
         def make_y(half, first):
             y_bank = psum.tile([P, 2, HALF], F32, name="y_bank", tag=("b_then_y", "c_then_y")[first // 2])
@@ -317,22 +327,43 @@ def tile_list_segment_reassortment_fitness_kernel(
             for rp in range(R_PASSES):
                 for chunk in range(CHUNKS * half, CHUNKS * (half + 1)):
                     multiply_b_c(rp, chunk)
-        prepare_wa(0, 0, [(on_vector, 64), (on_vector, 64)])
-        prepare_wa(1, 0, [(on_vector, 64), (on_scalar, 64)])
-        prepare_wa(0, 1, [(on_scalar, 64), (on_scalar, 64)])
-        prepare_wa(1, 1, [(on_scalar, 128)])
+        round_wa(0, 0, [(on_vector, 64), (on_vector, 64)])
+        quantise_wa(0, 0)
+        round_wa(1, 0, [(on_vector, 64), (on_scalar, 64)])
+        quantise_wa(1, 0)
+        round_wa(0, 1, [(on_scalar, 64), (on_scalar, 64)])
         for rp in range(R_PASSES):
-            make_h(rp, 0)
-        prepare_wd(0, AT_WD[0], [(on_scalar, 128)], 1)
-        prepare_wd(1, AT_WD[1], [(on_scalar, 80), (on_vector, 48)], 1)
+            load_wd(rp)
         bias_cols = staged([P, PACK], F32, "bias_cols", AT_BIAS)
         nc.sync.dma_start(bias_cols[:], bias.rearrange("(p i) -> p i", i=PACK))
         weights = staged([P, S], F32, "weights", AT_WGO)
         nc.sync.dma_start(weights[:], wgo)
         nc.sync.dma_start(place[:], offs2)
-        make_y(0, 0)
+        make_h(0, 0)
         make_h(0, 1)
+        quantise_wa(0, 1)
+        round_wa(1, 1, [(on_vector, 64), (on_scalar, 64)])
+        turn_h(0, 0)
+        make_h(0, 2)
+        quantise_wa(1, 1)
+        make_h(0, 3)
+        quantise_h(0, 0)
+        turn_h(0, 1)
+        round_wd(0, [(on_scalar, 128)])
+        make_h(1, 0)
         make_h(1, 1)
+        quantise_h(0, 1)
+        turn_h(1, 0)
+        make_h(1, 2)
+        round_wd(1, [(on_vector, 128)])
+        quantise_wd(0)
+        quantise_h(1, 0)
+        quantise_wd(1, 0, N // 2)
+        make_h(1, 3)
+        quantise_wd(1, N // 2, N)
+        make_y(0, 0)
+        turn_h(1, 1)
+        quantise_h(1, 1)
         make_y(0, 2)
         for first in range(0, PACK, 2):
             make_y(1, first)

@@ -23,50 +23,53 @@ P = 128
 PACK = 4
 PASS = P * PACK
 BANK = 512
-QUADS = 4
+QUAD = 32
+QUADS = P // QUAD
+ROWS = 4
+BLOCK = 8
 GROUP = 16
 K_PASSES = K // PASS
 R_PASSES = H // PASS
 HALVES = 2
 HALF = S // HALVES
 CHUNKS = HALF // P
-
-SHIFT = GROUP - 2
-MOVED = 112
-
-PIECE = PACK * BANK * 4
-PAGE = 4 * T2
-EDGE = 64
 WARM_UPS = 5
 WC_ROW = 4
-AT_V = 0
-AT_TS = AT_V
-AT_WC0 = 1024
-AT_WA00 = AT_WC0 + 4096
-AT_TS2 = AT_WA00
-AT_WB1 = 2 * PIECE
-AT_WC1 = AT_WB1 + 2048
-AT_WA10 = AT_WC1 + 4096
-AT_TAB0 = AT_WB1 + 2048 - EDGE
-AT_WA01 = AT_WA10 + PIECE
-AT_PAGES = AT_WA01 + PIECE
-AT_TAB1 = AT_PAGES - EDGE
-AT_WA11 = AT_PAGES + 2 * PAGE
-AT_WA = [AT_WA00, AT_WA10, AT_WA01, AT_WA11]
-AT_BIAS = AT_WA11 + PIECE
-AT_WD = [AT_BIAS + EDGE, AT_WA00]
-AT_WGO = AT_WD[0] + PIECE
+
+EDGE = 64
+PIECE = 4 * PACK * BANK
+PAGE = 4 * T2
+TABLE = 4 * T
+ROUNDED = 2 * PACK * BANK
+AT_WC0 = 0
+AT_TS = AT_WC0 + 4096 - EDGE
+AT_WA00 = AT_TS + T - EDGE
+AT_WC1 = AT_WA00 + PIECE
+AT_TAB0 = AT_WC1 + 4096 - EDGE
+AT_WA10 = AT_TAB0 + TABLE - EDGE
+AT_TAB1 = AT_WA10 + PIECE
+AT_PAGE2 = AT_TAB1
+AT_PAGE3 = AT_TAB1 + PAGE
+AT_WA01 = AT_TAB1 + TABLE
+AT_PICKED = AT_WA01 + PIECE - EDGE
+AT_WA11 = AT_PICKED + 1024 - EDGE
+AT_WD0 = AT_WA11 + PIECE
+AT_B00 = AT_WD0 + PIECE - EDGE
+AT_WD1 = AT_B00 + 2048 - EDGE
+AT_BIAS = AT_WD1 + PIECE
+AT_WGO = AT_BIAS + EDGE
+AT_G = AT_WGO + 2048
+AT_TAB = [AT_TAB0, AT_TAB1]
 AT_WC = [AT_WC0, AT_WC1]
-AT_Y = AT_WGO + 4096
-AT_G11 = AT_Y + 2048
-AT_WD_G = [AT_G11 + 4096, AT_G11 + 2 * 4096]
-WA_G_ON = {(0, 0): AT_WGO, (1, 1): AT_G11}
-V_ON = {(0, 0): AT_V}
-B_ON = {}
-BC_ON = {(0, 0): AT_G11, (1, 2): AT_WD_G[1]}
-HT_ON = {}
-H_ON = {(0, 1): AT_WD_G[0], (1, 1): AT_Y}
-Y_ON = {(0, 2): AT_Y, (0, 3): AT_Y + 1024}
+AT_WA = {(0, 0): AT_WA00, (1, 0): AT_WA10, (0, 1): AT_WA01, (1, 1): AT_WA11}
+AT_WD = [AT_WD0, AT_WD1]
+AT_PAGE = [None, None, AT_PAGE2, AT_PAGE3]
+AT_WA_G = {(0, 0): AT_G, (1, 0): AT_G + ROUNDED, (0, 1): AT_WA10 + EDGE, (1, 1): AT_G + 3 * ROUNDED}
+AT_WA_W = {(0, 1): AT_G + 2 * ROUNDED}
+AT_WD_G = [AT_G + 4 * ROUNDED, AT_G + 5 * ROUNDED]
+B_ON = {(0, 0): AT_B00, (0, 2): AT_BIAS, (0, 3): AT_WA_G[1, 0]}
+BC_ON = {(0, 1): AT_WA_W[0, 1], (0, 2): AT_WA_G[1, 1], (1, 1): AT_WD_G[1]}
+H_ON = {(0, 1): AT_WD_G[0]}
 
 
 def tile_list_segment_reassortment_fitness_kernel(
@@ -77,7 +80,8 @@ def tile_list_segment_reassortment_fitness_kernel(
     with ExitStack() as ctx:
         keep = ctx.enter_context(tc.tile_pool(name="keep", bufs=1))
         stage = ctx.enter_context(tc.tile_pool(name="stage", bufs=1))
-        psum = ctx.enter_context(tc.psum_pool(name="psum", bufs=2))
+        psum = ctx.enter_context(tc.psum_pool(name="psum", bufs=6))
+        psum_turn = ctx.enter_context(tc.psum_pool(name="psum_turn", bufs=2))
 
         def held(shape, dtype, name):
             return keep.tile(shape, dtype, name=name, align_bytes=64)
@@ -90,51 +94,30 @@ def tile_list_segment_reassortment_fitness_kernel(
 
         pick = held([P, S // GROUP], U16, "pick")
         place = held([P, S // GROUP], U16, "place")
-        ts_both = staged([P, K_PASSES * T], U8, "ts_both", AT_TS)
-        ts_picked = staged([P, K_PASSES, S], U8, "ts_picked", AT_BIAS - 512)
+        nc.sync.dma_start(pick[:], offs)
+        wb_sc = held([P, K_PASSES, H], U8, "wb_sc")
+        wc_sc = held([P, K_PASSES, H], U8, "wc_sc")
         v_scales = held([P, K_PASSES, S], U8, "v_scales")
+
+        def load_scale_rows(plane, scales, first):
+            by_row = scales.rearrange("g (d x) c -> x d g c", x=ROWS)
+            for x in range(ROWS):
+                nc.sync.dma_start(plane[:].bitcast(I32)[first + x : P : QUAD], by_row[x].bitcast(I32))
+
+        load_scale_rows(wb_sc, wb_scales, 0)
+        ts = [held([P, T], U8, "ts0"), staged([P, T], U8, "ts1", AT_TS)]
+        for g, engine in enumerate((nc.gpsimd, nc.vector)):
+            engine.memset(ts[g][:].bitcast(I32), 0)
+            nc.sync.dma_start(ts[g][:].bitcast(I32)[0:P:BLOCK], tab_scales[g].bitcast(I32))
         tab = {}
 
-        def load_table(g, offset):
-            tab[g] = staged([P, T], I32, "tab%d" % g, offset)
+        def load_table(g):
+            tab[g] = staged([P, T], I32, "tab%d" % g, AT_TAB[g])
             nc.sync.dma_start(tab[g][:], tab_words[g].rearrange("p t i -> p (t i)").bitcast(I32))
 
-        nc.sync.dma_start(pick[:], offs)
-        wb_w = {}
-
-        def load_wb(rp, offset):
-            wb_w[rp] = placed([P, K_PASSES, 2 * BANK], U8, "wb_w%d" % rp, offset)
-            cols = wb_words[:, :, 2 * rp * BANK : 2 * (rp + 1) * BANK]
-            nc.sync.dma_start(wb_w[rp][:].bitcast(I32), cols.rearrange("g p c -> p g c").bitcast(I32))
-
-        load_wb(0, None)
-
-        nc.gpsimd.memset(ts_both[:, 0:T].bitcast(I32), 0)
-        nc.vector.memset(ts_both[:, T : 2 * T].bitcast(I32), 0)
-        ts_second = staged([P, T], U8, "ts_second", AT_TS2)
-        w_sc = held([P, K_PASSES, H], U8, "w_sc")
-        nc.vector.memset(w_sc[:].bitcast(I32), 0)
-        nc.vector.memset(v_scales[:].bitcast(I32), 0)
-
-        def load_scale_rows(queue, tile, scales, first):
-            for d in range(QUADS):
-                queue.dma_start(
-                    tile.bitcast(I32)[32 * d + first : 32 * d + first + 4],
-                    scales[:, 4 * d : 4 * d + 4, :].rearrange("g x c -> x g c").bitcast(I32),
-                )
-
-        load_scale_rows(nc.sync, ts_both[:].rearrange("p (g t) -> p g t", g=K_PASSES), tab_scales, SHIFT)
-        load_table(0, AT_TAB0)
-        wc_w = {}
-
-        def load_wc(rp, offset):
-            wc_w[rp] = staged([P, K_PASSES, BANK], I32, "wc_w%d" % rp, offset)
-            cols = wc_words[:, :, rp * BANK : (rp + 1) * BANK, :]
-            nc.sync.dma_start(wc_w[rp][:], cols.rearrange("g p c i -> p g (c i)").bitcast(I32))
-
-        load_scale_rows(nc.sync, w_sc[:], wb_scales, 0)
-        load_table(1, AT_TAB1)
-        load_scale_rows(nc.sync, w_sc[:], wc_scales, WC_ROW)
+        load_table(0)
+        load_scale_rows(wc_sc, wc_scales, WC_ROW)
+        load_table(1)
 
         ones = held([P, P], F32, "ones")
         column = held([P, P], F32, "column")
@@ -145,71 +128,75 @@ def tile_list_segment_reassortment_fitness_kernel(
         nc.vector.tensor_tensor_scan(column[:], ones[:], ones[:], 0.0, MULT, ADD)
         nc.vector.transpose(row[:], column[:])
         for d in range(QUADS):
-            part = slice(32 * d, 32 * (d + 1))
-            nc.scalar.activation(apart[part, :], column[part, :], ABS, bias=row[part, 32 * d : 32 * d + 1], scale=-1.0)
+            part = slice(QUAD * d, QUAD * (d + 1))
+            nc.scalar.activation(apart[part, :], column[part, :], ABS, bias=row[part, QUAD * d : QUAD * d + 1], scale=-1.0)
         nc.scalar.activation(ident[:], apart[:], RELU, bias=1.0, scale=-1.0)
 
-        wa_raw = {}
+        wb_w = held([P, K_PASSES, 2 * H], U8, "wb_w")
+        nc.sync.dma_start(wb_w[:].bitcast(I32), wb_words.rearrange("g p c -> p g c").bitcast(I32))
+        nc.sync.dma_start(place[:], offs2)
+        wc_w, wa_raw, wd_raw = {}, {}, {}
+
+        def load_wc(rp):
+            wc_w[rp] = staged([P, K_PASSES, BANK], I32, "wc_w%d" % rp, AT_WC[rp])
+            cols = wc_words[:, :, rp * BANK : (rp + 1) * BANK, :]
+            nc.sync.dma_start(wc_w[rp][:], cols.rearrange("g p c i -> p g (c i)").bitcast(I32))
 
         def load_wa(g, rp):
-            wa_raw[g, rp] = staged([P, PACK, BANK], F32, "wa_raw%d%d" % (g, rp), AT_WA[K_PASSES * rp + g])
+            wa_raw[g, rp] = staged([P, PACK, BANK], F32, "wa_raw%d%d" % (g, rp), AT_WA[g, rp])
             rows = wa[g * PASS : (g + 1) * PASS, rp * BANK : (rp + 1) * BANK]
             nc.sync.dma_start(wa_raw[g, rp][:], rows.rearrange("(p t) c -> p t c", t=PACK))
+
+        def load_wd(rp):
+            wd_raw[rp] = staged([P, PACK, N], F32, "wd_raw%d" % rp, AT_WD[rp])
+            nc.sync.dma_start(wd_raw[rp][:], wd[rp * PASS : (rp + 1) * PASS, :].rearrange("(p t) n -> p t n", t=PACK))
 
         def entries(half):
             return slice(half * HALF, (half + 1) * HALF)
 
-        def offsets(half):
-            return pick[:, half * HALF // GROUP : (half + 1) * HALF // GROUP]
+        def offsets(lists, half):
+            return lists[:, half * HALF // GROUP : (half + 1) * HALF // GROUP]
 
-        def move_scale_rows(first, last):
+        ts_picked = staged([P, K_PASSES, S], U8, "ts_picked", AT_PICKED)
+        for g in range(K_PASSES):
+            nc.vector.tensor_copy(ts_picked[:, g, :], ts[g][:].indirect(pick[:]))
+        for x in range(ROWS):
             nc.sync.dma_start(
-                v_scales[:].rearrange("p g j -> p (g j)")[0:MOVED, first:last].bitcast(I32),
-                ts_picked[:].rearrange("p g j -> p (g j)")[SHIFT : SHIFT + MOVED, first:last].bitcast(I32),
+                v_scales[:].rearrange("p g j -> p (g j)").bitcast(I32)[x:P:QUAD],
+                ts_picked[:].rearrange("p g j -> p (g j)").bitcast(I32)[BLOCK * x : P : QUAD],
             )
-
-        nc.vector.tensor_copy(ts_second[:].bitcast(I32), ts_both[:, T : 2 * T].bitcast(I32))
-        nc.vector.tensor_copy(ts_picked[:, 1, entries(0)], ts_second[:].indirect(offsets(0)))
-        nc.vector.tensor_copy(ts_picked[:, 0, :], ts_both[:].indirect(pick[:]))
-        move_scale_rows(0, S + HALF)
-        load_wc(0, AT_WC[0])
-        unread = psum.tile([P, BANK], F32, name="unread", tag="turned")
+        load_wa(0, 0)
+        load_wc(0)
+        unread = psum_turn.tile([P, BANK], F32, name="unread", tag="turned")
         for n in range(WARM_UPS):
             nc.tensor.matmul_mx(
                 out=unread[:],
                 lhsT=tab[0][:, 0:P].bitcast(E4M3),
-                lhsT_scale=ts_picked[:, 0, 0:P],
+                lhsT_scale=ts_picked[:, 1, 0:P],
                 rhs=tab[0][:, 0:BANK].bitcast(E4M3),
-                rhs_scale=ts_picked[:, 0, :],
+                rhs_scale=ts_picked[:, 1, :],
                 start=True,
                 stop=True,
             )
-        nc.vector.tensor_copy(ts_picked[:, 1, entries(1)], ts_second[:].indirect(offsets(1)))
-        move_scale_rows(S + HALF, 2 * S)
-        load_wa(0, 0)
-        v_words = {}
+        v_words = held([P, S], U32, "v_words0")
+        nc.vector.tensor_copy(v_words[:], tab[0][:].bitcast(U32).indirect(pick[:]))
+        v_chunk = {(0, c): v_words[:, c * P : (c + 1) * P] for c in range(HALVES * CHUNKS)}
         for half in range(HALVES):
-            for g in range(K_PASSES):
-                v_words[g, half] = placed([P, HALF], U32, "v_words%d%d" % (g, half), V_ON.get((g, half)))
-                nc.vector.tensor_copy(v_words[g, half][:], tab[g][:].bitcast(U32).indirect(offsets(half)))
-
-        load_wb(1, AT_WB1)
-        load_wc(1, AT_WC[1])
+            v_half = held([P, HALF], U32, "v_words1%d" % half)
+            nc.vector.tensor_copy(v_half[:], tab[1][:].bitcast(U32).indirect(offsets(pick, half)))
+            for s in range(CHUNKS):
+                v_chunk[1, CHUNKS * half + s] = v_half[:, s * P : (s + 1) * P]
+        load_wc(1)
         load_wa(1, 0)
         load_wa(0, 1)
         load_wa(1, 1)
-        pages = [staged([P, T2], F32, "page%d" % i, AT_PAGES + i * PAGE) for i in range(2)]
-        pages = pages + [held([P, T2], F32, "page%d" % i) for i in range(2, PACK)]
-        for page in pages:
-            nc.vector.memset(page[:], 0.0)
 
         def project(bank, chunk, words, scales, fmt):
-            cols = slice(chunk * P, (chunk + 1) * P)
             for g in range(K_PASSES):
                 nc.tensor.matmul_mx(
                     out=bank[:],
-                    lhsT=v_words[g, chunk // CHUNKS][:, (chunk % CHUNKS) * P : (chunk % CHUNKS + 1) * P].bitcast(E4M3),
-                    lhsT_scale=v_scales[:, g, cols],
+                    lhsT=v_chunk[g, chunk].bitcast(E4M3),
+                    lhsT_scale=v_scales[:, g, chunk * P : (chunk + 1) * P],
                     rhs=words[g].bitcast(fmt),
                     rhs_scale=scales[g],
                     start=(g == 0),
@@ -231,27 +218,26 @@ def tile_list_segment_reassortment_fitness_kernel(
         def as_pairs(view):
             return view.rearrange("p (u m e) -> p u m e", u=2, e=2)
 
-        bc = {}
-        wa_q = {}
-        wd_q = {}
-        h_q, h_jr, h_rj, wa_g, wd_g, wd_raw = {}, {}, {}, {}, {}, {}
-        ys = {}
+        b_sb, bc, wa_q, wd_q, h_q, h_jr, h_rj, wa_g, wd_g, ys = {}, {}, {}, {}, {}, {}, {}, {}, {}, {}
 
-        def multiply_b_c(rp, chunk):
+        def make_b(rp, chunk):
             cols = slice(rp * BANK, (rp + 1) * BANK)
-            b_bank = psum.tile([P, BANK], F32, name="b_bank", tag="b_then_y")
-            project(b_bank, chunk, [wb_w[rp][:, g, :] for g in range(K_PASSES)],
-                    [w_sc[:, g, cols] for g in range(K_PASSES)], E2M1)
-            c_bank = psum.tile([P, BANK], F32, name="c_bank", tag="c_then_y")
+            b_bank = psum.tile([P, BANK], F32, name="b_bank", tag="sums")
+            project(b_bank, chunk, [wb_w[:, g, 2 * rp * BANK : 2 * (rp + 1) * BANK] for g in range(K_PASSES)],
+                    [wb_sc[:, g, cols] for g in range(K_PASSES)], E2M1)
+            b_sb[rp, chunk] = placed([P, BANK], F32, "b_sb%d%d" % (rp, chunk), B_ON.get((rp, chunk)))
+            nc.scalar.copy(as_pairs(b_sb[rp, chunk][:]), by_pairs(b_bank))
+
+        def multiply_by_c(rp, chunk):
+            cols = slice(rp * BANK, (rp + 1) * BANK)
+            c_bank = psum.tile([P, BANK], F32, name="c_bank", tag="sums")
             project(c_bank, chunk, [wc_w[rp][:, g, :] for g in range(K_PASSES)],
-                    [w_sc[WC_ROW:P, g, cols] for g in range(K_PASSES)], E4M3)
-            b_sb = placed([P, BANK], F32, "b_sb%d%d" % (rp, chunk), B_ON.get((rp, chunk)))
-            nc.scalar.copy(as_pairs(b_sb[:]), by_pairs(b_bank))
+                    [wc_sc[WC_ROW:P, g, cols] for g in range(K_PASSES)], E4M3)
             bc[rp, chunk] = placed([P, BANK], F32, "bc%d%d" % (rp, chunk), BC_ON.get((rp, chunk)))
-            nc.vector.tensor_tensor(as_pairs(bc[rp, chunk][:]), by_pairs(c_bank), as_pairs(b_sb[:]), MULT)
+            nc.vector.tensor_tensor(as_pairs(bc[rp, chunk][:]), by_pairs(c_bank), as_pairs(b_sb[rp, chunk][:]), MULT)
 
         def round_wa(g, rp, shares):
-            wa_g[g, rp] = placed([P, BANK * PACK], BF16, "wa_g%d%d" % (g, rp), WA_G_ON.get((g, rp)))
+            wa_g[g, rp] = staged([P, BANK * PACK], BF16, "wa_g%d%d" % (g, rp), AT_WA_G[g, rp])
             round_in_shares(
                 wa_g[g, rp][:].rearrange("p (c i t) -> p c t i", i=4, t=PACK),
                 wa_raw[g, rp][:].rearrange("p t (c i) -> p c t i", i=4),
@@ -259,25 +245,25 @@ def tile_list_segment_reassortment_fitness_kernel(
             )
 
         def quantise_wa(g, rp):
-            wa_q[g, rp] = (held([P, BANK], U32, "wa_w%d%d" % (g, rp)), held([P, BANK], U8, "wa_s%d%d" % (g, rp)))
+            wa_q[g, rp] = (placed([P, BANK], U32, "wa_w%d%d" % (g, rp), AT_WA_W.get((g, rp))), held([P, BANK], U8, "wa_s%d%d" % (g, rp)))
             quantise(wa_q[g, rp][0][:], wa_q[g, rp][1][:], wa_g[g, rp][:])
 
         def make_h(rp, chunk):
             half, s = divmod(chunk, CHUNKS)
             if s == 0:
                 h_jr[rp, half] = placed([P, CHUNKS, BANK], BF16, "h%d%d" % (rp, half), H_ON.get((rp, half)))
-            a_bank = psum.tile([P, BANK], F32, name="a_bank")
+            a_bank = psum.tile([P, BANK], F32, name="a_bank", tag="sums")
             project(a_bank, chunk, [wa_q[g, rp][0][:] for g in range(K_PASSES)],
                     [wa_q[g, rp][1][:] for g in range(K_PASSES)], E4M3)
             nc.vector.tensor_tensor(as_pairs(h_jr[rp, half][:, s, :]), by_pairs(a_bank), as_pairs(bc[rp, chunk][:]), MULT)
 
         def turn_h(rp, half):
             words = h_jr[rp, half][:].rearrange("p s r -> p (s r)").bitcast(F32)
-            turned = psum.tile([P, CHUNKS, 2, P], F32, name="turned", tag="turned")
+            turned = psum_turn.tile([P, CHUNKS, 2, P], F32, name="turned", tag="turned")
             for s in range(CHUNKS):
                 for u in range(2):
                     nc.tensor.transpose(turned[:, s, u, :], words[:, (2 * s + u) * P : (2 * s + u + 1) * P], ident[:])
-            h_rj[rp, half] = placed([P, HALF * PACK], BF16, "hT%d%d" % (rp, half), HT_ON.get((rp, half)))
+            h_rj[rp, half] = held([P, HALF * PACK], BF16, "hT%d%d" % (rp, half))
             nc.scalar.copy(
                 h_rj[rp, half][:].bitcast(F32).rearrange("p (s j u) -> p s j u", s=CHUNKS, u=2),
                 turned[:].rearrange("p s u j -> p s j u"),
@@ -287,10 +273,6 @@ def tile_list_segment_reassortment_fitness_kernel(
             h_q[rp, half] = (held([P, HALF], U32, "h_w%d%d" % (rp, half)), held([P, HALF], U8, "h_s%d%d" % (rp, half)))
             quantise(h_q[rp, half][0][:], h_q[rp, half][1][:], h_rj[rp, half][:])
 
-        def load_wd(rp):
-            wd_raw[rp] = staged([P, PACK, N], F32, "wd_raw%d" % rp, AT_WD[rp])
-            nc.sync.dma_start(wd_raw[rp][:], wd[rp * PASS : (rp + 1) * PASS, :].rearrange("(p t) n -> p t n", t=PACK))
-
         def round_wd(rp, shares):
             wd_g[rp] = staged([P, N * PACK], BF16, "wd_g%d" % rp, AT_WD_G[rp])
             round_in_shares(
@@ -299,13 +281,12 @@ def tile_list_segment_reassortment_fitness_kernel(
                 shares,
             )
 
-        def quantise_wd(rp, first=0, last=N):
-            if first == 0:
-                wd_q[rp] = (held([P, N], U32, "wd_w%d" % rp), held([P, N], U8, "wd_s%d" % rp))
-            quantise(wd_q[rp][0][:, first:last], wd_q[rp][1][:, first:last], wd_g[rp][:, PACK * first : PACK * last])
+        def quantise_wd(rp):
+            wd_q[rp] = (held([P, N], U32, "wd_w%d" % rp), held([P, N], U8, "wd_s%d" % rp))
+            quantise(wd_q[rp][0][:], wd_q[rp][1][:], wd_g[rp][:])
 
         def make_y(half, first):
-            y_bank = psum.tile([P, 2, HALF], F32, name="y_bank", tag=("b_then_y", "c_then_y")[first // 2])
+            y_bank = psum.tile([P, 2, HALF], F32, name="y_bank", tag="sums")
             for i in (first, first + 1):
                 cols = slice(i * P, (i + 1) * P)
                 for rp in range(R_PASSES):
@@ -319,63 +300,70 @@ def tile_list_segment_reassortment_fitness_kernel(
                         stop=(rp == R_PASSES - 1),
                     )
             for i in (first, first + 1):
-                ys[half, i] = placed([P, HALF], F32, "y%d%d" % (half, i), Y_ON.get((half, i)))
+                ys[half, i] = held([P, HALF], F32, "y%d%d" % (half, i))
                 nc.scalar.activation(ys[half, i][:], y_bank[:, i - first, :], IDENTITY, bias=bias_cols[:, i : i + 1])
 
         on_vector, on_scalar = nc.vector.tensor_copy, nc.scalar.copy
-        for half in range(HALVES):
-            for rp in range(R_PASSES):
-                for chunk in range(CHUNKS * half, CHUNKS * (half + 1)):
-                    multiply_b_c(rp, chunk)
-        round_wa(0, 0, [(on_vector, 64), (on_vector, 64)])
+        def multiply_b_c(rp, chunk):
+            make_b(rp, chunk)
+            multiply_by_c(rp, chunk)
+
+        for chunk in range(HALVES * CHUNKS):
+            make_b(0, chunk)
+        for chunk in range(CHUNKS):
+            make_b(1, chunk)
+        round_wa(0, 0, [(on_vector, 128)])
         quantise_wa(0, 0)
-        round_wa(1, 0, [(on_vector, 64), (on_scalar, 64)])
-        quantise_wa(1, 0)
-        round_wa(0, 1, [(on_scalar, 64), (on_scalar, 64)])
+        for chunk in range(HALVES * CHUNKS):
+            multiply_by_c(0, chunk)
         for rp in range(R_PASSES):
             load_wd(rp)
-        bias_cols = staged([P, PACK], F32, "bias_cols", AT_BIAS)
-        nc.sync.dma_start(bias_cols[:], bias.rearrange("(p i) -> p i", i=PACK))
         weights = staged([P, S], F32, "weights", AT_WGO)
         nc.sync.dma_start(weights[:], wgo)
-        nc.sync.dma_start(place[:], offs2)
+        bias_cols = staged([P, PACK], F32, "bias_cols", AT_BIAS)
+        nc.sync.dma_start(bias_cols[:], bias.rearrange("(p i) -> p i", i=PACK))
+        multiply_by_c(1, 0)
+        multiply_by_c(1, 1)
+        round_wa(1, 0, [(on_vector, 32), (on_scalar, 96)])
+        multiply_b_c(1, 2)
+        quantise_wa(1, 0)
+        multiply_b_c(1, 3)
+        round_wa(0, 1, [(on_scalar, 128)])
         make_h(0, 0)
         make_h(0, 1)
-        quantise_wa(0, 1)
-        round_wa(1, 1, [(on_vector, 64), (on_scalar, 64)])
-        turn_h(0, 0)
         make_h(0, 2)
-        quantise_wa(1, 1)
+        round_wa(1, 1, [(on_vector, 48), (on_scalar, 80)])
+        quantise_wa(0, 1)
         make_h(0, 3)
-        quantise_h(0, 0)
+        quantise_wa(1, 1)
+        turn_h(0, 0)
         turn_h(0, 1)
+        quantise_h(0, 0)
         round_wd(0, [(on_scalar, 128)])
         make_h(1, 0)
         make_h(1, 1)
         quantise_h(0, 1)
         turn_h(1, 0)
         make_h(1, 2)
-        round_wd(1, [(on_vector, 128)])
-        quantise_wd(0)
-        quantise_h(1, 0)
-        quantise_wd(1, 0, N // 2)
         make_h(1, 3)
-        quantise_wd(1, N // 2, N)
-        make_y(0, 0)
+        quantise_wd(0)
+        round_wd(1, [(on_vector, 48), (on_scalar, 80)])
         turn_h(1, 1)
+        quantise_h(1, 0)
+        quantise_wd(1)
         quantise_h(1, 1)
-        make_y(0, 2)
-        for first in range(0, PACK, 2):
-            make_y(1, first)
+        for half in range(HALVES):
+            for first in range(0, PACK, 2):
+                make_y(half, first)
 
+        pages = [placed([P, T2], F32, "page%d" % i, AT_PAGE[i]) for i in range(PACK)]
+        for page in pages:
+            nc.gpsimd.memset(page[:], 0.0)
         rows = out.rearrange("(p i) t -> p i t", i=PACK)
         for half in range(HALVES):
             for i in range(PACK):
                 nc.vector.tensor_tensor(
-                    pages[i][:].indirect(place[:, half * HALF // GROUP : (half + 1) * HALF // GROUP]),
-                    ys[half, i][:],
-                    weights[:, entries(half)],
-                    MULT,
+                    pages[i][:].indirect(offsets(place, half)), ys[half, i][:], weights[:, entries(half)], MULT
                 )
                 if half == HALVES - 1:
                     nc.sync.dma_start(rows[:, i, :], pages[i][:])

@@ -358,7 +358,7 @@ def tile_list_segment_reassortment_fitness_kernel(
 
         pages = [placed([P, T2], F32, "page%d" % i, AT_PAGE[i]) for i in range(PACK)]
         for page in pages:
-            nc.gpsimd.memset(page[:], 0.0)
+            nc.vector.memset(page[:], 0.0)
         rows = out.rearrange("(p i) t -> p i t", i=PACK)
         for half in range(HALVES):
             for i in range(PACK):

@@ -212,12 +212,6 @@ def tile_list_segment_reassortment_fitness_kernel(
         def quantise(words, scales, grouped):
             nc.vector.quantize_mx(out=words.bitcast(E4M3), scales=scales, in_=grouped)
 
-        def by_pairs(bank):
-            return bank[:].rearrange("p (m u e) -> p u m e", u=2, e=2)
-
-        def as_pairs(view):
-            return view.rearrange("p (u m e) -> p u m e", u=2, e=2)
-
         b_sb, bc, wa_q, wd_q, h_q, h_jr, h_rj, wa_g, wd_g, ys = {}, {}, {}, {}, {}, {}, {}, {}, {}, {}
 
         def make_b(rp, chunk):
@@ -226,7 +220,7 @@ def tile_list_segment_reassortment_fitness_kernel(
             project(b_bank, chunk, [wb_w[:, g, 2 * rp * BANK : 2 * (rp + 1) * BANK] for g in range(K_PASSES)],
                     [wb_sc[:, g, cols] for g in range(K_PASSES)], E2M1)
             b_sb[rp, chunk] = placed([P, BANK], F32, "b_sb%d%d" % (rp, chunk), B_ON.get((rp, chunk)))
-            nc.scalar.copy(as_pairs(b_sb[rp, chunk][:]), by_pairs(b_bank))
+            nc.scalar.copy(b_sb[rp, chunk][:], b_bank[:])
 
         def multiply_by_c(rp, chunk):
             cols = slice(rp * BANK, (rp + 1) * BANK)
@@ -234,7 +228,7 @@ def tile_list_segment_reassortment_fitness_kernel(
             project(c_bank, chunk, [wc_w[rp][:, g, :] for g in range(K_PASSES)],
                     [wc_sc[WC_ROW:P, g, cols] for g in range(K_PASSES)], E4M3)
             bc[rp, chunk] = placed([P, BANK], F32, "bc%d%d" % (rp, chunk), BC_ON.get((rp, chunk)))
-            nc.vector.tensor_tensor(as_pairs(bc[rp, chunk][:]), by_pairs(c_bank), as_pairs(b_sb[rp, chunk][:]), MULT)
+            nc.vector.tensor_tensor(bc[rp, chunk][:], c_bank[:], b_sb[rp, chunk][:], MULT)
 
         def round_wa(g, rp, shares):
             wa_g[g, rp] = staged([P, BANK * PACK], BF16, "wa_g%d%d" % (g, rp), AT_WA_G[g, rp])
@@ -255,14 +249,14 @@ def tile_list_segment_reassortment_fitness_kernel(
             a_bank = psum.tile([P, BANK], F32, name="a_bank", tag="sums")
             project(a_bank, chunk, [wa_q[g, rp][0][:] for g in range(K_PASSES)],
                     [wa_q[g, rp][1][:] for g in range(K_PASSES)], E4M3)
-            nc.vector.tensor_tensor(as_pairs(h_jr[rp, half][:, s, :]), by_pairs(a_bank), as_pairs(bc[rp, chunk][:]), MULT)
+            nc.vector.tensor_tensor(h_jr[rp, half][:, s, :], a_bank[:], bc[rp, chunk][:], MULT)
 
         def turn_h(rp, half):
             words = h_jr[rp, half][:].rearrange("p s r -> p (s r)").bitcast(F32)
             turned = psum_turn.tile([P, CHUNKS, 2, P], F32, name="turned", tag="turned")
             for s in range(CHUNKS):
                 for u in range(2):
-                    nc.tensor.transpose(turned[:, s, u, :], words[:, (2 * s + u) * P : (2 * s + u + 1) * P], ident[:])
+                    nc.tensor.transpose(turned[:, s, u, :], words[:, 2 * s * P + u : 2 * (s + 1) * P : 2], ident[:])
             h_rj[rp, half] = held([P, HALF * PACK], BF16, "hT%d%d" % (rp, half))
             nc.scalar.copy(
                 h_rj[rp, half][:].bitcast(F32).rearrange("p (s j u) -> p s j u", s=CHUNKS, u=2),

@@ -44,10 +44,10 @@ ROUNDED = 2 * PACK * BANK
 AT_WC0 = 0
 AT_TS = AT_WC0 + 4096 - EDGE
 AT_WA00 = AT_TS + T - EDGE
-AT_WC1 = AT_WA00 + PIECE
-AT_TAB0 = AT_WC1 + 4096 - EDGE
-AT_WA10 = AT_TAB0 + TABLE - EDGE
-AT_TAB1 = AT_WA10 + PIECE
+AT_WA10 = AT_WA00 + PIECE
+AT_TAB0 = AT_WA10 + PIECE - EDGE
+AT_WC1 = AT_TAB0 + TABLE - EDGE
+AT_TAB1 = AT_WC1 + 4096
 AT_PAGE2 = AT_TAB1
 AT_PAGE3 = AT_TAB1 + PAGE
 AT_WA01 = AT_TAB1 + TABLE
@@ -64,12 +64,15 @@ AT_WC = [AT_WC0, AT_WC1]
 AT_WA = {(0, 0): AT_WA00, (1, 0): AT_WA10, (0, 1): AT_WA01, (1, 1): AT_WA11}
 AT_WD = [AT_WD0, AT_WD1]
 AT_PAGE = [None, None, AT_PAGE2, AT_PAGE3]
-AT_WA_G = {(0, 0): AT_G, (1, 0): AT_G + ROUNDED, (0, 1): AT_WA10 + EDGE, (1, 1): AT_G + 3 * ROUNDED}
-AT_WA_W = {(0, 1): AT_G + 2 * ROUNDED}
-AT_WD_G = [AT_G + 4 * ROUNDED, AT_G + 5 * ROUNDED]
-B_ON = {(0, 0): AT_B00, (0, 2): AT_BIAS, (0, 3): AT_WA_G[1, 0]}
-BC_ON = {(0, 1): AT_WA_W[0, 1], (0, 2): AT_WA_G[1, 1], (1, 1): AT_WD_G[1]}
-H_ON = {(0, 1): AT_WD_G[0]}
+AT_WA_G = {(0, 0): AT_G, (1, 0): AT_G + ROUNDED, (0, 1): AT_G + ROUNDED, (1, 1): AT_G + 2 * ROUNDED}
+AT_WD_G = [AT_G + 3 * ROUNDED, AT_G + 4 * ROUNDED]
+AT_Y = AT_G + 5 * ROUNDED
+AT_W = AT_Y + 2048
+AT_WA_W = {(1, 0): AT_W, (0, 1): AT_W + 2048, (1, 1): AT_W + 2 * 2048}
+B_ON = {(0, 0): AT_B00, (0, 2): AT_BIAS, (1, 1): AT_WA_W[1, 0], (1, 2): AT_WA_G[1, 1]}
+BC_ON = {(0, 2): AT_WA_W[0, 1], (0, 3): AT_WA_W[1, 1], (1, 1): AT_WD_G[1]}
+H_ON = {(0, 1): AT_WD_G[0], (1, 1): AT_Y}
+Y_ON = {(0, 1): AT_Y, (0, 2): AT_Y + 1024}
 
 
 def tile_list_segment_reassortment_fitness_kernel(
@@ -106,7 +109,7 @@ def tile_list_segment_reassortment_fitness_kernel(
 
         load_scale_rows(wb_sc, wb_scales, 0)
         ts = [held([P, T], U8, "ts0"), staged([P, T], U8, "ts1", AT_TS)]
-        for g, engine in enumerate((nc.gpsimd, nc.vector)):
+        for g, engine in enumerate((nc.vector, nc.vector)):
             engine.memset(ts[g][:].bitcast(I32), 0)
             nc.sync.dma_start(ts[g][:].bitcast(I32)[0:P:BLOCK], tab_scales[g].bitcast(I32))
         tab = {}
@@ -186,8 +189,8 @@ def tile_list_segment_reassortment_fitness_kernel(
             nc.vector.tensor_copy(v_half[:], tab[1][:].bitcast(U32).indirect(offsets(pick, half)))
             for s in range(CHUNKS):
                 v_chunk[1, CHUNKS * half + s] = v_half[:, s * P : (s + 1) * P]
-        load_wc(1)
         load_wa(1, 0)
+        load_wc(1)
         load_wa(0, 1)
         load_wa(1, 1)
 
@@ -236,6 +239,14 @@ def tile_list_segment_reassortment_fitness_kernel(
                 wa_g[g, rp][:].rearrange("p (c i t) -> p c t i", i=4, t=PACK),
                 wa_raw[g, rp][:].rearrange("p t (c i) -> p c t i", i=4),
                 shares,
+            )
+
+        def round_wa_on_gpsimd(g, rp):
+            wa_g[g, rp] = staged([P, BANK * PACK], BF16, "wa_g%d%d" % (g, rp), AT_WA_G[g, rp])
+            nc.gpsimd.tensor_scalar(
+                wa_g[g, rp][:].rearrange("p (c t) -> p c t", t=PACK),
+                wa_raw[g, rp][:].rearrange("p t c -> p c t"),
+                1.0, 0.0, MULT, ADD,
             )
 
         def quantise_wa(g, rp):
@@ -294,7 +305,7 @@ def tile_list_segment_reassortment_fitness_kernel(
                         stop=(rp == R_PASSES - 1),
                     )
             for i in (first, first + 1):
-                ys[half, i] = held([P, HALF], F32, "y%d%d" % (half, i))
+                ys[half, i] = placed([P, HALF], F32, "y%d%d" % (half, i), Y_ON.get((half, i)))
                 nc.scalar.activation(ys[half, i][:], y_bank[:, i - first, :], IDENTITY, bias=bias_cols[:, i : i + 1])
 
         on_vector, on_scalar = nc.vector.tensor_copy, nc.scalar.copy
@@ -316,17 +327,17 @@ def tile_list_segment_reassortment_fitness_kernel(
         nc.sync.dma_start(weights[:], wgo)
         bias_cols = staged([P, PACK], F32, "bias_cols", AT_BIAS)
         nc.sync.dma_start(bias_cols[:], bias.rearrange("(p i) -> p i", i=PACK))
+        round_wa_on_gpsimd(1, 0)
         multiply_by_c(1, 0)
         multiply_by_c(1, 1)
-        round_wa(1, 0, [(on_vector, 32), (on_scalar, 96)])
-        multiply_b_c(1, 2)
         quantise_wa(1, 0)
+        round_wa_on_gpsimd(0, 1)
+        multiply_b_c(1, 2)
         multiply_b_c(1, 3)
-        round_wa(0, 1, [(on_scalar, 128)])
+        round_wa(1, 1, [(on_scalar, 128)])
         make_h(0, 0)
         make_h(0, 1)
         make_h(0, 2)
-        round_wa(1, 1, [(on_vector, 48), (on_scalar, 80)])
         quantise_wa(0, 1)
         make_h(0, 3)
         quantise_wa(1, 1)
@@ -338,17 +349,18 @@ def tile_list_segment_reassortment_fitness_kernel(
         make_h(1, 1)
         quantise_h(0, 1)
         turn_h(1, 0)
-        make_h(1, 2)
-        make_h(1, 3)
-        quantise_wd(0)
         round_wd(1, [(on_vector, 48), (on_scalar, 80)])
-        turn_h(1, 1)
+        quantise_wd(0)
         quantise_h(1, 0)
+        make_h(1, 2)
         quantise_wd(1)
+        make_h(1, 3)
+        turn_h(1, 1)
+        for first in range(0, PACK, 2):
+            make_y(0, first)
         quantise_h(1, 1)
-        for half in range(HALVES):
-            for first in range(0, PACK, 2):
-                make_y(half, first)
+        for first in range(0, PACK, 2):
+            make_y(1, first)
 
         pages = [placed([P, T2], F32, "page%d" % i, AT_PAGE[i]) for i in range(PACK)]
         for page in pages:

@@ -58,7 +58,8 @@ AT_B00 = AT_WD0 + PIECE - EDGE
 AT_WD1 = AT_B00 + 2048 - EDGE
 AT_BIAS = AT_WD1 + PIECE
 AT_WGO = AT_BIAS + EDGE
-AT_G = AT_WGO + 2048
+AT_ONES = AT_WGO + 2048
+AT_G = AT_ONES + 2048
 AT_TAB = [AT_TAB0, AT_TAB1]
 AT_WC = [AT_WC0, AT_WC1]
 AT_WA = {(0, 0): AT_WA00, (1, 0): AT_WA10, (0, 1): AT_WA01, (1, 1): AT_WA11}
@@ -70,8 +71,9 @@ AT_Y = AT_G + 5 * ROUNDED
 AT_W = AT_Y + 2048
 AT_WA_W = {(1, 0): AT_W, (0, 1): AT_W + 2048, (1, 1): AT_W + 2 * 2048}
 B_ON = {(0, 0): AT_B00, (0, 2): AT_BIAS, (1, 1): AT_WA_W[1, 0], (1, 2): AT_WA_G[1, 1]}
-BC_ON = {(0, 2): AT_WA_W[0, 1], (0, 3): AT_WA_W[1, 1], (1, 1): AT_WD_G[1]}
-H_ON = {(0, 1): AT_WD_G[0], (1, 1): AT_Y}
+BC_ON = {(0, 1): AT_WA_W[0, 1], (0, 2): AT_WA_W[1, 1], (1, 0): AT_WD_G[1]}
+HT_ON = {}
+H_ON = {(0, 0): AT_WD_G[0], (1, 1): AT_Y}
 Y_ON = {(0, 1): AT_Y, (0, 2): AT_Y + 1024}
 
 
@@ -99,15 +101,16 @@ def tile_list_segment_reassortment_fitness_kernel(
         place = held([P, S // GROUP], U16, "place")
         nc.sync.dma_start(pick[:], offs)
         wb_sc = held([P, K_PASSES, H], U8, "wb_sc")
-        wc_sc = held([P, K_PASSES, H], U8, "wc_sc")
         v_scales = held([P, K_PASSES, S], U8, "v_scales")
 
-        def load_scale_rows(plane, scales, first):
+        def load_scale_rows(queue, plane, scales, first):
             by_row = scales.rearrange("g (d x) c -> x d g c", x=ROWS)
             for x in range(ROWS):
-                nc.sync.dma_start(plane[:].bitcast(I32)[first + x : P : QUAD], by_row[x].bitcast(I32))
+                queue.dma_start(plane[:].bitcast(I32)[first + x : P : QUAD], by_row[x].bitcast(I32))
 
-        load_scale_rows(wb_sc, wb_scales, 0)
+        wb_w = held([P, K_PASSES, 2 * H], U8, "wb_w")
+        nc.sync.dma_start(wb_w[:].bitcast(I32), wb_words.rearrange("g p c -> p g c").bitcast(I32))
+        load_scale_rows(nc.sync, wb_sc, wb_scales, 0)
         ts = [held([P, T], U8, "ts0"), staged([P, T], U8, "ts1", AT_TS)]
         for g, engine in enumerate((nc.vector, nc.vector)):
             engine.memset(ts[g][:].bitcast(I32), 0)
@@ -119,10 +122,9 @@ def tile_list_segment_reassortment_fitness_kernel(
             nc.sync.dma_start(tab[g][:], tab_words[g].rearrange("p t i -> p (t i)").bitcast(I32))
 
         load_table(0)
-        load_scale_rows(wc_sc, wc_scales, WC_ROW)
         load_table(1)
 
-        ones = held([P, P], F32, "ones")
+        ones = staged([P, P], F32, "ones", AT_ONES)
         column = held([P, P], F32, "column")
         row = held([P, P], F32, "row")
         apart = held([P, P], F32, "apart")
@@ -130,13 +132,13 @@ def tile_list_segment_reassortment_fitness_kernel(
         nc.vector.memset(ones[:], 1.0)
         nc.vector.tensor_tensor_scan(column[:], ones[:], ones[:], 0.0, MULT, ADD)
         nc.vector.transpose(row[:], column[:])
+        wc_sc = staged([P, K_PASSES, H], U8, "wc_sc", AT_ONES)
+        load_scale_rows(nc.gpsimd, wc_sc, wc_scales, WC_ROW)
         for d in range(QUADS):
             part = slice(QUAD * d, QUAD * (d + 1))
             nc.scalar.activation(apart[part, :], column[part, :], ABS, bias=row[part, QUAD * d : QUAD * d + 1], scale=-1.0)
         nc.scalar.activation(ident[:], apart[:], RELU, bias=1.0, scale=-1.0)
 
-        wb_w = held([P, K_PASSES, 2 * H], U8, "wb_w")
-        nc.sync.dma_start(wb_w[:].bitcast(I32), wb_words.rearrange("g p c -> p g c").bitcast(I32))
         nc.sync.dma_start(place[:], offs2)
         wc_w, wa_raw, wd_raw = {}, {}, {}
 
@@ -206,6 +208,9 @@ def tile_list_segment_reassortment_fitness_kernel(
                     stop=(g == K_PASSES - 1),
                 )
 
+        def on_gpsimd(dst, src):
+            nc.gpsimd.tensor_scalar(dst.rearrange("p c t i -> p c i t"), src.rearrange("p c t i -> p c i t"), 1.0, 0.0, MULT, ADD)
+
         def round_in_shares(dst, src, shares):
             first = 0
             for copy, count in shares:
@@ -241,14 +246,6 @@ def tile_list_segment_reassortment_fitness_kernel(
                 shares,
             )
 
-        def round_wa_on_gpsimd(g, rp):
-            wa_g[g, rp] = staged([P, BANK * PACK], BF16, "wa_g%d%d" % (g, rp), AT_WA_G[g, rp])
-            nc.gpsimd.tensor_scalar(
-                wa_g[g, rp][:].rearrange("p (c t) -> p c t", t=PACK),
-                wa_raw[g, rp][:].rearrange("p t c -> p c t"),
-                1.0, 0.0, MULT, ADD,
-            )
-
         def quantise_wa(g, rp):
             wa_q[g, rp] = (placed([P, BANK], U32, "wa_w%d%d" % (g, rp), AT_WA_W.get((g, rp))), held([P, BANK], U8, "wa_s%d%d" % (g, rp)))
             quantise(wa_q[g, rp][0][:], wa_q[g, rp][1][:], wa_g[g, rp][:])
@@ -268,7 +265,7 @@ def tile_list_segment_reassortment_fitness_kernel(
             for s in range(CHUNKS):
                 for u in range(2):
                     nc.tensor.transpose(turned[:, s, u, :], words[:, 2 * s * P + u : 2 * (s + 1) * P : 2], ident[:])
-            h_rj[rp, half] = held([P, HALF * PACK], BF16, "hT%d%d" % (rp, half))
+            h_rj[rp, half] = placed([P, HALF * PACK], BF16, "hT%d%d" % (rp, half), HT_ON.get((rp, half)))
             nc.scalar.copy(
                 h_rj[rp, half][:].bitcast(F32).rearrange("p (s j u) -> p s j u", s=CHUNKS, u=2),
                 turned[:].rearrange("p s u j -> p s j u"),
@@ -327,37 +324,37 @@ def tile_list_segment_reassortment_fitness_kernel(
         nc.sync.dma_start(weights[:], wgo)
         bias_cols = staged([P, PACK], F32, "bias_cols", AT_BIAS)
         nc.sync.dma_start(bias_cols[:], bias.rearrange("(p i) -> p i", i=PACK))
-        round_wa_on_gpsimd(1, 0)
+        round_wa(1, 0, [(on_gpsimd, 128)])
         multiply_by_c(1, 0)
         multiply_by_c(1, 1)
         quantise_wa(1, 0)
-        round_wa_on_gpsimd(0, 1)
+        round_wa(0, 1, [(on_gpsimd, 128)])
         multiply_b_c(1, 2)
         multiply_b_c(1, 3)
         round_wa(1, 1, [(on_scalar, 128)])
         make_h(0, 0)
         make_h(0, 1)
-        make_h(0, 2)
         quantise_wa(0, 1)
-        make_h(0, 3)
+        make_h(0, 2)
         quantise_wa(1, 1)
+        make_h(0, 3)
         turn_h(0, 0)
-        turn_h(0, 1)
         quantise_h(0, 0)
         round_wd(0, [(on_scalar, 128)])
         make_h(1, 0)
         make_h(1, 1)
-        quantise_h(0, 1)
-        turn_h(1, 0)
         round_wd(1, [(on_vector, 48), (on_scalar, 80)])
+        turn_h(1, 0)
+        turn_h(0, 1)
         quantise_wd(0)
-        quantise_h(1, 0)
         make_h(1, 2)
         quantise_wd(1)
+        quantise_h(1, 0)
         make_h(1, 3)
         turn_h(1, 1)
         for first in range(0, PACK, 2):
             make_y(0, first)
+        quantise_h(0, 1)
         quantise_h(1, 1)
         for first in range(0, PACK, 2):
             make_y(1, first)

@@ -71,7 +71,7 @@ AT_Y = AT_G + 5 * ROUNDED
 AT_W = AT_Y + 2048
 AT_WA_W = {(1, 0): AT_W, (0, 1): AT_W + 2048, (1, 1): AT_W + 2 * 2048}
 B_ON = {(0, 0): AT_B00, (0, 2): AT_BIAS, (1, 1): AT_WA_W[1, 0], (1, 2): AT_WA_G[1, 1]}
-BC_ON = {(0, 1): AT_WA_W[0, 1], (0, 2): AT_WA_W[1, 1], (1, 0): AT_WD_G[1]}
+BC_ON = {(0, 2): AT_WA_W[0, 1], (0, 3): AT_WA_W[1, 1], (1, 0): AT_WD_G[1]}
 HT_ON = {}
 H_ON = {(0, 0): AT_WD_G[0], (1, 1): AT_Y}
 Y_ON = {(0, 1): AT_Y, (0, 2): AT_Y + 1024}
@@ -306,10 +306,6 @@ def tile_list_segment_reassortment_fitness_kernel(
                 nc.scalar.activation(ys[half, i][:], y_bank[:, i - first, :], IDENTITY, bias=bias_cols[:, i : i + 1])
 
         on_vector, on_scalar = nc.vector.tensor_copy, nc.scalar.copy
-        def multiply_b_c(rp, chunk):
-            make_b(rp, chunk)
-            multiply_by_c(rp, chunk)
-
         for chunk in range(HALVES * CHUNKS):
             make_b(0, chunk)
         for chunk in range(CHUNKS):
@@ -325,19 +321,20 @@ def tile_list_segment_reassortment_fitness_kernel(
         bias_cols = staged([P, PACK], F32, "bias_cols", AT_BIAS)
         nc.sync.dma_start(bias_cols[:], bias.rearrange("(p i) -> p i", i=PACK))
         round_wa(1, 0, [(on_gpsimd, 128)])
+        make_b(1, 2)
+        make_b(1, 3)
         multiply_by_c(1, 0)
         multiply_by_c(1, 1)
         quantise_wa(1, 0)
-        round_wa(0, 1, [(on_gpsimd, 128)])
-        multiply_b_c(1, 2)
-        multiply_b_c(1, 3)
+        round_wa(0, 1, [(on_gpsimd, 96), (on_scalar, 32)])
+        multiply_by_c(1, 2)
+        multiply_by_c(1, 3)
         round_wa(1, 1, [(on_scalar, 128)])
-        make_h(0, 0)
-        make_h(0, 1)
+        for chunk in range(3):
+            make_h(0, chunk)
         quantise_wa(0, 1)
-        make_h(0, 2)
-        quantise_wa(1, 1)
         make_h(0, 3)
+        quantise_wa(1, 1)
         turn_h(0, 0)
         quantise_h(0, 0)
         round_wd(0, [(on_scalar, 128)])

@@ -71,9 +71,9 @@ AT_Y = AT_G + 5 * ROUNDED
 AT_W = AT_Y + 2048
 AT_WA_W = {(1, 0): AT_W, (0, 1): AT_W + 2048, (1, 1): AT_W + 2 * 2048}
 B_ON = {(0, 0): AT_B00, (0, 2): AT_BIAS, (1, 1): AT_WA_W[1, 0], (1, 2): AT_WA_G[1, 1]}
-BC_ON = {(0, 2): AT_WA_W[0, 1], (0, 3): AT_WA_W[1, 1], (1, 0): AT_WD_G[1]}
+BC_ON = {(0, 2): AT_WA_W[0, 1], (0, 3): AT_WA_W[1, 1], (1, 1): AT_WD_G[1]}
 HT_ON = {}
-H_ON = {(0, 0): AT_WD_G[0], (1, 1): AT_Y}
+H_ON = {(0, 1): AT_WD_G[0], (1, 1): AT_Y}
 Y_ON = {(0, 1): AT_Y, (0, 2): AT_Y + 1024}
 
 
@@ -336,22 +336,22 @@ def tile_list_segment_reassortment_fitness_kernel(
         make_h(0, 3)
         quantise_wa(1, 1)
         turn_h(0, 0)
+        turn_h(0, 1)
         quantise_h(0, 0)
         round_wd(0, [(on_scalar, 128)])
         make_h(1, 0)
         make_h(1, 1)
-        round_wd(1, [(on_vector, 48), (on_scalar, 80)])
+        quantise_h(0, 1)
         turn_h(1, 0)
-        turn_h(0, 1)
+        round_wd(1, [(on_vector, 48), (on_scalar, 80)])
         quantise_wd(0)
+        quantise_h(1, 0)
         make_h(1, 2)
         quantise_wd(1)
-        quantise_h(1, 0)
         make_h(1, 3)
         turn_h(1, 1)
         for first in range(0, PACK, 2):
             make_y(0, first)
-        quantise_h(0, 1)
         quantise_h(1, 1)
         for first in range(0, PACK, 2):
             make_y(1, first)

@@ -85,7 +85,8 @@ def tile_list_segment_reassortment_fitness_kernel(
     with ExitStack() as ctx:
         keep = ctx.enter_context(tc.tile_pool(name="keep", bufs=1))
         stage = ctx.enter_context(tc.tile_pool(name="stage", bufs=1))
-        psum = ctx.enter_context(tc.psum_pool(name="psum", bufs=6))
+        psum = ctx.enter_context(tc.psum_pool(name="psum", bufs=5))
+        psum_late = ctx.enter_context(tc.psum_pool(name="psum_late", bufs=1))
         psum_turn = ctx.enter_context(tc.psum_pool(name="psum_turn", bufs=2))
 
         def held(shape, dtype, name):
@@ -224,7 +225,7 @@ def tile_list_segment_reassortment_fitness_kernel(
 
         def make_b(rp, chunk):
             cols = slice(rp * BANK, (rp + 1) * BANK)
-            b_bank = psum.tile([P, BANK], F32, name="b_bank", tag="sums")
+            b_bank = (psum_late if (rp, chunk) == (1, 1) else psum).tile([P, BANK], F32, name="b_bank", tag="sums")
             project(b_bank, chunk, [wb_w[:, g, 2 * rp * BANK : 2 * (rp + 1) * BANK] for g in range(K_PASSES)],
                     [wb_sc[:, g, cols] for g in range(K_PASSES)], E2M1)
             b_sb[rp, chunk] = placed([P, BANK], F32, "b_sb%d%d" % (rp, chunk), B_ON.get((rp, chunk)))
@@ -254,7 +255,7 @@ def tile_list_segment_reassortment_fitness_kernel(
             half, s = divmod(chunk, CHUNKS)
             if s == 0:
                 h_jr[rp, half] = placed([P, CHUNKS, BANK], BF16, "h%d%d" % (rp, half), H_ON.get((rp, half)))
-            a_bank = psum.tile([P, BANK], F32, name="a_bank", tag="sums")
+            a_bank = (psum_late if rp == 1 and chunk > 0 else psum).tile([P, BANK], F32, name="a_bank", tag="sums")
             project(a_bank, chunk, [wa_q[g, rp][0][:] for g in range(K_PASSES)],
                     [wa_q[g, rp][1][:] for g in range(K_PASSES)], E4M3)
             nc.vector.tensor_tensor(h_jr[rp, half][:, s, :], a_bank[:], bc[rp, chunk][:], MULT)

@@ -35,6 +35,7 @@ HALF = S // HALVES
 CHUNKS = HALF // P
 WARM_UPS = 5
 WC_ROW = 4
+SPLIT_PAGES = 2
 
 EDGE = 64
 PIECE = 4 * PACK * BANK
@@ -58,8 +59,7 @@ AT_B00 = AT_WD0 + PIECE - EDGE
 AT_WD1 = AT_B00 + 2048 - EDGE
 AT_BIAS = AT_WD1 + PIECE
 AT_WGO = AT_BIAS + EDGE
-AT_ONES = AT_WGO + 2048
-AT_G = AT_ONES + 2048
+AT_G = AT_WGO + 2048
 AT_TAB = [AT_TAB0, AT_TAB1]
 AT_WC = [AT_WC0, AT_WC1]
 AT_WA = {(0, 0): AT_WA00, (1, 0): AT_WA10, (0, 1): AT_WA01, (1, 1): AT_WA11}
@@ -74,7 +74,7 @@ B_ON = {(0, 0): AT_B00, (0, 2): AT_BIAS, (1, 1): AT_WA_W[1, 0], (1, 2): AT_WA_G[
 BC_ON = {(0, 2): AT_WA_W[0, 1], (0, 3): AT_WA_W[1, 1], (1, 1): AT_WD_G[1]}
 HT_ON = {}
 H_ON = {(0, 1): AT_WD_G[0], (1, 1): AT_Y}
-Y_ON = {(0, 1): AT_Y, (0, 2): AT_Y + 1024}
+Y_ON = {(0, 1): AT_Y}
 
 
 def tile_list_segment_reassortment_fitness_kernel(
@@ -104,14 +104,14 @@ def tile_list_segment_reassortment_fitness_kernel(
         wb_sc = held([P, K_PASSES, H], U8, "wb_sc")
         v_scales = held([P, K_PASSES, S], U8, "v_scales")
 
-        def load_scale_rows(queue, plane, scales, first):
+        def load_scale_rows(plane, scales, first):
             by_row = scales.rearrange("g (d x) c -> x d g c", x=ROWS)
             for x in range(ROWS):
-                queue.dma_start(plane[:].bitcast(I32)[first + x : P : QUAD], by_row[x].bitcast(I32))
+                nc.sync.dma_start(plane[:].bitcast(I32)[first + x : P : QUAD], by_row[x].bitcast(I32))
 
         wb_w = held([P, K_PASSES, 2 * H], U8, "wb_w")
         nc.sync.dma_start(wb_w[:].bitcast(I32), wb_words.rearrange("g p c -> p g c").bitcast(I32))
-        load_scale_rows(nc.sync, wb_sc, wb_scales, 0)
+        load_scale_rows(wb_sc, wb_scales, 0)
         ts = [held([P, T], U8, "ts0"), staged([P, T], U8, "ts1", AT_TS)]
         for g, engine in enumerate((nc.vector, nc.vector)):
             engine.memset(ts[g][:].bitcast(I32), 0)
@@ -123,9 +123,11 @@ def tile_list_segment_reassortment_fitness_kernel(
             nc.sync.dma_start(tab[g][:], tab_words[g].rearrange("p t i -> p (t i)").bitcast(I32))
 
         load_table(0)
+        wc_sc = held([P, K_PASSES, H], U8, "wc_sc")
+        load_scale_rows(wc_sc, wc_scales, WC_ROW)
         load_table(1)
 
-        ones = staged([P, P], F32, "ones", AT_ONES)
+        ones = held([P, P], F32, "ones")
         column = held([P, P], F32, "column")
         row = held([P, P], F32, "row")
         apart = held([P, P], F32, "apart")
@@ -133,8 +135,6 @@ def tile_list_segment_reassortment_fitness_kernel(
         nc.vector.memset(ones[:], 1.0)
         nc.vector.tensor_tensor_scan(column[:], ones[:], ones[:], 0.0, MULT, ADD)
         nc.vector.transpose(row[:], column[:])
-        wc_sc = staged([P, K_PASSES, H], U8, "wc_sc", AT_ONES)
-        load_scale_rows(nc.gpsimd, wc_sc, wc_scales, WC_ROW)
         for d in range(QUADS):
             part = slice(QUAD * d, QUAD * (d + 1))
             nc.scalar.activation(apart[part, :], column[part, :], ABS, bias=row[part, QUAD * d : QUAD * d + 1], scale=-1.0)
@@ -303,8 +303,13 @@ def tile_list_segment_reassortment_fitness_kernel(
                         stop=(rp == R_PASSES - 1),
                     )
             for i in (first, first + 1):
-                ys[half, i] = placed([P, HALF], F32, "y%d%d" % (half, i), Y_ON.get((half, i)))
-                nc.scalar.activation(ys[half, i][:], y_bank[:, i - first, :], IDENTITY, bias=bias_cols[:, i : i + 1])
+                if i < SPLIT_PAGES:
+                    ys[half, i] = placed([P, HALF], F32, "y%d%d" % (half, i), Y_ON.get((half, i)))[:]
+                else:
+                    if half == 0:
+                        ys[i] = held([P, S], F32, "y%d" % i)
+                    ys[half, i] = ys[i][:, entries(half)]
+                nc.scalar.activation(ys[half, i], y_bank[:, i - first, :], IDENTITY, bias=bias_cols[:, i : i + 1])
 
         on_vector, on_scalar = nc.vector.tensor_copy, nc.scalar.copy
         for chunk in range(HALVES * CHUNKS):
@@ -354,17 +359,22 @@ def tile_list_segment_reassortment_fitness_kernel(
         for first in range(0, PACK, 2):
             make_y(0, first)
         quantise_h(1, 1)
-        for first in range(0, PACK, 2):
-            make_y(1, first)
+        make_y(1, 2)
+        make_y(1, 0)
 
         pages = [placed([P, T2], F32, "page%d" % i, AT_PAGE[i]) for i in range(PACK)]
         for page in pages:
             nc.vector.memset(page[:], 0.0)
         rows = out.rearrange("(p i) t -> p i t", i=PACK)
-        for half in range(HALVES):
-            for i in range(PACK):
-                nc.vector.tensor_tensor(
-                    pages[i][:].indirect(offsets(place, half)), ys[half, i][:], weights[:, entries(half)], MULT
-                )
-                if half == HALVES - 1:
-                    nc.sync.dma_start(rows[:, i, :], pages[i][:])
+
+        def scatter_half(half, i):
+            nc.vector.tensor_tensor(pages[i][:].indirect(offsets(place, half)), ys[half, i], weights[:, entries(half)], MULT)
+
+        for i in range(SPLIT_PAGES):
+            scatter_half(0, i)
+        for i in range(SPLIT_PAGES, PACK):
+            nc.vector.tensor_tensor(pages[i][:].indirect(place[:]), ys[i][:], weights[:], MULT)
+            nc.sync.dma_start(rows[:, i, :], pages[i][:])
+        for i in range(SPLIT_PAGES):
+            scatter_half(1, i)
+            nc.sync.dma_start(rows[:, i, :], pages[i][:])

@@ -32,49 +32,39 @@ K_PASSES = K // PASS
 R_PASSES = H // PASS
 HALVES = 2
 HALF = S // HALVES
-CHUNKS = HALF // P
-WARM_UPS = 5
-WC_ROW = 4
-SPLIT_PAGES = 2
+CHUNKS = S // P
+UNIT = BANK // 2
+WARM_UPS = 3
 
-EDGE = 64
-PIECE = 4 * PACK * BANK
-PAGE = 4 * T2
-TABLE = 4 * T
-ROUNDED = 2 * PACK * BANK
-AT_WC0 = 0
-AT_TS = AT_WC0 + 4096 - EDGE
-AT_WA00 = AT_TS + T - EDGE
-AT_WA10 = AT_WA00 + PIECE
-AT_TAB0 = AT_WA10 + PIECE - EDGE
-AT_WC1 = AT_TAB0 + TABLE - EDGE
-AT_TAB1 = AT_WC1 + 4096
-AT_PAGE2 = AT_TAB1
-AT_PAGE3 = AT_TAB1 + PAGE
-AT_WA01 = AT_TAB1 + TABLE
-AT_PICKED = AT_WA01 + PIECE - EDGE
-AT_WA11 = AT_PICKED + 1024 - EDGE
-AT_WD0 = AT_WA11 + PIECE
-AT_B00 = AT_WD0 + PIECE - EDGE
-AT_WD1 = AT_B00 + 2048 - EDGE
-AT_BIAS = AT_WD1 + PIECE
-AT_WGO = AT_BIAS + EDGE
-AT_G = AT_WGO + 2048
-AT_TAB = [AT_TAB0, AT_TAB1]
-AT_WC = [AT_WC0, AT_WC1]
-AT_WA = {(0, 0): AT_WA00, (1, 0): AT_WA10, (0, 1): AT_WA01, (1, 1): AT_WA11}
-AT_WD = [AT_WD0, AT_WD1]
-AT_PAGE = [None, None, AT_PAGE2, AT_PAGE3]
-AT_WA_G = {(0, 0): AT_G, (1, 0): AT_G + ROUNDED, (0, 1): AT_G + ROUNDED, (1, 1): AT_G + 2 * ROUNDED}
-AT_WD_G = [AT_G + 3 * ROUNDED, AT_G + 4 * ROUNDED]
-AT_Y = AT_G + 5 * ROUNDED
-AT_W = AT_Y + 2048
-AT_WA_W = {(1, 0): AT_W, (0, 1): AT_W + 2048, (1, 1): AT_W + 2 * 2048}
-B_ON = {(0, 0): AT_B00, (0, 2): AT_BIAS, (1, 1): AT_WA_W[1, 0], (1, 2): AT_WA_G[1, 1]}
-BC_ON = {(0, 2): AT_WA_W[0, 1], (0, 3): AT_WA_W[1, 1], (1, 1): AT_WD_G[1]}
-HT_ON = {}
-H_ON = {(0, 1): AT_WD_G[0], (1, 1): AT_Y}
-Y_ON = {(0, 1): AT_Y}
+KIB = 1024
+AT_WA00 = 0
+AT_TS1 = 7 * KIB
+AT_WC0 = 8 * KIB
+AT_WC1 = 12 * KIB
+AT_TAB0 = 14 * KIB
+AT_WA10 = 16 * KIB
+AT_WA01 = 24 * KIB
+AT_TAB1 = 32 * KIB - 256
+AT_PAGE0 = 32 * KIB
+AT_PAGE1 = 36 * KIB
+AT_WA11 = 40 * KIB
+AT_PICKED1 = 48 * KIB - 512
+AT_B0 = 48 * KIB
+AT_B = {(0, 0): AT_B0, (0, 1): AT_B0 + 2 * KIB, (0, 2): AT_B0 + 4 * KIB, (0, 3): AT_B0 + 6 * KIB,
+        (1, 0): 56 * KIB, (1, 1): 58 * KIB, (1, 2): AT_WA10, (1, 3): AT_WA10 + 2 * KIB}
+AT_BC = 60 * KIB
+AT_G00 = 76 * KIB
+AT_G10 = 80 * KIB
+AT_H01 = 84 * KIB
+AT_HT00 = 86 * KIB
+AT_HT11 = 88 * KIB
+AT_HT = {(0, 0): AT_HT00, (1, 1): AT_HT11}
+AT_PAGE2 = 92 * KIB
+AT_PAGE3 = 96 * KIB
+
+
+def at_bc(rp, chunk):
+    return AT_BC + 2 * KIB * (CHUNKS * rp + chunk)
 
 
 def tile_list_segment_reassortment_fitness_kernel(
@@ -85,53 +75,63 @@ def tile_list_segment_reassortment_fitness_kernel(
     with ExitStack() as ctx:
         keep = ctx.enter_context(tc.tile_pool(name="keep", bufs=1))
         stage = ctx.enter_context(tc.tile_pool(name="stage", bufs=1))
-        psum = ctx.enter_context(tc.psum_pool(name="psum", bufs=5))
-        psum_late = ctx.enter_context(tc.psum_pool(name="psum_late", bufs=1))
-        psum_turn = ctx.enter_context(tc.psum_pool(name="psum_turn", bufs=2))
+        psum = ctx.enter_context(tc.psum_pool(name="psum", bufs=1))
 
-        def held(shape, dtype, name):
-            return keep.tile(shape, dtype, name=name, align_bytes=64)
+        def placed(shape, dtype, name, offset=None):
+            if offset is None:
+                return keep.tile(shape, dtype, name=name, align_bytes=256)
+            return stage.tile(shape, dtype, name=name, align_bytes=256, offset=offset)
 
-        def staged(shape, dtype, name, offset):
-            return stage.tile(shape, dtype, name=name, align_bytes=64, offset=offset)
+        def bank(number, shape, name):
+            return psum.tile(shape, F32, name=name, tag="bank%d" % number)
 
-        def placed(shape, dtype, name, offset):
-            return held(shape, dtype, name) if offset is None else staged(shape, dtype, name, offset)
-
-        pick = held([P, S // GROUP], U16, "pick")
-        place = held([P, S // GROUP], U16, "place")
+        pick = placed([P, S // GROUP], U16, "pick")
+        place = placed([P, S // GROUP], U16, "place")
         nc.sync.dma_start(pick[:], offs)
-        wb_sc = held([P, K_PASSES, H], U8, "wb_sc")
-        v_scales = held([P, K_PASSES, S], U8, "v_scales")
 
-        def load_scale_rows(plane, scales, first):
+        def load_scale_rows(queues, plane, scales):
             by_row = scales.rearrange("g (d x) c -> x d g c", x=ROWS)
-            for x in range(ROWS):
-                nc.sync.dma_start(plane[:].bitcast(I32)[first + x : P : QUAD], by_row[x].bitcast(I32))
+            for x, queue in enumerate(queues):
+                queue.dma_start(plane[:].bitcast(I32)[x:P:QUAD], by_row[x].bitcast(I32))
 
-        wb_w = held([P, K_PASSES, 2 * H], U8, "wb_w")
-        nc.sync.dma_start(wb_w[:].bitcast(I32), wb_words.rearrange("g p c -> p g c").bitcast(I32))
-        load_scale_rows(wb_sc, wb_scales, 0)
-        ts = [held([P, T], U8, "ts0"), staged([P, T], U8, "ts1", AT_TS)]
-        for g, engine in enumerate((nc.vector, nc.vector)):
+        wb_sc = placed([P, K_PASSES, H], U8, "wb_sc")
+        wc_sc = placed([P, K_PASSES, H], U8, "wc_sc")
+        ts = [placed([P, T], U8, "ts0", AT_TAB1), placed([P, T], U8, "ts1", AT_TS1)]
+        load_scale_rows([nc.sync, nc.scalar, nc.scalar, nc.scalar], wb_sc, wb_scales)
+        for g, engine in enumerate((nc.gpsimd, nc.vector)):
             engine.memset(ts[g][:].bitcast(I32), 0)
             nc.sync.dma_start(ts[g][:].bitcast(I32)[0:P:BLOCK], tab_scales[g].bitcast(I32))
-        tab = {}
+        load_scale_rows([nc.gpsimd] * ROWS, wc_sc, wc_scales)
 
-        def load_table(g):
-            tab[g] = staged([P, T], I32, "tab%d" % g, AT_TAB[g])
+        tab, wc_w, wa_raw, wd_raw = {}, {}, {}, {}
+
+        def load_table(g, offset):
+            tab[g] = placed([P, T], I32, "tab%d" % g, offset)
             nc.sync.dma_start(tab[g][:], tab_words[g].rearrange("p t i -> p (t i)").bitcast(I32))
 
-        load_table(0)
-        wc_sc = held([P, K_PASSES, H], U8, "wc_sc")
-        load_scale_rows(wc_sc, wc_scales, WC_ROW)
-        load_table(1)
+        def load_wc(rp, offset):
+            wc_w[rp] = placed([P, K_PASSES, BANK], I32, "wc_w%d" % rp, offset)
+            cols = wc_words[:, :, rp * BANK : (rp + 1) * BANK, :]
+            nc.sync.dma_start(wc_w[rp][:], cols.rearrange("g p c i -> p g (c i)").bitcast(I32))
 
-        ones = held([P, P], F32, "ones")
-        column = held([P, P], F32, "column")
-        row = held([P, P], F32, "row")
-        apart = held([P, P], F32, "apart")
-        ident = held([P, P], F32, "ident")
+        def load_wa(g, rp, offset):
+            wa_raw[g, rp] = placed([P, PACK, BANK], F32, "wa_raw%d%d" % (g, rp), offset)
+            rows = wa[g * PASS : (g + 1) * PASS, rp * BANK : (rp + 1) * BANK]
+            nc.sync.dma_start(wa_raw[g, rp][:], rows.rearrange("(p t) c -> p t c", t=PACK))
+
+        def load_wd(rp, offset):
+            wd_raw[rp] = placed([P, PACK, N], F32, "wd_raw%d" % rp, offset)
+            nc.sync.dma_start(wd_raw[rp][:], wd[rp * PASS : (rp + 1) * PASS, :].rearrange("(p t) n -> p t n", t=PACK))
+
+        load_table(0, AT_TAB0)
+        wb_w = placed([P, K_PASSES, 2 * H], U8, "wb_w")
+        nc.sync.dma_start(wb_w[:].bitcast(I32), wb_words.rearrange("g p c -> p g c").bitcast(I32))
+
+        ones = placed([P, P], F32, "ones")
+        column = placed([P, P], F32, "column")
+        row = placed([P, P], F32, "row")
+        apart = placed([P, P], F32, "apart")
+        ident = placed([P, P], F32, "ident")
         nc.vector.memset(ones[:], 1.0)
         nc.vector.tensor_tensor_scan(column[:], ones[:], ones[:], 0.0, MULT, ADD)
         nc.vector.transpose(row[:], column[:])
@@ -140,241 +140,245 @@ def tile_list_segment_reassortment_fitness_kernel(
             nc.scalar.activation(apart[part, :], column[part, :], ABS, bias=row[part, QUAD * d : QUAD * d + 1], scale=-1.0)
         nc.scalar.activation(ident[:], apart[:], RELU, bias=1.0, scale=-1.0)
 
-        nc.sync.dma_start(place[:], offs2)
-        wc_w, wa_raw, wd_raw = {}, {}, {}
+        picked, v_scales, v_chunk, pages = {}, {}, {}, {}
 
-        def load_wc(rp):
-            wc_w[rp] = staged([P, K_PASSES, BANK], I32, "wc_w%d" % rp, AT_WC[rp])
-            cols = wc_words[:, :, rp * BANK : (rp + 1) * BANK, :]
-            nc.sync.dma_start(wc_w[rp][:], cols.rearrange("g p c i -> p g (c i)").bitcast(I32))
+        def pick_scales(g, offset):
+            picked[g] = placed([P, S], U8, "picked%d" % g, offset)
+            nc.vector.tensor_copy(picked[g][:], ts[g][:].indirect(pick[:]))
+            v_scales[g] = placed([P, S], U8, "v_scales%d" % g)
+            for x in range(ROWS):
+                nc.sync.dma_start(v_scales[g][:].bitcast(I32)[x:P:QUAD], picked[g][:].bitcast(I32)[BLOCK * x : P : QUAD])
 
-        def load_wa(g, rp):
-            wa_raw[g, rp] = staged([P, PACK, BANK], F32, "wa_raw%d%d" % (g, rp), AT_WA[g, rp])
-            rows = wa[g * PASS : (g + 1) * PASS, rp * BANK : (rp + 1) * BANK]
-            nc.sync.dma_start(wa_raw[g, rp][:], rows.rearrange("(p t) c -> p t c", t=PACK))
+        def pick_words(g, first, count):
+            words = placed([P, count * P], U32, "v_words%d%d" % (g, first))
+            lists = pick[:, first * P // GROUP : (first + count) * P // GROUP]
+            nc.vector.tensor_copy(words[:], tab[g][:].bitcast(U32).indirect(lists))
+            for s in range(count):
+                v_chunk[g, first + s] = words[:, s * P : (s + 1) * P]
 
-        def load_wd(rp):
-            wd_raw[rp] = staged([P, PACK, N], F32, "wd_raw%d" % rp, AT_WD[rp])
-            nc.sync.dma_start(wd_raw[rp][:], wd[rp * PASS : (rp + 1) * PASS, :].rearrange("(p t) n -> p t n", t=PACK))
+        def zero_page(i, offset):
+            pages[i] = placed([P, T2], F32, "page%d" % i, offset)
+            nc.gpsimd.memset(pages[i][:], 0.0)
 
-        def entries(half):
-            return slice(half * HALF, (half + 1) * HALF)
-
-        def offsets(lists, half):
-            return lists[:, half * HALF // GROUP : (half + 1) * HALF // GROUP]
-
-        ts_picked = staged([P, K_PASSES, S], U8, "ts_picked", AT_PICKED)
-        for g in range(K_PASSES):
-            nc.vector.tensor_copy(ts_picked[:, g, :], ts[g][:].indirect(pick[:]))
-        for x in range(ROWS):
-            nc.sync.dma_start(
-                v_scales[:].rearrange("p g j -> p (g j)").bitcast(I32)[x:P:QUAD],
-                ts_picked[:].rearrange("p g j -> p (g j)").bitcast(I32)[BLOCK * x : P : QUAD],
-            )
-        load_wa(0, 0)
-        load_wc(0)
-        unread = psum_turn.tile([P, BANK], F32, name="unread", tag="turned")
+        pick_scales(0, None)
+        load_table(1, AT_TAB1)
+        pick_scales(1, AT_PICKED1)
+        load_wc(0, AT_WC0)
+        load_wa(0, 0, AT_WA00)
+        unread = bank(7, [P, BANK], "unread")
         for n in range(WARM_UPS):
             nc.tensor.matmul_mx(
                 out=unread[:],
                 lhsT=tab[0][:, 0:P].bitcast(E4M3),
-                lhsT_scale=ts_picked[:, 1, 0:P],
+                lhsT_scale=picked[0][:, 0:P],
                 rhs=tab[0][:, 0:BANK].bitcast(E4M3),
-                rhs_scale=ts_picked[:, 1, :],
+                rhs_scale=picked[0][:],
                 start=True,
                 stop=True,
             )
-        v_words = held([P, S], U32, "v_words0")
-        nc.vector.tensor_copy(v_words[:], tab[0][:].bitcast(U32).indirect(pick[:]))
-        v_chunk = {(0, c): v_words[:, c * P : (c + 1) * P] for c in range(HALVES * CHUNKS)}
         for half in range(HALVES):
-            v_half = held([P, HALF], U32, "v_words1%d" % half)
-            nc.vector.tensor_copy(v_half[:], tab[1][:].bitcast(U32).indirect(offsets(pick, half)))
-            for s in range(CHUNKS):
-                v_chunk[1, CHUNKS * half + s] = v_half[:, s * P : (s + 1) * P]
-        load_wa(1, 0)
-        load_wc(1)
-        load_wa(0, 1)
-        load_wa(1, 1)
+            pick_words(0, 2 * half, 2)
+        load_wc(1, AT_WC1)
+        load_wa(1, 0, AT_WA10)
+        for half in range(HALVES):
+            pick_words(1, 2 * half, 2)
+        load_wa(0, 1, AT_WA01)
+        load_wa(1, 1, AT_WA11)
+        zero_page(0, AT_PAGE0)
+        zero_page(1, AT_PAGE1)
 
-        def project(bank, chunk, words, scales, fmt):
-            for g in range(K_PASSES):
-                nc.tensor.matmul_mx(
-                    out=bank[:],
-                    lhsT=v_chunk[g, chunk].bitcast(E4M3),
-                    lhsT_scale=v_scales[:, g, chunk * P : (chunk + 1) * P],
-                    rhs=words[g].bitcast(fmt),
-                    rhs_scale=scales[g],
-                    start=(g == 0),
-                    stop=(g == K_PASSES - 1),
-                )
+        def project(sums, chunk, g, words, scales, fmt):
+            nc.tensor.matmul_mx(
+                out=sums[:],
+                lhsT=v_chunk[g, chunk].bitcast(E4M3),
+                lhsT_scale=v_scales[g][:, chunk * P : (chunk + 1) * P],
+                rhs=words.bitcast(fmt),
+                rhs_scale=scales,
+                start=(g == 0),
+                stop=(g == K_PASSES - 1),
+            )
 
         def on_gpsimd(dst, src):
             nc.gpsimd.tensor_scalar(dst.rearrange("p c t i -> p c i t"), src.rearrange("p c t i -> p c i t"), 1.0, 0.0, MULT, ADD)
 
-        def round_in_shares(dst, src, shares):
-            first = 0
-            for copy, count in shares:
-                copy(dst[:, first : first + count], src[:, first : first + count])
-                first = first + count
+        on_vector, on_scalar = nc.vector.tensor_copy, nc.scalar.copy
 
         def quantise(words, scales, grouped):
             nc.vector.quantize_mx(out=words.bitcast(E4M3), scales=scales, in_=grouped)
 
-        b_sb, bc, wa_q, wd_q, h_q, h_jr, h_rj, wa_g, wd_g, ys = {}, {}, {}, {}, {}, {}, {}, {}, {}, {}
+        b_bank, b_sb, bc, wa_g, wa_q, h_jr, h_rj, h_q, wd_g, wd_q = {}, {}, {}, {}, {}, {}, {}, {}, {}, {}
 
-        def make_b(rp, chunk):
-            cols = slice(rp * BANK, (rp + 1) * BANK)
-            b_bank = (psum_late if (rp, chunk) == (1, 1) else psum).tile([P, BANK], F32, name="b_bank", tag="sums")
-            project(b_bank, chunk, [wb_w[:, g, 2 * rp * BANK : 2 * (rp + 1) * BANK] for g in range(K_PASSES)],
-                    [wb_sc[:, g, cols] for g in range(K_PASSES)], E2M1)
-            b_sb[rp, chunk] = placed([P, BANK], F32, "b_sb%d%d" % (rp, chunk), B_ON.get((rp, chunk)))
-            nc.scalar.copy(b_sb[rp, chunk][:], b_bank[:])
+        def b_pass(rp, chunk, g):
+            if g == 0:
+                b_bank[rp, chunk] = bank(CHUNKS * rp + chunk, [P, BANK], "b_bank")
+            project(b_bank[rp, chunk], chunk, g, wb_w[:, g, 2 * rp * BANK : 2 * (rp + 1) * BANK],
+                    wb_sc[:, g, rp * BANK : (rp + 1) * BANK], E2M1)
 
-        def multiply_by_c(rp, chunk):
-            cols = slice(rp * BANK, (rp + 1) * BANK)
-            c_bank = psum.tile([P, BANK], F32, name="c_bank", tag="sums")
-            project(c_bank, chunk, [wc_w[rp][:, g, :] for g in range(K_PASSES)],
-                    [wc_sc[WC_ROW:P, g, cols] for g in range(K_PASSES)], E4M3)
-            bc[rp, chunk] = placed([P, BANK], F32, "bc%d%d" % (rp, chunk), BC_ON.get((rp, chunk)))
+        def copy_b(rp, chunk):
+            b_sb[rp, chunk] = placed([P, BANK], F32, "b_sb%d%d" % (rp, chunk), AT_B[rp, chunk])
+            nc.scalar.copy(b_sb[rp, chunk][:], b_bank[rp, chunk][:])
+
+        def multiply_by_c(rp, chunk, number):
+            c_bank = bank(number, [P, BANK], "c_bank")
+            for g in range(K_PASSES):
+                project(c_bank, chunk, g, wc_w[rp][:, g, :], wc_sc[:, g, rp * BANK : (rp + 1) * BANK], E4M3)
+            bc[rp, chunk] = placed([P, BANK], F32, "bc%d%d" % (rp, chunk), at_bc(rp, chunk))
             nc.vector.tensor_tensor(bc[rp, chunk][:], c_bank[:], b_sb[rp, chunk][:], MULT)
 
-        def round_wa(g, rp, shares):
-            wa_g[g, rp] = staged([P, BANK * PACK], BF16, "wa_g%d%d" % (g, rp), AT_WA_G[g, rp])
-            round_in_shares(
-                wa_g[g, rp][:].rearrange("p (c i t) -> p c t i", i=4, t=PACK),
-                wa_raw[g, rp][:].rearrange("p t (c i) -> p c t i", i=4),
-                shares,
+        def round_wa(g, rp, first, count, copy, offset):
+            wa_g[g, rp, first] = placed([P, count * PACK], BF16, "wa_g%d%d%d" % (g, rp, first), offset)
+            copy(
+                wa_g[g, rp, first][:].rearrange("p (c i t) -> p c t i", i=4, t=PACK),
+                wa_raw[g, rp][:, :, first : first + count].rearrange("p t (c i) -> p c t i", i=4),
             )
 
-        def quantise_wa(g, rp):
-            wa_q[g, rp] = (placed([P, BANK], U32, "wa_w%d%d" % (g, rp), AT_WA_W.get((g, rp))), held([P, BANK], U8, "wa_s%d%d" % (g, rp)))
-            quantise(wa_q[g, rp][0][:], wa_q[g, rp][1][:], wa_g[g, rp][:])
+        def quantise_wa(g, rp, first, count, offset=None):
+            if (g, rp) not in wa_q:
+                wa_q[g, rp] = (placed([P, BANK], U32, "wa_w%d%d" % (g, rp), offset), placed([P, BANK], U8, "wa_s%d%d" % (g, rp)))
+            cols = slice(first, first + count)
+            quantise(wa_q[g, rp][0][:, cols], wa_q[g, rp][1][:, cols], wa_g[g, rp, first][:])
 
-        def make_h(rp, chunk):
-            half, s = divmod(chunk, CHUNKS)
+        def make_h(rp, chunk, number):
+            half, s = divmod(chunk, 2)
             if s == 0:
-                h_jr[rp, half] = placed([P, CHUNKS, BANK], BF16, "h%d%d" % (rp, half), H_ON.get((rp, half)))
-            a_bank = (psum_late if rp == 1 and chunk > 0 else psum).tile([P, BANK], F32, name="a_bank", tag="sums")
-            project(a_bank, chunk, [wa_q[g, rp][0][:] for g in range(K_PASSES)],
-                    [wa_q[g, rp][1][:] for g in range(K_PASSES)], E4M3)
+                h_jr[rp, half] = placed([P, 2, BANK], BF16, "h%d%d" % (rp, half), AT_H01 if (rp, half) == (0, 1) else None)
+            a_bank = bank(number, [P, BANK], "a_bank")
+            for g in range(K_PASSES):
+                project(a_bank, chunk, g, wa_q[g, rp][0][:], wa_q[g, rp][1][:], E4M3)
             nc.vector.tensor_tensor(h_jr[rp, half][:, s, :], a_bank[:], bc[rp, chunk][:], MULT)
 
-        def turn_h(rp, half):
+        def turn_h(rp, half, number):
             words = h_jr[rp, half][:].rearrange("p s r -> p (s r)").bitcast(F32)
-            turned = psum_turn.tile([P, CHUNKS, 2, P], F32, name="turned", tag="turned")
-            for s in range(CHUNKS):
+            turned = bank(number, [P, 2, 2, P], "turned")
+            for s in range(2):
                 for u in range(2):
                     nc.tensor.transpose(turned[:, s, u, :], words[:, 2 * s * P + u : 2 * (s + 1) * P : 2], ident[:])
-            h_rj[rp, half] = placed([P, HALF * PACK], BF16, "hT%d%d" % (rp, half), HT_ON.get((rp, half)))
+            h_rj[rp, half] = placed([P, HALF * PACK], BF16, "hT%d%d" % (rp, half), AT_HT.get((rp, half)))
             nc.scalar.copy(
-                h_rj[rp, half][:].bitcast(F32).rearrange("p (s j u) -> p s j u", s=CHUNKS, u=2),
+                h_rj[rp, half][:].bitcast(F32).rearrange("p (s j u) -> p s j u", s=2, u=2),
                 turned[:].rearrange("p s u j -> p s j u"),
             )
 
         def quantise_h(rp, half):
-            h_q[rp, half] = (held([P, HALF], U32, "h_w%d%d" % (rp, half)), held([P, HALF], U8, "h_s%d%d" % (rp, half)))
-            quantise(h_q[rp, half][0][:], h_q[rp, half][1][:], h_rj[rp, half][:])
+            if half == 0:
+                h_q[rp] = (placed([P, S], U32, "h_w%d" % rp), placed([P, S], U8, "h_s%d" % rp))
+            cols = slice(half * HALF, (half + 1) * HALF)
+            quantise(h_q[rp][0][:, cols], h_q[rp][1][:, cols], h_rj[rp, half][:])
 
-        def round_wd(rp, shares):
-            wd_g[rp] = staged([P, N * PACK], BF16, "wd_g%d" % rp, AT_WD_G[rp])
-            round_in_shares(
-                wd_g[rp][:].rearrange("p (i m t) -> p m t i", i=PACK, t=PACK),
-                wd_raw[rp][:].rearrange("p t (m i) -> p m t i", i=PACK),
-                shares,
+        def round_wd(rp, first, copy, offset):
+            wd_g[rp, first] = placed([P, 2, P * PACK], BF16, "wd_g%d%d" % (rp, first), offset)
+            copy(
+                wd_g[rp, first][:].rearrange("p i (m t) -> p m t i", t=PACK),
+                wd_raw[rp][:].rearrange("p t (m i) -> p m t i", i=PACK)[:, :, :, first : first + 2],
             )
 
-        def quantise_wd(rp):
-            wd_q[rp] = (held([P, N], U32, "wd_w%d" % rp), held([P, N], U8, "wd_s%d" % rp))
-            quantise(wd_q[rp][0][:], wd_q[rp][1][:], wd_g[rp][:])
+        def quantise_wd(rp, first, count, offset=None):
+            words = placed([P, count * P], U32, "wd_w%d%d" % (rp, first), offset)
+            scales = placed([P, count * P], U8, "wd_s%d%d" % (rp, first))
+            pair = first - first % 2
+            grouped = wd_g[rp, pair][:, first - pair : first - pair + count, :]
+            quantise(words[:], scales[:], grouped.rearrange("p i c -> p (i c)"))
+            for i in range(count):
+                wd_q[rp, first + i] = (words[:, i * P : (i + 1) * P], scales[:, i * P : (i + 1) * P])
 
-        def make_y(half, first):
-            y_bank = psum.tile([P, 2, HALF], F32, name="y_bank", tag="sums")
-            for i in (first, first + 1):
-                cols = slice(i * P, (i + 1) * P)
-                for rp in range(R_PASSES):
-                    nc.tensor.matmul_mx(
-                        out=y_bank[:, i - first, :],
-                        lhsT=wd_q[rp][0][:, cols].bitcast(E4M3),
-                        lhsT_scale=wd_q[rp][1][:, cols],
-                        rhs=h_q[rp, half][0][:].bitcast(E4M3),
-                        rhs_scale=h_q[rp, half][1][:],
-                        start=(rp == 0),
-                        stop=(rp == R_PASSES - 1),
-                    )
-            for i in (first, first + 1):
-                if i < SPLIT_PAGES:
-                    ys[half, i] = placed([P, HALF], F32, "y%d%d" % (half, i), Y_ON.get((half, i)))[:]
-                else:
-                    if half == 0:
-                        ys[i] = held([P, S], F32, "y%d" % i)
-                    ys[half, i] = ys[i][:, entries(half)]
-                nc.scalar.activation(ys[half, i], y_bank[:, i - first, :], IDENTITY, bias=bias_cols[:, i : i + 1])
-
-        on_vector, on_scalar = nc.vector.tensor_copy, nc.scalar.copy
-        for chunk in range(HALVES * CHUNKS):
-            make_b(0, chunk)
-        for chunk in range(CHUNKS):
-            make_b(1, chunk)
-        round_wa(0, 0, [(on_vector, 128)])
-        quantise_wa(0, 0)
-        for chunk in range(HALVES * CHUNKS):
-            multiply_by_c(0, chunk)
-        for rp in range(R_PASSES):
-            load_wd(rp)
-        weights = staged([P, S], F32, "weights", AT_WGO)
-        nc.sync.dma_start(weights[:], wgo)
-        bias_cols = staged([P, PACK], F32, "bias_cols", AT_BIAS)
-        nc.sync.dma_start(bias_cols[:], bias.rearrange("(p i) -> p i", i=PACK))
-        round_wa(1, 0, [(on_gpsimd, 128)])
-        make_b(1, 2)
-        make_b(1, 3)
-        multiply_by_c(1, 0)
-        multiply_by_c(1, 1)
-        quantise_wa(1, 0)
-        round_wa(0, 1, [(on_gpsimd, 96), (on_scalar, 32)])
-        multiply_by_c(1, 2)
-        multiply_by_c(1, 3)
-        round_wa(1, 1, [(on_scalar, 128)])
-        for chunk in range(3):
-            make_h(0, chunk)
-        quantise_wa(0, 1)
-        make_h(0, 3)
-        quantise_wa(1, 1)
-        turn_h(0, 0)
-        turn_h(0, 1)
-        quantise_h(0, 0)
-        round_wd(0, [(on_scalar, 128)])
-        make_h(1, 0)
-        make_h(1, 1)
-        quantise_h(0, 1)
-        turn_h(1, 0)
-        round_wd(1, [(on_vector, 48), (on_scalar, 80)])
-        quantise_wd(0)
-        quantise_h(1, 0)
-        make_h(1, 2)
-        quantise_wd(1)
-        make_h(1, 3)
-        turn_h(1, 1)
-        for first in range(0, PACK, 2):
-            make_y(0, first)
-        quantise_h(1, 1)
-        make_y(1, 2)
-        make_y(1, 0)
-
-        pages = [placed([P, T2], F32, "page%d" % i, AT_PAGE[i]) for i in range(PACK)]
-        for page in pages:
-            nc.vector.memset(page[:], 0.0)
         rows = out.rearrange("(p i) t -> p i t", i=PACK)
+        ys = {}
 
-        def scatter_half(half, i):
-            nc.vector.tensor_tensor(pages[i][:].indirect(offsets(place, half)), ys[half, i], weights[:, entries(half)], MULT)
+        def make_y(i, number, first, count):
+            y_bank = bank(number, [P, count], "y_bank")
+            for rp in range(R_PASSES):
+                nc.tensor.matmul_mx(
+                    out=y_bank[:],
+                    lhsT=wd_q[rp, i][0].bitcast(E4M3),
+                    lhsT_scale=wd_q[rp, i][1],
+                    rhs=h_q[rp][0][:, first : first + count].bitcast(E4M3),
+                    rhs_scale=h_q[rp][1][:, first : first + count],
+                    start=(rp == 0),
+                    stop=(rp == R_PASSES - 1),
+                )
+            return y_bank
 
-        for i in range(SPLIT_PAGES):
-            scatter_half(0, i)
-        for i in range(SPLIT_PAGES, PACK):
-            nc.vector.tensor_tensor(pages[i][:].indirect(place[:]), ys[i][:], weights[:], MULT)
-            nc.sync.dma_start(rows[:, i, :], pages[i][:])
-        for i in range(SPLIT_PAGES):
-            scatter_half(1, i)
-            nc.sync.dma_start(rows[:, i, :], pages[i][:])
+        def add_bias(i, first, y_bank, offset=None):
+            ys[i, first] = placed(y_bank.shape, F32, "y%d%d" % (i, first), offset)
+            nc.scalar.activation(ys[i, first][:], y_bank[:], IDENTITY, bias=bias_cols[:, i : i + 1])
+
+        def scatter(i, first, count):
+            lists = place[:, first // GROUP : (first + count) // GROUP]
+            nc.vector.tensor_tensor(pages[i][:].indirect(lists), ys[i, first][:], weights[:, first : first + count], MULT)
+            if first + count == S:
+                nc.sync.dma_start(rows[:, i, :], pages[i][:])
+
+        for rp in range(R_PASSES):
+            for chunk in range(CHUNKS):
+                b_pass(rp, chunk, 0)
+        for chunk in range(CHUNKS):
+            b_pass(0, chunk, 1)
+            copy_b(0, chunk)
+        round_wa(0, 0, 0, BANK, on_gpsimd, AT_G00)
+        load_wd(0, AT_WA00)
+        for chunk in range(CHUNKS):
+            multiply_by_c(0, chunk, chunk)
+            b_pass(1, chunk, 1)
+        load_wd(1, AT_B0)
+        for chunk in range(2):
+            copy_b(1, chunk)
+        round_wa(1, 0, 0, UNIT, on_scalar, AT_G10)
+        round_wa(1, 0, UNIT, UNIT, on_gpsimd, None)
+        for chunk in range(2, CHUNKS):
+            copy_b(1, chunk)
+        multiply_by_c(1, 0, 4)
+        quantise_wa(0, 0, 0, BANK, AT_B[1, 0])
+        multiply_by_c(1, 1, 5)
+        quantise_wa(1, 0, UNIT, UNIT)
+        quantise_wa(1, 0, 0, UNIT)
+        multiply_by_c(1, 2, 5)
+        round_wa(0, 1, 0, BANK, on_gpsimd, AT_G10)
+        round_wa(1, 1, 0, UNIT, on_scalar, AT_G00)
+        make_h(0, 0, 0)
+        weights = placed([P, S], F32, "weights", at_bc(0, 0))
+        nc.sync.dma_start(weights[:], wgo)
+        make_h(0, 1, 1)
+        bias_cols = placed([P, PACK], F32, "bias_cols", at_bc(0, 1))
+        nc.sync.dma_start(bias_cols[:], bias.rearrange("(p i) -> p i", i=PACK))
+        turn_h(0, 0, 4)
+        nc.sync.dma_start(place[:], offs2)
+        make_h(0, 2, 2)
+        make_h(0, 3, 3)
+        turn_h(0, 1, 6)
+        round_wa(1, 1, UNIT, UNIT, on_vector, at_bc(0, 2))
+        quantise_wa(0, 1, 0, BANK, at_bc(0, 3))
+        quantise_wa(1, 1, 0, UNIT)
+        quantise_wa(1, 1, UNIT, UNIT)
+        multiply_by_c(1, 3, 4)
+        round_wd(0, 0, on_scalar, AT_H01)
+        quantise_h(0, 0)
+        round_wd(0, 2, on_scalar, AT_HT00)
+        make_h(1, 0, 7)
+        quantise_h(0, 1)
+        make_h(1, 1, 0)
+        turn_h(1, 0, 3)
+        quantise_wd(0, 0, 2)
+        make_h(1, 2, 1)
+        make_h(1, 3, 2)
+        turn_h(1, 1, 5)
+        round_wd(1, 0, on_vector, at_bc(1, 2))
+        quantise_h(1, 0)
+        quantise_wd(1, 0, 2)
+        first_half = [make_y(0, 6, 0, HALF), make_y(1, 7, 0, HALF)]
+        quantise_h(1, 1)
+        quantise_wd(0, 2, 2, AT_HT11)
+        for i in range(2):
+            add_bias(i, 0, first_half[i])
+        round_wd(1, 2, on_scalar, AT_HT00)
+        for i in range(2):
+            add_bias(i, HALF, make_y(i, i, HALF, HALF), [AT_PAGE2, AT_PAGE3][i])
+        for i in range(2):
+            scatter(i, 0, HALF)
+        quantise_wd(1, 2, 2)
+        for i in (2, 3):
+            add_bias(i, 0, make_y(i, i, 0, S))
+        for i in range(2):
+            scatter(i, HALF, HALF)
+            zero_page(i + 2, [AT_PAGE2, AT_PAGE3][i])
+        for i in (2, 3):
+            scatter(i, 0, S)

@@ -36,6 +36,9 @@ CHUNKS = S // P
 UNIT = BANK // 2
 WARM_UPS = 3
 
+B_BANK = {(0, 0): 0, (0, 1): 1, (0, 2): 2, (0, 3): 3, (1, 0): 4, (1, 1): 5, (1, 2): 6, (1, 3): 3}
+C_BANK = [7, 0, 1, 2]
+
 KIB = 1024
 AT_WA00 = 0
 AT_TS1 = 7 * KIB
@@ -61,6 +64,7 @@ AT_HT11 = 88 * KIB
 AT_HT = {(0, 0): AT_HT00, (1, 1): AT_HT11}
 AT_PAGE2 = 92 * KIB
 AT_PAGE3 = 96 * KIB
+AT_PICKED0 = 96 * KIB - 256
 
 
 def at_bc(rp, chunk):
@@ -156,11 +160,11 @@ def tile_list_segment_reassortment_fitness_kernel(
             for s in range(count):
                 v_chunk[g, first + s] = words[:, s * P : (s + 1) * P]
 
-        def zero_page(i, offset):
+        def zero_page(i, engine, offset):
             pages[i] = placed([P, T2], F32, "page%d" % i, offset)
-            nc.gpsimd.memset(pages[i][:], 0.0)
+            engine.memset(pages[i][:], 0.0)
 
-        pick_scales(0, None)
+        pick_scales(0, AT_PICKED0)
         load_table(1, AT_TAB1)
         pick_scales(1, AT_PICKED1)
         load_wc(0, AT_WC0)
@@ -184,8 +188,10 @@ def tile_list_segment_reassortment_fitness_kernel(
             pick_words(1, 2 * half, 2)
         load_wa(0, 1, AT_WA01)
         load_wa(1, 1, AT_WA11)
-        zero_page(0, AT_PAGE0)
-        zero_page(1, AT_PAGE1)
+        zero_page(2, nc.vector, AT_PAGE2)
+        zero_page(3, nc.vector, AT_PAGE3)
+        zero_page(0, nc.gpsimd, AT_PAGE0)
+        zero_page(1, nc.gpsimd, AT_PAGE1)
 
         def project(sums, chunk, g, words, scales, fmt):
             nc.tensor.matmul_mx(
@@ -210,13 +216,13 @@ def tile_list_segment_reassortment_fitness_kernel(
 
         def b_pass(rp, chunk, g):
             if g == 0:
-                b_bank[rp, chunk] = bank(CHUNKS * rp + chunk, [P, BANK], "b_bank")
+                b_bank[rp, chunk] = bank(B_BANK[rp, chunk], [P, BANK], "b_bank")
             project(b_bank[rp, chunk], chunk, g, wb_w[:, g, 2 * rp * BANK : 2 * (rp + 1) * BANK],
                     wb_sc[:, g, rp * BANK : (rp + 1) * BANK], E2M1)
 
-        def copy_b(rp, chunk):
+        def copy_b(rp, chunk, copy):
             b_sb[rp, chunk] = placed([P, BANK], F32, "b_sb%d%d" % (rp, chunk), AT_B[rp, chunk])
-            nc.scalar.copy(b_sb[rp, chunk][:], b_bank[rp, chunk][:])
+            copy(b_sb[rp, chunk][:], b_bank[rp, chunk][:])
 
         def multiply_by_c(rp, chunk, number):
             c_bank = bank(number, [P, BANK], "c_bank")
@@ -308,24 +314,25 @@ def tile_list_segment_reassortment_fitness_kernel(
             if first + count == S:
                 nc.sync.dma_start(rows[:, i, :], pages[i][:])
 
-        for rp in range(R_PASSES):
-            for chunk in range(CHUNKS):
-                b_pass(rp, chunk, 0)
+        for rp, chunk in list(B_BANK)[:-1]:
+            b_pass(rp, chunk, 0)
         for chunk in range(CHUNKS):
             b_pass(0, chunk, 1)
-            copy_b(0, chunk)
+            copy_b(0, chunk, on_vector if chunk == 0 else on_scalar)
         round_wa(0, 0, 0, BANK, on_gpsimd, AT_G00)
         load_wd(0, AT_WA00)
         for chunk in range(CHUNKS):
-            multiply_by_c(0, chunk, chunk)
+            multiply_by_c(0, chunk, C_BANK[chunk])
+            if chunk == CHUNKS - 1:
+                b_pass(1, chunk, 0)
             b_pass(1, chunk, 1)
         load_wd(1, AT_B0)
         for chunk in range(2):
-            copy_b(1, chunk)
+            copy_b(1, chunk, on_scalar)
         round_wa(1, 0, 0, UNIT, on_scalar, AT_G10)
         round_wa(1, 0, UNIT, UNIT, on_gpsimd, None)
         for chunk in range(2, CHUNKS):
-            copy_b(1, chunk)
+            copy_b(1, chunk, on_scalar)
         multiply_by_c(1, 0, 4)
         quantise_wa(0, 0, 0, BANK, AT_B[1, 0])
         multiply_by_c(1, 1, 5)
@@ -334,16 +341,16 @@ def tile_list_segment_reassortment_fitness_kernel(
         multiply_by_c(1, 2, 5)
         round_wa(0, 1, 0, BANK, on_gpsimd, AT_G10)
         round_wa(1, 1, 0, UNIT, on_scalar, AT_G00)
-        make_h(0, 0, 0)
+        make_h(0, 0, 7)
         weights = placed([P, S], F32, "weights", at_bc(0, 0))
         nc.sync.dma_start(weights[:], wgo)
-        make_h(0, 1, 1)
+        make_h(0, 1, 0)
         bias_cols = placed([P, PACK], F32, "bias_cols", at_bc(0, 1))
         nc.sync.dma_start(bias_cols[:], bias.rearrange("(p i) -> p i", i=PACK))
         turn_h(0, 0, 4)
         nc.sync.dma_start(place[:], offs2)
-        make_h(0, 2, 2)
-        make_h(0, 3, 3)
+        make_h(0, 2, 1)
+        make_h(0, 3, 2)
         turn_h(0, 1, 6)
         round_wa(1, 1, UNIT, UNIT, on_vector, at_bc(0, 2))
         quantise_wa(0, 1, 0, BANK, at_bc(0, 3))
@@ -353,32 +360,31 @@ def tile_list_segment_reassortment_fitness_kernel(
         round_wd(0, 0, on_scalar, AT_H01)
         quantise_h(0, 0)
         round_wd(0, 2, on_scalar, AT_HT00)
-        make_h(1, 0, 7)
+        make_h(1, 0, 3)
         quantise_h(0, 1)
-        make_h(1, 1, 0)
-        turn_h(1, 0, 3)
+        make_h(1, 1, 7)
+        turn_h(1, 0, 2)
         quantise_wd(0, 0, 2)
-        make_h(1, 2, 1)
-        make_h(1, 3, 2)
+        make_h(1, 2, 0)
+        make_h(1, 3, 1)
         turn_h(1, 1, 5)
         round_wd(1, 0, on_vector, at_bc(1, 2))
         quantise_h(1, 0)
         quantise_wd(1, 0, 2)
-        first_half = [make_y(0, 6, 0, HALF), make_y(1, 7, 0, HALF)]
+        first_half = [make_y(0, 6, 0, HALF), make_y(1, 3, 0, HALF)]
         quantise_h(1, 1)
         quantise_wd(0, 2, 2, AT_HT11)
         for i in range(2):
             add_bias(i, 0, first_half[i])
         round_wd(1, 2, on_scalar, AT_HT00)
         for i in range(2):
-            add_bias(i, HALF, make_y(i, i, HALF, HALF), [AT_PAGE2, AT_PAGE3][i])
+            add_bias(i, HALF, make_y(i, [7, 0][i], HALF, HALF))
         for i in range(2):
             scatter(i, 0, HALF)
         quantise_wd(1, 2, 2)
         for i in (2, 3):
-            add_bias(i, 0, make_y(i, i, 0, S))
+            add_bias(i, 0, make_y(i, i - 1, 0, S))
         for i in range(2):
             scatter(i, HALF, HALF)
-            zero_page(i + 2, [AT_PAGE2, AT_PAGE3][i])
         for i in (2, 3):
             scatter(i, 0, S)

@@ -61,7 +61,8 @@ AT_G10 = 80 * KIB
 AT_H01 = 84 * KIB
 AT_HT00 = 86 * KIB
 AT_HT11 = 88 * KIB
-AT_HT = {(0, 0): AT_HT00, (1, 1): AT_HT11}
+AT_HT01 = 102 * KIB
+AT_HT = {(0, 0): AT_HT00, (0, 1): AT_HT01, (1, 1): AT_HT11}
 AT_PAGE2 = 92 * KIB
 AT_PAGE3 = 96 * KIB
 AT_PICKED0 = 96 * KIB - 256
@@ -206,6 +207,9 @@ def tile_list_segment_reassortment_fitness_kernel(
 
         def on_gpsimd(dst, src):
             nc.gpsimd.tensor_scalar(dst.rearrange("p c t i -> p c i t"), src.rearrange("p c t i -> p c i t"), 1.0, 0.0, MULT, ADD)
+
+        def on_gpsimd_by_page(dst, src):
+            nc.gpsimd.tensor_scalar(dst.rearrange("p m t i -> p i m t"), src.rearrange("p m t i -> p i m t"), 1.0, 0.0, MULT, ADD)
 
         on_vector, on_scalar = nc.vector.tensor_copy, nc.scalar.copy
 
@@ -360,17 +364,17 @@ def tile_list_segment_reassortment_fitness_kernel(
         round_wd(0, 0, on_scalar, AT_H01)
         quantise_h(0, 0)
         round_wd(0, 2, on_scalar, AT_HT00)
-        make_h(1, 0, 3)
         quantise_h(0, 1)
+        round_wd(1, 0, on_gpsimd_by_page, AT_HT01)
+        make_h(1, 0, 3)
         make_h(1, 1, 7)
         turn_h(1, 0, 2)
-        quantise_wd(0, 0, 2)
         make_h(1, 2, 0)
         make_h(1, 3, 1)
         turn_h(1, 1, 5)
-        round_wd(1, 0, on_vector, at_bc(1, 2))
+        quantise_wd(0, 0, 2, at_bc(1, 2))
+        quantise_wd(1, 0, 2, at_bc(1, 3))
         quantise_h(1, 0)
-        quantise_wd(1, 0, 2)
         first_half = [make_y(0, 6, 0, HALF), make_y(1, 3, 0, HALF)]
         quantise_h(1, 1)
         quantise_wd(0, 2, 2, AT_HT11)

@@ -59,10 +59,9 @@ AT_BC = 60 * KIB
 AT_G00 = 76 * KIB
 AT_G10 = 80 * KIB
 AT_H01 = 84 * KIB
-AT_HT00 = 86 * KIB
 AT_HT11 = 88 * KIB
-AT_HT01 = 102 * KIB
-AT_HT = {(0, 0): AT_HT00, (0, 1): AT_HT01, (1, 1): AT_HT11}
+AT_HT0 = 102 * KIB
+AT_HT = {(1, 1): AT_HT11}
 AT_PAGE2 = 92 * KIB
 AT_PAGE3 = 96 * KIB
 AT_PICKED0 = 96 * KIB - 256
@@ -263,17 +262,22 @@ def tile_list_segment_reassortment_fitness_kernel(
             for s in range(2):
                 for u in range(2):
                     nc.tensor.transpose(turned[:, s, u, :], words[:, 2 * s * P + u : 2 * (s + 1) * P : 2], ident[:])
-            h_rj[rp, half] = placed([P, HALF * PACK], BF16, "hT%d%d" % (rp, half), AT_HT.get((rp, half)))
+            if (rp, half) == (0, 0):
+                h_rj[0] = placed([P, S * PACK], BF16, "hT0", AT_HT0)
+            if rp == 0:
+                h_rj[rp, half] = h_rj[0][:, half * HALF * PACK : (half + 1) * HALF * PACK]
+            else:
+                h_rj[rp, half] = placed([P, HALF * PACK], BF16, "hT%d%d" % (rp, half), AT_HT.get((rp, half)))[:]
             nc.scalar.copy(
-                h_rj[rp, half][:].bitcast(F32).rearrange("p (s j u) -> p s j u", s=2, u=2),
+                h_rj[rp, half].bitcast(F32).rearrange("p (s j u) -> p s j u", s=2, u=2),
                 turned[:].rearrange("p s u j -> p s j u"),
             )
 
-        def quantise_h(rp, half):
-            if half == 0:
-                h_q[rp] = (placed([P, S], U32, "h_w%d" % rp), placed([P, S], U8, "h_s%d" % rp))
-            cols = slice(half * HALF, (half + 1) * HALF)
-            quantise(h_q[rp][0][:, cols], h_q[rp][1][:, cols], h_rj[rp, half][:])
+        def quantise_h(rp, first, count, grouped):
+            if first == 0:
+                h_q[rp] = (placed([P, S], U32, "h_w%d" % rp, [at_bc(1, 2), None][rp]), placed([P, S], U8, "h_s%d" % rp))
+            cols = slice(first, first + count)
+            quantise(h_q[rp][0][:, cols], h_q[rp][1][:, cols], grouped)
 
         def round_wd(rp, first, copy, offset):
             wd_g[rp, first] = placed([P, 2, P * PACK], BF16, "wd_g%d%d" % (rp, first), offset)
@@ -344,7 +348,7 @@ def tile_list_segment_reassortment_fitness_kernel(
         quantise_wa(1, 0, 0, UNIT)
         multiply_by_c(1, 2, 5)
         round_wa(0, 1, 0, BANK, on_gpsimd, AT_G10)
-        round_wa(1, 1, 0, UNIT, on_scalar, AT_G00)
+        round_wa(1, 1, 0, BANK, on_scalar, AT_G00)
         make_h(0, 0, 7)
         weights = placed([P, S], F32, "weights", at_bc(0, 0))
         nc.sync.dma_start(weights[:], wgo)
@@ -356,31 +360,28 @@ def tile_list_segment_reassortment_fitness_kernel(
         make_h(0, 2, 1)
         make_h(0, 3, 2)
         turn_h(0, 1, 6)
-        round_wa(1, 1, UNIT, UNIT, on_vector, at_bc(0, 2))
-        quantise_wa(0, 1, 0, BANK, at_bc(0, 3))
-        quantise_wa(1, 1, 0, UNIT)
-        quantise_wa(1, 1, UNIT, UNIT)
-        multiply_by_c(1, 3, 4)
-        round_wd(0, 0, on_scalar, AT_H01)
-        quantise_h(0, 0)
-        round_wd(0, 2, on_scalar, AT_HT00)
-        quantise_h(0, 1)
-        round_wd(1, 0, on_gpsimd_by_page, AT_HT01)
+        quantise_wa(0, 1, 0, BANK, at_bc(0, 2))
+        multiply_by_c(1, 3, 5)
+        quantise_wa(1, 1, 0, BANK, at_bc(0, 3))
+        round_wd(0, 0, on_scalar, AT_H01 - KIB)
+        round_wd(0, 2, on_scalar, AT_H01 + KIB)
+        round_wd(1, 0, on_gpsimd_by_page, AT_G00)
         make_h(1, 0, 3)
         make_h(1, 1, 7)
         turn_h(1, 0, 2)
         make_h(1, 2, 0)
         make_h(1, 3, 1)
-        turn_h(1, 1, 5)
-        quantise_wd(0, 0, 2, at_bc(1, 2))
-        quantise_wd(1, 0, 2, at_bc(1, 3))
-        quantise_h(1, 0)
+        turn_h(1, 1, 4)
+        quantise_h(0, 0, S, h_rj[0][:])
+        quantise_wd(0, 0, 2, at_bc(1, 3))
+        quantise_wd(1, 0, 2, AT_HT0)
+        quantise_h(1, 0, HALF, h_rj[1, 0])
         first_half = [make_y(0, 6, 0, HALF), make_y(1, 3, 0, HALF)]
-        quantise_h(1, 1)
+        quantise_h(1, HALF, HALF, h_rj[1, 1])
         quantise_wd(0, 2, 2, AT_HT11)
         for i in range(2):
             add_bias(i, 0, first_half[i])
-        round_wd(1, 2, on_scalar, AT_HT00)
+        round_wd(1, 2, on_scalar, AT_H01 + KIB)
         for i in range(2):
             add_bias(i, HALF, make_y(i, [7, 0][i], HALF, HALF))
         for i in range(2):

@@ -34,7 +34,6 @@ HALVES = 2
 HALF = S // HALVES
 CHUNKS = S // P
 UNIT = BANK // 2
-WARM_UPS = 3
 
 B_BANK = {(0, 0): 0, (0, 1): 1, (0, 2): 2, (0, 3): 3, (1, 0): 4, (1, 1): 5, (1, 2): 6, (1, 3): 3}
 C_BANK = [7, 0, 1, 2]
@@ -169,17 +168,6 @@ def tile_list_segment_reassortment_fitness_kernel(
         pick_scales(1, AT_PICKED1)
         load_wc(0, AT_WC0)
         load_wa(0, 0, AT_WA00)
-        unread = bank(7, [P, BANK], "unread")
-        for n in range(WARM_UPS):
-            nc.tensor.matmul_mx(
-                out=unread[:],
-                lhsT=tab[0][:, 0:P].bitcast(E4M3),
-                lhsT_scale=picked[0][:, 0:P],
-                rhs=tab[0][:, 0:BANK].bitcast(E4M3),
-                rhs_scale=picked[0][:],
-                start=True,
-                stop=True,
-            )
         for half in range(HALVES):
             pick_words(0, 2 * half, 2)
         load_wc(1, AT_WC1)

@@ -267,18 +267,18 @@ def tile_list_segment_reassortment_fitness_kernel(
             cols = slice(first, first + count)
             quantise(h_q[rp][0][:, cols], h_q[rp][1][:, cols], grouped)
 
-        def round_wd(rp, first, copy, offset):
-            wd_g[rp, first] = placed([P, 2, P * PACK], BF16, "wd_g%d%d" % (rp, first), offset)
+        def round_wd(rp, first, count, copy, offset):
+            wd_g[rp, first] = placed([P, count, P * PACK], BF16, "wd_g%d%d" % (rp, first), offset)
             copy(
                 wd_g[rp, first][:].rearrange("p i (m t) -> p m t i", t=PACK),
-                wd_raw[rp][:].rearrange("p t (m i) -> p m t i", i=PACK)[:, :, :, first : first + 2],
+                wd_raw[rp][:].rearrange("p t (m i) -> p m t i", i=PACK)[:, :, :, first : first + count],
             )
 
         def quantise_wd(rp, first, count, offset=None):
             words = placed([P, count * P], U32, "wd_w%d%d" % (rp, first), offset)
             scales = placed([P, count * P], U8, "wd_s%d%d" % (rp, first))
-            pair = first - first % 2
-            grouped = wd_g[rp, pair][:, first - pair : first - pair + count, :]
+            begin = first if (rp, first) in wd_g else 0
+            grouped = wd_g[rp, begin][:, first - begin : first - begin + count, :]
             quantise(words[:], scales[:], grouped.rearrange("p i c -> p (i c)"))
             for i in range(count):
                 wd_q[rp, first + i] = (words[:, i * P : (i + 1) * P], scales[:, i * P : (i + 1) * P])
@@ -351,25 +351,25 @@ def tile_list_segment_reassortment_fitness_kernel(
         quantise_wa(0, 1, 0, BANK, at_bc(0, 2))
         multiply_by_c(1, 3, 5)
         quantise_wa(1, 1, 0, BANK, at_bc(0, 3))
-        round_wd(0, 0, on_scalar, AT_H01 - KIB)
-        round_wd(0, 2, on_scalar, AT_H01 + KIB)
-        round_wd(1, 0, on_gpsimd_by_page, AT_G00)
+        round_wd(0, 0, PACK, on_scalar, AT_H01)
+        round_wd(1, 0, 2, on_gpsimd_by_page, AT_G00)
         make_h(1, 0, 3)
         make_h(1, 1, 7)
         turn_h(1, 0, 2)
         make_h(1, 2, 0)
         make_h(1, 3, 1)
         turn_h(1, 1, 4)
-        quantise_h(0, 0, S, h_rj[0][:])
+        quantise_h(0, 0, HALF, h_rj[0, 0])
         quantise_wd(0, 0, 2, at_bc(1, 3))
-        quantise_wd(1, 0, 2, AT_HT0)
+        quantise_wd(1, 0, 2, at_bc(1, 3) + KIB)
         quantise_h(1, 0, HALF, h_rj[1, 0])
         first_half = [make_y(0, 6, 0, HALF), make_y(1, 3, 0, HALF)]
+        quantise_h(0, HALF, HALF, h_rj[0, 1])
         quantise_h(1, HALF, HALF, h_rj[1, 1])
         quantise_wd(0, 2, 2, AT_HT11)
         for i in range(2):
             add_bias(i, 0, first_half[i])
-        round_wd(1, 2, on_scalar, AT_H01 + KIB)
+        round_wd(1, 2, 2, on_scalar, AT_H01)
         for i in range(2):
             add_bias(i, HALF, make_y(i, [7, 0][i], HALF, HALF))
         for i in range(2):

@@ -59,15 +59,15 @@ AT_G00 = 76 * KIB
 AT_G10 = 80 * KIB
 AT_H01 = 84 * KIB
 AT_HT11 = 88 * KIB
-AT_HT0 = 102 * KIB
-AT_HT = {(1, 1): AT_HT11}
+AT_FIRST_R = 102 * KIB
+AT_SECOND_W = 110 * KIB
 AT_PAGE2 = 92 * KIB
 AT_PAGE3 = 96 * KIB
 AT_PICKED0 = 96 * KIB - 256
 
 
 def at_bc(rp, chunk):
-    return AT_BC + 2 * KIB * (CHUNKS * rp + chunk)
+    return AT_SECOND_W if (rp, chunk) == (1, 2) else AT_BC + 2 * KIB * (CHUNKS * rp + chunk)
 
 
 def tile_list_segment_reassortment_fitness_kernel(
@@ -238,50 +238,34 @@ def tile_list_segment_reassortment_fitness_kernel(
         def make_h(rp, chunk, number):
             half, s = divmod(chunk, 2)
             if s == 0:
-                h_jr[rp, half] = placed([P, 2, BANK], BF16, "h%d%d" % (rp, half), AT_H01 if (rp, half) == (0, 1) else None)
+                h_jr[rp, half] = placed([P, 2, BANK], BF16, "h%d%d" % (rp, half), None)
             a_bank = bank(number, [P, BANK], "a_bank")
             for g in range(K_PASSES):
                 project(a_bank, chunk, g, wa_q[g, rp][0][:], wa_q[g, rp][1][:], E4M3)
             nc.vector.tensor_tensor(h_jr[rp, half][:, s, :], a_bank[:], bc[rp, chunk][:], MULT)
 
-        def turn_h(rp, half, number):
+        def turn_h(rp, half, number, grouped):
             words = h_jr[rp, half][:].rearrange("p s r -> p (s r)").bitcast(F32)
             turned = bank(number, [P, 2, 2, P], "turned")
             for s in range(2):
                 for u in range(2):
                     nc.tensor.transpose(turned[:, s, u, :], words[:, 2 * s * P + u : 2 * (s + 1) * P : 2], ident[:])
-            if (rp, half) == (0, 0):
-                h_rj[0] = placed([P, S * PACK], BF16, "hT0", AT_HT0)
-            if rp == 0:
-                h_rj[rp, half] = h_rj[0][:, half * HALF * PACK : (half + 1) * HALF * PACK]
-            else:
-                h_rj[rp, half] = placed([P, HALF * PACK], BF16, "hT%d%d" % (rp, half), AT_HT.get((rp, half)))[:]
             nc.scalar.copy(
-                h_rj[rp, half].bitcast(F32).rearrange("p (s j u) -> p s j u", s=2, u=2),
+                grouped.bitcast(F32).rearrange("p (s j u) -> p s j u", s=2, u=2),
                 turned[:].rearrange("p s u j -> p s j u"),
             )
 
-        def quantise_h(rp, first, count, grouped):
-            if first == 0:
-                h_q[rp] = (placed([P, S], U32, "h_w%d" % rp, [at_bc(1, 2), None][rp]), placed([P, S], U8, "h_s%d" % rp))
-            cols = slice(first, first + count)
-            quantise(h_q[rp][0][:, cols], h_q[rp][1][:, cols], grouped)
-
-        def round_wd(rp, first, count, copy, offset):
-            wd_g[rp, first] = placed([P, count, P * PACK], BF16, "wd_g%d%d" % (rp, first), offset)
+        def round_pair(rp, first, copy, grouped):
             copy(
-                wd_g[rp, first][:].rearrange("p i (m t) -> p m t i", t=PACK),
-                wd_raw[rp][:].rearrange("p t (m i) -> p m t i", i=PACK)[:, :, :, first : first + count],
+                grouped.rearrange("p (i m t) -> p m t i", i=2, t=PACK),
+                wd_raw[rp][:].rearrange("p t (m i) -> p m t i", i=PACK)[:, :, :, first : first + 2],
             )
 
-        def quantise_wd(rp, first, count, offset=None):
-            words = placed([P, count * P], U32, "wd_w%d%d" % (rp, first), offset)
-            scales = placed([P, count * P], U8, "wd_s%d%d" % (rp, first))
-            begin = first if (rp, first) in wd_g else 0
-            grouped = wd_g[rp, begin][:, first - begin : first - begin + count, :]
-            quantise(words[:], scales[:], grouped.rearrange("p i c -> p (i c)"))
-            for i in range(count):
-                wd_q[rp, first + i] = (words[:, i * P : (i + 1) * P], scales[:, i * P : (i + 1) * P])
+        def operand(codes, first, count):
+            return codes[0][:, first : first + count], codes[1][:, first : first + count]
+
+        def quantise_part(codes, first, count, grouped):
+            quantise(*operand(codes, first, count), grouped)
 
         rows = out.rearrange("(p i) t -> p i t", i=PACK)
         ys = {}
@@ -343,38 +327,52 @@ def tile_list_segment_reassortment_fitness_kernel(
         make_h(0, 1, 0)
         bias_cols = placed([P, PACK], F32, "bias_cols", at_bc(0, 1))
         nc.sync.dma_start(bias_cols[:], bias.rearrange("(p i) -> p i", i=PACK))
-        turn_h(0, 0, 4)
+        first_r = placed([P, 4, HALF * PACK], BF16, "first_r", AT_FIRST_R)
+        turn_h(0, 0, 4, first_r[:, 1, :])
         nc.sync.dma_start(place[:], offs2)
         make_h(0, 2, 1)
         make_h(0, 3, 2)
-        turn_h(0, 1, 6)
+        turn_h(0, 1, 6, first_r[:, 2, :])
         quantise_wa(0, 1, 0, BANK, at_bc(0, 2))
         multiply_by_c(1, 3, 5)
         quantise_wa(1, 1, 0, BANK, at_bc(0, 3))
-        round_wd(0, 0, PACK, on_scalar, AT_H01)
-        round_wd(1, 0, 2, on_gpsimd_by_page, AT_G00)
+        nc.scalar.copy(
+            first_r[:, 0:4:3, :].rearrange("p j (k m t) -> p m t j k", k=2, t=PACK),
+            wd_raw[0][:].rearrange("p t (m j k) -> p m t j k", j=2, k=2),
+        )
+        second_r = placed([P, 2, HALF * PACK], BF16, "second_r", AT_G00)
+        round_pair(1, 0, on_gpsimd_by_page, second_r[:, 0, :])
         make_h(1, 0, 3)
         make_h(1, 1, 7)
-        turn_h(1, 0, 2)
+        turn_h(1, 0, 2, second_r[:, 1, :])
         make_h(1, 2, 0)
-        make_h(1, 3, 1)
-        turn_h(1, 1, 4)
-        quantise_h(0, 0, HALF, h_rj[0, 0])
-        quantise_wd(0, 0, 2, at_bc(1, 3))
-        quantise_wd(1, 0, 2, at_bc(1, 3) + KIB)
-        quantise_h(1, 0, HALF, h_rj[1, 0])
+        first_q = (placed([P, 4 * HALF], U32, "first_w", at_bc(1, 0)), placed([P, 4 * HALF], U8, "first_s"))
+        quantise_part(first_q, 0, 2 * HALF, first_r[:, 0:2, :].rearrange("p a c -> p (a c)"))
+        second_q = (placed([P, 3 * HALF], U32, "second_w", AT_SECOND_W), placed([P, 3 * HALF], U8, "second_s"))
+        quantise_part(second_q, 0, 2 * HALF, second_r[:].rearrange("p a c -> p (a c)"))
+        h_q[0], h_q[1] = operand(first_q, HALF, S), operand(second_q, HALF, S)
+        for i in range(2):
+            wd_q[0, i] = operand(first_q, i * P, P)
+            wd_q[0, 2 + i] = operand(first_q, 3 * HALF + i * P, P)
+            wd_q[1, i] = operand(second_q, i * P, P)
         first_half = [make_y(0, 6, 0, HALF), make_y(1, 3, 0, HALF)]
-        quantise_h(0, HALF, HALF, h_rj[0, 1])
-        quantise_h(1, HALF, HALF, h_rj[1, 1])
-        quantise_wd(0, 2, 2, AT_HT11)
+        make_h(1, 3, 1)
+        last_h = placed([P, HALF * PACK], BF16, "last_h")
         for i in range(2):
             add_bias(i, 0, first_half[i])
-        round_wd(1, 2, 2, on_scalar, AT_H01)
+        turn_h(1, 1, 4, last_h[:])
+        quantise_part(first_q, 2 * HALF, 2 * HALF, first_r[:, 2:4, :].rearrange("p a c -> p (a c)"))
+        scatter(0, 0, HALF)
+        quantise_part(second_q, 2 * HALF, HALF, last_h[:])
+        last_pair = placed([P, HALF * PACK], BF16, "last_pair", AT_FIRST_R)
+        round_pair(1, 2, on_scalar, last_pair[:])
         for i in range(2):
             add_bias(i, HALF, make_y(i, [7, 0][i], HALF, HALF))
+        scatter(1, 0, HALF)
+        last_q = (placed([P, HALF], U32, "last_w"), placed([P, HALF], U8, "last_s"))
+        quantise_part(last_q, 0, HALF, last_pair[:])
         for i in range(2):
-            scatter(i, 0, HALF)
-        quantise_wd(1, 2, 2)
+            wd_q[1, 2 + i] = operand(last_q, i * P, P)
         for i in (2, 3):
             add_bias(i, 0, make_y(i, i - 1, 0, S))
         for i in range(2):

from contextlib import ExitStack

import concourse.mybir as mybir

K, H, N, T, S, T2 = 1024, 1024, 512, 2048, 512, 1024
FLOPS = 2 * S * (3 * K * H + H * N)

F32 = mybir.dt.float32
BF16 = mybir.dt.bfloat16
I32 = mybir.dt.int32
U32 = mybir.dt.uint32
U16 = mybir.dt.uint16
U8 = mybir.dt.uint8
E4M3 = mybir.dt.float8_e4m3fn_x4
E2M1 = mybir.dt.float4_e2m1fn_x4
MULT = mybir.AluOpType.mult
ADD = mybir.AluOpType.add
IDENTITY = mybir.ActivationFunctionType.Identity
ABS = mybir.ActivationFunctionType.Abs
RELU = mybir.ActivationFunctionType.Relu

P = 128
PACK = 4
PASS = P * PACK
BANK = 512
QUAD = 32
QUADS = P // QUAD
ROWS = 4
BLOCK = 8
GROUP = 16
K_PASSES = K // PASS
R_PASSES = H // PASS
HALVES = 2
HALF = S // HALVES
CHUNKS = S // P
UNIT = BANK // 2

B_BANK = {(0, 0): 0, (0, 1): 1, (0, 2): 2, (0, 3): 3, (1, 0): 4, (1, 1): 5, (1, 2): 6, (1, 3): 3}
C_BANK = [7, 0, 1, 2]

KIB = 1024
AT_WA00 = 0
AT_TS1 = 7 * KIB
AT_WC0 = 8 * KIB
AT_WC1 = 12 * KIB
AT_TAB0 = 14 * KIB
AT_WA10 = 16 * KIB
AT_WA01 = 24 * KIB
AT_TAB1 = 32 * KIB - 256
AT_PAGE0 = 32 * KIB
AT_PAGE1 = 36 * KIB
AT_WA11 = 40 * KIB
AT_PICKED1 = 48 * KIB - 512
AT_B0 = 48 * KIB
AT_B = {(0, 0): AT_B0, (0, 1): AT_B0 + 2 * KIB, (0, 2): AT_B0 + 4 * KIB, (0, 3): AT_B0 + 6 * KIB,
        (1, 0): 56 * KIB, (1, 1): 58 * KIB, (1, 2): AT_WA10, (1, 3): AT_WA10 + 2 * KIB}
AT_BC = 60 * KIB
AT_G00 = 76 * KIB
AT_G10 = 80 * KIB
AT_H01 = 84 * KIB
AT_HT11 = 88 * KIB
AT_FIRST_R = 102 * KIB
AT_SECOND_W = 110 * KIB
AT_PAGE2 = 92 * KIB
AT_PAGE3 = 96 * KIB
AT_PICKED0 = 96 * KIB - 256


def at_bc(rp, chunk):
    return AT_SECOND_W if (rp, chunk) == (1, 2) else AT_BC + 2 * KIB * (CHUNKS * rp + chunk)


def tile_list_segment_reassortment_fitness_kernel(
    tc, tab_words, tab_scales, offs, wa, wb_words, wb_scales, wc_words, wc_scales, wd, bias, offs2, wgo, out
):
    nc = tc.nc

    with ExitStack() as ctx:
        keep = ctx.enter_context(tc.tile_pool(name="keep", bufs=1))
        stage = ctx.enter_context(tc.tile_pool(name="stage", bufs=1))
        psum = ctx.enter_context(tc.psum_pool(name="psum", bufs=1))

        def placed(shape, dtype, name, offset=None):
            if offset is None:
                return keep.tile(shape, dtype, name=name, align_bytes=256)
            return stage.tile(shape, dtype, name=name, align_bytes=256, offset=offset)

        def bank(number, shape, name):
            return psum.tile(shape, F32, name=name, tag="bank%d" % number)

        pick = placed([P, S // GROUP], U16, "pick")
        place = placed([P, S // GROUP], U16, "place")
        nc.sync.dma_start(pick[:], offs)

        def load_scale_rows(queues, plane, scales):
            by_row = scales.rearrange("g (d x) c -> x d g c", x=ROWS)
            for x, queue in enumerate(queues):
                queue.dma_start(plane[:].bitcast(I32)[x:P:QUAD], by_row[x].bitcast(I32))

        wb_sc = placed([P, K_PASSES, H], U8, "wb_sc")
        wc_sc = placed([P, K_PASSES, H], U8, "wc_sc")
        ts = [placed([P, T], U8, "ts0", AT_TAB1), placed([P, T], U8, "ts1", AT_TS1)]
        load_scale_rows([nc.sync, nc.scalar, nc.scalar, nc.scalar], wb_sc, wb_scales)
        for g, engine in enumerate((nc.gpsimd, nc.vector)):
            engine.memset(ts[g][:].bitcast(I32), 0)
            nc.sync.dma_start(ts[g][:].bitcast(I32)[0:P:BLOCK], tab_scales[g].bitcast(I32))
        load_scale_rows([nc.gpsimd] * ROWS, wc_sc, wc_scales)

        tab, wc_w, wa_raw, wd_raw = {}, {}, {}, {}

        def load_table(g, offset):
            tab[g] = placed([P, T], I32, "tab%d" % g, offset)
            nc.sync.dma_start(tab[g][:], tab_words[g].rearrange("p t i -> p (t i)").bitcast(I32))

        def load_wc(rp, offset):
            wc_w[rp] = placed([P, K_PASSES, BANK], I32, "wc_w%d" % rp, offset)
            cols = wc_words[:, :, rp * BANK : (rp + 1) * BANK, :]
            nc.sync.dma_start(wc_w[rp][:], cols.rearrange("g p c i -> p g (c i)").bitcast(I32))

        def load_wa(g, rp, offset):
            wa_raw[g, rp] = placed([P, PACK, BANK], F32, "wa_raw%d%d" % (g, rp), offset)
            rows = wa[g * PASS : (g + 1) * PASS, rp * BANK : (rp + 1) * BANK]
            nc.sync.dma_start(wa_raw[g, rp][:], rows.rearrange("(p t) c -> p t c", t=PACK))

        def load_wd(rp, offset):
            wd_raw[rp] = placed([P, PACK, N], F32, "wd_raw%d" % rp, offset)
            nc.sync.dma_start(wd_raw[rp][:], wd[rp * PASS : (rp + 1) * PASS, :].rearrange("(p t) n -> p t n", t=PACK))

        load_table(0, AT_TAB0)
        wb_w = placed([P, K_PASSES, 2 * H], U8, "wb_w")
        nc.sync.dma_start(wb_w[:].bitcast(I32), wb_words.rearrange("g p c -> p g c").bitcast(I32))

        ones = placed([P, P], F32, "ones")
        column = placed([P, P], F32, "column")
        row = placed([P, P], F32, "row")
        apart = placed([P, P], F32, "apart")
        ident = placed([P, P], F32, "ident")
        nc.vector.memset(ones[:], 1.0)
        nc.vector.tensor_tensor_scan(column[:], ones[:], ones[:], 0.0, MULT, ADD)
        nc.vector.transpose(row[:], column[:])
        for d in range(QUADS):
            part = slice(QUAD * d, QUAD * (d + 1))
            nc.scalar.activation(apart[part, :], column[part, :], ABS, bias=row[part, QUAD * d : QUAD * d + 1], scale=-1.0)
        nc.scalar.activation(ident[:], apart[:], RELU, bias=1.0, scale=-1.0)

        picked, v_scales, v_chunk, pages = {}, {}, {}, {}

        def pick_scales(g, offset):
            picked[g] = placed([P, S], U8, "picked%d" % g, offset)
            nc.vector.tensor_copy(picked[g][:], ts[g][:].indirect(pick[:]))
            v_scales[g] = placed([P, S], U8, "v_scales%d" % g)
            for x in range(ROWS):
                nc.sync.dma_start(v_scales[g][:].bitcast(I32)[x:P:QUAD], picked[g][:].bitcast(I32)[BLOCK * x : P : QUAD])

        def pick_words(g, first, count):
            words = placed([P, count * P], U32, "v_words%d%d" % (g, first))
            lists = pick[:, first * P // GROUP : (first + count) * P // GROUP]
            nc.vector.tensor_copy(words[:], tab[g][:].bitcast(U32).indirect(lists))
            for s in range(count):
                v_chunk[g, first + s] = words[:, s * P : (s + 1) * P]

        def zero_page(i, engine, offset):
            pages[i] = placed([P, T2], F32, "page%d" % i, offset)
            engine.memset(pages[i][:], 0.0)

        pick_scales(0, AT_PICKED0)
        load_table(1, AT_TAB1)
        pick_scales(1, AT_PICKED1)
        load_wc(0, AT_WC0)
        load_wa(0, 0, AT_WA00)
        for half in range(HALVES):
            pick_words(0, 2 * half, 2)
        load_wc(1, AT_WC1)
        load_wa(1, 0, AT_WA10)
        for half in range(HALVES):
            pick_words(1, 2 * half, 2)
        load_wa(0, 1, AT_WA01)
        load_wa(1, 1, AT_WA11)
        zero_page(2, nc.vector, AT_PAGE2)
        zero_page(3, nc.vector, AT_PAGE3)
        zero_page(0, nc.gpsimd, AT_PAGE0)
        zero_page(1, nc.gpsimd, AT_PAGE1)

        def project(sums, chunk, g, words, scales, fmt):
            nc.tensor.matmul_mx(
                out=sums[:],
                lhsT=v_chunk[g, chunk].bitcast(E4M3),
                lhsT_scale=v_scales[g][:, chunk * P : (chunk + 1) * P],
                rhs=words.bitcast(fmt),
                rhs_scale=scales,
                start=(g == 0),
                stop=(g == K_PASSES - 1),
            )

        def on_gpsimd(dst, src):
            nc.gpsimd.tensor_scalar(dst.rearrange("p c t i -> p c i t"), src.rearrange("p c t i -> p c i t"), 1.0, 0.0, MULT, ADD)

        def on_gpsimd_by_page(dst, src):
            nc.gpsimd.tensor_scalar(dst.rearrange("p m t i -> p i m t"), src.rearrange("p m t i -> p i m t"), 1.0, 0.0, MULT, ADD)

        on_vector, on_scalar = nc.vector.tensor_copy, nc.scalar.copy

        def quantise(words, scales, grouped):
            nc.vector.quantize_mx(out=words.bitcast(E4M3), scales=scales, in_=grouped)

        b_bank, b_sb, bc, wa_g, wa_q, h_jr, h_rj, h_q, wd_g, wd_q = {}, {}, {}, {}, {}, {}, {}, {}, {}, {}

        def b_pass(rp, chunk, g):
            if g == 0:
                b_bank[rp, chunk] = bank(B_BANK[rp, chunk], [P, BANK], "b_bank")
            project(b_bank[rp, chunk], chunk, g, wb_w[:, g, 2 * rp * BANK : 2 * (rp + 1) * BANK],
                    wb_sc[:, g, rp * BANK : (rp + 1) * BANK], E2M1)

        def copy_b(rp, chunk, copy):
            b_sb[rp, chunk] = placed([P, BANK], F32, "b_sb%d%d" % (rp, chunk), AT_B[rp, chunk])
            copy(b_sb[rp, chunk][:], b_bank[rp, chunk][:])

        def multiply_by_c(rp, chunk, number):
            c_bank = bank(number, [P, BANK], "c_bank")
            for g in range(K_PASSES):
                project(c_bank, chunk, g, wc_w[rp][:, g, :], wc_sc[:, g, rp * BANK : (rp + 1) * BANK], E4M3)
            bc[rp, chunk] = placed([P, BANK], F32, "bc%d%d" % (rp, chunk), at_bc(rp, chunk))
            nc.vector.tensor_tensor(bc[rp, chunk][:], c_bank[:], b_sb[rp, chunk][:], MULT)

        def round_wa(g, rp, first, count, copy, offset):
            wa_g[g, rp, first] = placed([P, count * PACK], BF16, "wa_g%d%d%d" % (g, rp, first), offset)
            copy(
                wa_g[g, rp, first][:].rearrange("p (c i t) -> p c t i", i=4, t=PACK),
                wa_raw[g, rp][:, :, first : first + count].rearrange("p t (c i) -> p c t i", i=4),
            )

        def quantise_wa(g, rp, first, count, offset=None):
            if (g, rp) not in wa_q:
                wa_q[g, rp] = (placed([P, BANK], U32, "wa_w%d%d" % (g, rp), offset), placed([P, BANK], U8, "wa_s%d%d" % (g, rp)))
            cols = slice(first, first + count)
            quantise(wa_q[g, rp][0][:, cols], wa_q[g, rp][1][:, cols], wa_g[g, rp, first][:])

        def make_h(rp, chunk, number):
            half, s = divmod(chunk, 2)
            if s == 0:
                h_jr[rp, half] = placed([P, 2, BANK], BF16, "h%d%d" % (rp, half), None)
            a_bank = bank(number, [P, BANK], "a_bank")
            for g in range(K_PASSES):
                project(a_bank, chunk, g, wa_q[g, rp][0][:], wa_q[g, rp][1][:], E4M3)
            nc.vector.tensor_tensor(h_jr[rp, half][:, s, :], a_bank[:], bc[rp, chunk][:], MULT)

        def turn_h(rp, half, number, grouped):
            words = h_jr[rp, half][:].rearrange("p s r -> p (s r)").bitcast(F32)
            turned = bank(number, [P, 2, 2, P], "turned")
            for s in range(2):
                for u in range(2):
                    nc.tensor.transpose(turned[:, s, u, :], words[:, 2 * s * P + u : 2 * (s + 1) * P : 2], ident[:])
            nc.scalar.copy(
                grouped.bitcast(F32).rearrange("p (s j u) -> p s j u", s=2, u=2),
                turned[:].rearrange("p s u j -> p s j u"),
            )

        def round_pair(rp, first, copy, grouped):
            copy(
                grouped.rearrange("p (i m t) -> p m t i", i=2, t=PACK),
                wd_raw[rp][:].rearrange("p t (m i) -> p m t i", i=PACK)[:, :, :, first : first + 2],
            )

        def operand(codes, first, count):
            return codes[0][:, first : first + count], codes[1][:, first : first + count]

        def quantise_part(codes, first, count, grouped):
            quantise(*operand(codes, first, count), grouped)

        rows = out.rearrange("(p i) t -> p i t", i=PACK)
        ys = {}

        def make_y(i, number, first, count):
            y_bank = bank(number, [P, count], "y_bank")
            for rp in range(R_PASSES):
                nc.tensor.matmul_mx(
                    out=y_bank[:],
                    lhsT=wd_q[rp, i][0].bitcast(E4M3),
                    lhsT_scale=wd_q[rp, i][1],
                    rhs=h_q[rp][0][:, first : first + count].bitcast(E4M3),
                    rhs_scale=h_q[rp][1][:, first : first + count],
                    start=(rp == 0),
                    stop=(rp == R_PASSES - 1),
                )
            return y_bank

        def add_bias(i, first, y_bank, offset=None):
            ys[i, first] = placed(y_bank.shape, F32, "y%d%d" % (i, first), offset)
            nc.scalar.activation(ys[i, first][:], y_bank[:], IDENTITY, bias=bias_cols[:, i : i + 1])

        def scatter(i, first, count):
            lists = place[:, first // GROUP : (first + count) // GROUP]
            nc.vector.tensor_tensor(pages[i][:].indirect(lists), ys[i, first][:], weights[:, first : first + count], MULT)
            if first + count == S:
                nc.sync.dma_start(rows[:, i, :], pages[i][:])

        for rp, chunk in list(B_BANK)[:-1]:
            b_pass(rp, chunk, 0)
        for chunk in range(CHUNKS):
            b_pass(0, chunk, 1)
            copy_b(0, chunk, on_vector if chunk == 0 else on_scalar)
        round_wa(0, 0, 0, BANK, on_gpsimd, AT_G00)
        load_wd(0, AT_WA00)
        for chunk in range(CHUNKS):
            multiply_by_c(0, chunk, C_BANK[chunk])
            if chunk == CHUNKS - 1:
                b_pass(1, chunk, 0)
            b_pass(1, chunk, 1)
        load_wd(1, AT_B0)
        for chunk in range(2):
            copy_b(1, chunk, on_scalar)
        round_wa(1, 0, 0, UNIT, on_scalar, AT_G10)
        round_wa(1, 0, UNIT, UNIT, on_gpsimd, None)
        for chunk in range(2, CHUNKS):
            copy_b(1, chunk, on_scalar)
        multiply_by_c(1, 0, 4)
        quantise_wa(0, 0, 0, BANK, AT_B[1, 0])
        multiply_by_c(1, 1, 5)
        quantise_wa(1, 0, UNIT, UNIT)
        quantise_wa(1, 0, 0, UNIT)
        multiply_by_c(1, 2, 5)
        round_wa(0, 1, 0, BANK, on_gpsimd, AT_G10)
        round_wa(1, 1, 0, BANK, on_scalar, AT_G00)
        make_h(0, 0, 7)
        weights = placed([P, S], F32, "weights", at_bc(0, 0))
        nc.sync.dma_start(weights[:], wgo)
        make_h(0, 1, 0)
        bias_cols = placed([P, PACK], F32, "bias_cols", at_bc(0, 1))
        nc.sync.dma_start(bias_cols[:], bias.rearrange("(p i) -> p i", i=PACK))
        first_r = placed([P, 4, HALF * PACK], BF16, "first_r", AT_FIRST_R)
        turn_h(0, 0, 4, first_r[:, 1, :])
        nc.sync.dma_start(place[:], offs2)
        make_h(0, 2, 1)
        make_h(0, 3, 2)
        turn_h(0, 1, 6, first_r[:, 2, :])
        quantise_wa(0, 1, 0, BANK, at_bc(0, 2))
        multiply_by_c(1, 3, 5)
        quantise_wa(1, 1, 0, BANK, at_bc(0, 3))
        nc.scalar.copy(
            first_r[:, 0:4:3, :].rearrange("p j (k m t) -> p m t j k", k=2, t=PACK),
            wd_raw[0][:].rearrange("p t (m j k) -> p m t j k", j=2, k=2),
        )
        second_r = placed([P, 2, HALF * PACK], BF16, "second_r", AT_G00)
        round_pair(1, 0, on_gpsimd_by_page, second_r[:, 0, :])
        make_h(1, 0, 3)
        make_h(1, 1, 7)
        turn_h(1, 0, 2, second_r[:, 1, :])
        make_h(1, 2, 0)
        first_q = (placed([P, 4 * HALF], U32, "first_w", at_bc(1, 0)), placed([P, 4 * HALF], U8, "first_s"))
        quantise_part(first_q, 0, 2 * HALF, first_r[:, 0:2, :].rearrange("p a c -> p (a c)"))
        second_q = (placed([P, 3 * HALF], U32, "second_w", AT_SECOND_W), placed([P, 3 * HALF], U8, "second_s"))
        quantise_part(second_q, 0, 2 * HALF, second_r[:].rearrange("p a c -> p (a c)"))
        h_q[0], h_q[1] = operand(first_q, HALF, S), operand(second_q, HALF, S)
        for i in range(2):
            wd_q[0, i] = operand(first_q, i * P, P)
            wd_q[0, 2 + i] = operand(first_q, 3 * HALF + i * P, P)
            wd_q[1, i] = operand(second_q, i * P, P)
        first_half = [make_y(0, 6, 0, HALF), make_y(1, 3, 0, HALF)]
        make_h(1, 3, 1)
        last_h = placed([P, HALF * PACK], BF16, "last_h")
        for i in range(2):
            add_bias(i, 0, first_half[i])
        turn_h(1, 1, 4, last_h[:])
        quantise_part(first_q, 2 * HALF, 2 * HALF, first_r[:, 2:4, :].rearrange("p a c -> p (a c)"))
        scatter(0, 0, HALF)
        quantise_part(second_q, 2 * HALF, HALF, last_h[:])
        last_pair = placed([P, HALF * PACK], BF16, "last_pair", AT_FIRST_R)
        round_pair(1, 2, on_scalar, last_pair[:])
        for i in range(2):
            add_bias(i, HALF, make_y(i, [7, 0][i], HALF, HALF))
        scatter(1, 0, HALF)
        last_q = (placed([P, HALF], U32, "last_w"), placed([P, HALF], U8, "last_s"))
        quantise_part(last_q, 0, HALF, last_pair[:])
        for i in range(2):
            wd_q[1, 2 + i] = operand(last_q, i * P, P)
        for i in (2, 3):
            add_bias(i, 0, make_y(i, i - 1, 0, S))
        for i in range(2):
            scatter(i, HALF, HALF)
        for i in (2, 3):
            scatter(i, 0, S)
